import numpy as np, ml_dtypes
CORES = [2,6,10,14,18,22,26,30]
N = 8
BF = ml_dtypes.bfloat16
def gentries(a):
    return np.ascontiguousarray(a.reshape(8, 16, -1).transpose(0, 2, 1)).reshape(8, -1)
def gtable(e):
    e = np.asarray(e); return np.ascontiguousarray(e.reshape(8, -1, 16).transpose(0, 2, 1)).reshape(128, -1).astype(np.int32)
W, NB, T, CA, LV, LI, LG = 4096, 2048, 5, 3, 9, 3, 1
P, S = NB // 16, W // (NB // 16)
def parts(rng):
    return rng.integers(0, 256, (N, 8, 16, W)), rng.integers(0, 256, (N, 8, 16, P)), rng.integers(0, 16, (N, 8, 16)), rng.integers(0, W, (N, 8, NB)), rng.integers(0, W, (N, 8, NB))
def pack(x, z, w, a, b):
    return {"xt": np.reshape(x, (N, 128, W)).astype(np.float32).astype(BF), "zp": np.reshape(z, (N, 128, P)).astype(np.float32).astype(BF), "wl": np.reshape(w, (N, 128, 1)).astype(np.float32).astype(BF),
            "ba": np.stack([gtable(v) for v in a]), "bb": np.stack([gtable(v) for v in b])}
def setup_inputs(rng):
    x, z, w, a, b = parts(rng)
    return pack(x, z, w, a, np.where(rng.random(b.shape) < 0.125, a, b))
def setup_inputs_corners(rng):
    x, z, w, a, b = parts(rng); pol = 255 * (np.arange(8) & 1)
    good = rng.random((N, 8, W)) < 0.5; good[..., W - 4:W - 1] = False
    far = np.abs(pol[None, :, None, None] - rng.integers(128, 256, x.shape))
    x = np.where(good[:, :, None, :], pol[None, :, None, None], far)
    z = np.broadcast_to(pol[None, :, None, None], z.shape).copy()
    o = np.argsort(rng.random((N, 8, 16)), axis=-1); v = rng.choice(np.array([128, 200]), (N, 8, 16))
    x[..., W - 4] = 128; x[..., W - 3] = np.where(o < LV, v, 60); x[..., W - 2] = np.where(o < LV - 1, v, 60)
    own = np.arange(NB).reshape(P, 16)
    for q in range(N):
        for g in range(8):
            pa, pb = rng.integers(0, W, 8192), rng.integers(0, W, 8192); pc = ((pa * pb >> 5) + pa + 37 * pb) & (W - 1); k = good[q, g]
            yes = np.flatnonzero(~k[pa] & ~k[pb] & k[pc] & (pa != pb)); no = np.flatnonzero((k[pa] | k[pb]) & (pa != pb))
            n = rng.choice(np.array([0, 1, CA - 1, CA, CA + 1, 16]), P); n[P - 1] = CA; n[0] = 16; n[2] = CA + 1
            m = np.argsort(rng.random((P, 16)), axis=1) < n[:, None]
            i = np.where(m, yes[rng.integers(0, len(yes), (P, 16))], no[rng.integers(0, len(no), (P, 16))]); aa, bb = pa[i], pb[i]
            kp = rng.integers(0, 12, P); kp[0] = 9; kp[P - 1] = 9; kp[2] = 9; kp[1] = 2; kp[P - 2] = 3; kp[3] = 0; kp[P - 3] = 1
            s = (kp == 0) | (kp == 2) | (kp == 3); aa[s] = own[s]; bb[s] = own[s]
            e = (W - 1) * rng.integers(0, 2, (P, 16)); aa[kp == 1] = e[kp == 1]; bb[kp == 1] = e[kp == 1]
            aa[kp == 4] = e[kp == 4]; bb[kp == 4] = W - 1 - e[kp == 4]
            slot = rng.integers(0, 16, P)
            for c, col in ((2, W - 3), (3, W - 2)):
                r = np.flatnonzero(kp == c); aa[r, slot[r]] = W - 4; bb[r, slot[r]] = col; z[q, g][:, r] = x[q, g, :, col][:, None]
            a[q, g] = aa.reshape(-1); b[q, g] = bb.reshape(-1)
    b[1] = a[1]
    w[:, 0] = 0; w[:, 1] = 15; w[:, 2] = 0; w[:, 2, 15] = 15; w[:, 3] = 15 * rng.integers(0, 2, (N, 16))
    return pack(x, z, w, a, b)
def setup_inputs_ends(rng):
    kind = rng.integers(0, 4, (N, 8, 1, W)); x = 255 * np.where(kind > 1, rng.integers(0, 2, (N, 8, 16, W)), kind)
    x = np.where((kind == 3) & (rng.random(x.shape) < 0.25), x ^ 1, x)
    hi = np.arange(8) & 1
    x[..., 0] = 255 * (1 - hi)[None, :, None]; x[..., W - 1] = 255 * hi[None, :, None]; x[0, ::2, :, W - 37] = 255
    cc = (((W - 1) * (W - 2) >> 5) + W - 1 + 37 * (W - 2)) & (W - 1)
    x[:, 1::2, :, W - 2] = 255; x[:, 1::2, :, cc] = 255
    zk = rng.integers(0, 3, (N, 8, 1, P)); z = 255 * np.where(zk == 2, rng.integers(0, 2, (N, 8, 16, P)), zk)
    w = 15 * rng.integers(0, 2, (N, 8, 16)); w[:, 1] = 15; w[:, 7] = 15; w[:, 2] = 0
    sh = (N, 8, NB)
    a = np.where(rng.random(sh) < 0.8, (W - 1) * rng.integers(0, 2, sh), rng.integers(0, W, sh))
    b = np.where(rng.random(sh) < 0.8, (W - 1) * rng.integers(0, 2, sh), rng.integers(0, W, sh))
    n = rng.integers(10, 17, (8, P, 1)); n[:, 0] = 16; n[:, P - 1] = 16
    m = (np.argsort(rng.random((8, P, 16)), axis=-1) < n).reshape(8, NB); top = ((W - 1) * hi)[:, None]
    a[0] = np.where(m, top, a[0]); b[0] = np.where(m, W - 1 - top, b[0])
    z[0] = 255 * (np.argsort(rng.random((8, 16, P)), axis=1) < rng.integers(0, 7, (8, 1, P)))
    for q in range(1, N):
        for g in (1, 7):
            for i, va, vb, vz in ((0, 0, W - 1, 255), (P - 1, 0, W - 1, 255), (1, W - 1, 0, 0), (P - 2, W - 1, 0, 0), (2, W - 1, W - 2, 0), (P - 3, W - 1, W - 2, 0)):
                a[q, g, 16 * i:16 * i + 16] = va; b[q, g, 16 * i:16 * i + 16] = vb; z[q, g, :, i] = vz
    return pack(x, z, w, a, b)
def setup_inputs_spread(rng):
    x, z, w, a, b = parts(rng)
    x = (np.exp2(8 * rng.random((N, 8, 1, W))) * rng.random(x.shape)).astype(np.int64)
    z = (np.exp2(8 * rng.random((N, 8, 1, P))) * rng.random(z.shape)).astype(np.int64)
    w = w >> rng.integers(0, 5, w.shape)
    a = (W * rng.random(a.shape) ** rng.integers(1, 5, (N, 8, 1))).astype(np.int64); b = (W * rng.random(b.shape) ** rng.integers(1, 5, (N, 8, 1))).astype(np.int64)
    return pack(x, z, w, np.minimum(a, W - 1), np.minimum(b, W - 1))
def setup_inputs_ties(rng):
    x, z, w, a, b = parts(rng)
    base = rng.integers(0, 256, (N, 8, 16, 6)); base[:, ::2] = rng.choice(np.array([0, 1, 128, 254, 255]), (N, 4, 16, 6))
    x = np.take_along_axis(base, rng.integers(0, 6, (N, 8, 1, W)), 3)
    z = np.where(rng.random((N, 8, 1, P)) < 0.75, np.take_along_axis(base, rng.integers(0, 6, (N, 8, 1, P)), 3), z)
    m = rng.random((N, 8, P, 1)) < 0.25
    a = a.reshape(N, 8, P, 16); b = b.reshape(N, 8, P, 16); b = np.where(rng.random(b.shape) < 0.125, a, b)
    a = np.where(m, a[..., :1], a).reshape(N, 8, NB); b = np.where(m, b[..., :1], b).reshape(N, 8, NB)
    return pack(x, z, w, a, b)
def check_inputs(d):
    bad = []
    for k, lo, hi in (("xt", 0, 255), ("zp", 0, 255), ("wl", 0, 15), ("ba", 0, W - 1), ("bb", 0, W - 1)):
        v = np.asarray(d[k]).astype(np.float64)
        if not np.all((v >= lo) & (v <= hi) & (v == np.floor(v))): bad.append("range of " + k)
    return bad
def reference(xt, zp, wl, ba, bb):
    X = xt.astype(np.float32).astype(np.int32).reshape(N, 8, 16, W); z = zp.astype(np.float32).astype(np.int32).reshape(N, 8, 16, P)
    w = wl.astype(np.float32).astype(np.int32).reshape(N, 8, 16, 1)
    L = [np.stack([gentries(v) for v in m]).astype(np.int32) for m in (ba, bb)]
    I = np.zeros((N, 8, NB), np.int32); G = np.zeros((N, 8, NB), np.int32); rej = [0] * N
    def before(m):
        m = m.astype(np.int32).reshape(8, P, 16)
        return (np.add.accumulate(m, axis=2) - m).reshape(8, NB)
    for t in range(T):
        now = [0] * N
        for q in range(N):
            s = (q + t) % N
            H = L[t % 2][q]; O = L[1 - t % 2][q]; C = ((H * O >> 5) + H + 37 * O) & (W - 1)
            h, o, c = [np.take_along_axis(X[s], v[:, None, :], 2) for v in (H, O, C)]
            zz = np.repeat(z[q], 16, axis=2); dh, do, dc = [np.add.reduce(np.abs(v - zz), axis=1) for v in (h, o, c)]
            live = H != O
            rec = live & (do <= np.minimum(dh, dc))
            want = live & ~rec & (dc < dh) & (G[q] < LG); am = want & (before(want) < CA)
            ins = live & ~rec & ~am
            ch = np.where(rec[:, None, :], o, np.where(am[:, None, :], c, h))
            V = np.add.reduce((ch - h).reshape(8, 16, P, 16), axis=3)
            ok = np.add.reduce((V >= 0).astype(np.int32), axis=1) >= LV
            now[s] = int(np.add.reduce((~ok).astype(np.int64), axis=None)); yes = np.repeat(ok, 16, axis=1)
            I[q] += ins | ((rec | am) & ~yes); G[q] += am & yes
            H2 = np.where(yes & rec, O, np.where(yes & am, C, H))
            sp = I[q] >= LI; v = np.where((before(sp) & 1) == 1, C, H)
            H2 = np.where(sp, v, H2); O2 = np.where(sp, v, O); I[q] = np.where(sp, 0, I[q])
            M = np.maximum.reduce(ch.reshape(8, 16, P, 16), axis=3); u = np.add.reduce(w[s] * M, axis=1) & (W - 1)
            O2 = np.where(live, O2, ((H * np.repeat(u, 16, axis=1) >> 5) + H + rej[s]) & (W - 1))
            L[t % 2][q] = H2; L[1 - t % 2][q] = O2
            if t < T - 1:
                z[q] = np.abs(z[q] - M)
                at = (S * np.arange(P)[None, :] + (u & (S - 1)))[:, None, :]
                np.put_along_axis(X[s], at, (np.take_along_axis(X[s], at, 2) + M) >> 1, 2)
        rej = now
    home = [(s - (T - 1)) % N for s in range(N)]
    ya, yb, yi, yg = [np.stack([gtable(m[q]) for q in home]).astype(np.float32) for m in (L[0], L[1], I, G)]
    return {"ya": ya, "yb": yb, "yi": yi, "yg": yg}

@@ -1,0 +1,536 @@
+import numpy as np
+from concourse.mybir import AluOpType as OP, ActivationFunctionType as AF
+
+NT = 5
+NH = 2
+NPK = 64
+NB = 16 * NPK
+NPC = 2
+PCB = NB // NPC
+PCK = NPK // NPC
+
+SCRATCH = {"X": ("sbuf", [128, 4096], "bfloat16"), "ia": ("sbuf", [128, 128], "int32"), "ib": ("sbuf", [128, 128], "int32"),
+           "wc": ("sbuf", [128, 1], "bfloat16"), "r32": ("sbuf", [128, 1], "float32"), "ri": ("sbuf", [128, 1], "int32"),
+           "rj": ("sbuf", [128, 1], "int32"), "mi": ("sbuf", [128, 64], "int32"), "mj": ("sbuf", [128, 64], "int32"),
+           "base0": ("sbuf", [128, 64], "float32"), "Q": ("sbuf", [128, 144], "bfloat16"),
+           "zmask": ("sbuf", [128, NB], "bfloat16"), "K32": ("sbuf", [128, NT], "float32"), "ks": ("sbuf", [128, 2 * NT], "float32"),
+           "SI": ("sbuf", [128, 256], "float32")}
+F32 = ("P", "dhs", "Hc", "thr", "m", "s1", "cho", "um", "sc", "P2", "ad", "hsb", "spoh", "kset")
+I32 = ("S", "ci", "ui", "u12", "u5", "gx", "gs", "S2", "fx", "pc", "od2")
+SMALL = {}
+for _n in ("ones", "bt", "BM", "I", "nI", "n8I", "c91", "c200", "n300", "n3I", "TRI", "TRI16", "Wb"):
+    SCRATCH[_n] = ("sbuf", [128, 128], "bfloat16")
+SCRATCH["o16f"] = ("sbuf", [128, 128], "float32")
+for _t in range(NT):
+    SCRATCH["L%d" % _t] = ("sbuf", [128, 256], "float32")
+    SCRATCH["Z%d" % _t] = ("sbuf", [128, 384], "bfloat16")
+    SCRATCH["SL%d" % _t] = ("sbuf", [128, 256], "float32")
+    SCRATCH["SZ%d" % _t] = ("sbuf", [128, 384], "bfloat16")
+for _h in range(NH):
+    for _n in ("zbuf", "zexp", "hr", "ha", "od", "orl", "cd", "cabs", "ch", "Mf"):
+        SCRATCH["%s_%d" % (_n, _h)] = ("sbuf", [128, NB], "bfloat16")
+    SCRATCH["ho16_%d" % _h] = ("sbuf", [128, 128], "uint16")
+    for _n in ("c16", "ch16"):
+        SCRATCH["%s_%d" % (_n, _h)] = ("sbuf", [128, 64], "uint16")
+    SCRATCH["u16_%d" % _h] = ("sbuf", [128, 4], "uint16")
+    for _i, _n in enumerate(F32):
+        SMALL["%s_%d" % (_n, _h)] = ("F_%d" % _h, 64 * _i)
+    SCRATCH["F_%d" % _h] = ("sbuf", [128, 64 * len(F32)], "float32")
+    for _i, _n in enumerate(I32):
+        SMALL["%s_%d" % (_n, _h)] = ("J_%d" % _h, 64 * _i)
+    SCRATCH["J_%d" % _h] = ("sbuf", [128, 64 * len(I32)], "int32")
+    for _n in ("set", "rec", "w", "am", "yv", "acc", "inc", "sp", "dm"):
+        SCRATCH["%s_%d" % (_n, _h)] = ("sbuf", [128, 64], "bfloat16")
+for _b in range(8):
+    SCRATCH["ps%d" % _b] = ("psum", [128, 512], "float32")
+
+SEMAPHORES = ["qv", "qa", "qt", "qg", "loc"] + ["in%d" % _i for _i in range(7)] + ["out%d" % _i for _i in range(8)] + \
+    ["arr_%d_%d_%s" % (_t, _h, _k) for _t in range(1, NT) for _h in range(NH) for _k in "LZN"]
+
+PS = {}
+for _h in range(NH):
+    for _i, _n in enumerate(("dh", "do", "dc", "dhp", "V", "cnt", "cntv", "u")):
+        PS[_n, _h] = (2 + _h, _i)
+    for _i, _n in enumerate(("H", "L", "OH", "L2", "O1", "zd", "cnt2", "hsum")):
+        PS[_n, _h] = (4 + _h, _i)
+    for _i, _n in enumerate(("CH", "d", "tmp")):
+        PS[_n, _h] = (6, 3 * _h + _i)
+    for _i, _n in enumerate(("incs", "Gs", "In", "I2")):
+        PS[_n, _h] = (7, 4 * _h + _i)
+PS["mask", 0] = (6, 6)
+
+CY = 0.83e-3 * 1.2
+PCY = 0.55 * 1e-3
+GA = 1.6
+WAKE, OWN = 0.16, 0.16
+BONUS, WINDOW = 0, 0.005
+OFFS = {'zbuf_1': -2.0, 'ps4:L20': -2.2, 'dhs_1': 1.0, 'ps5:H1': -3.1, 'ps5:L21': -2.0, 'hsb_1': -10.0, 'ps5:OH1': 15.0, 'ps6:tmp1': 11.0,
+        'Hc_1': 8.0, 'od_0.0': -3.0, 'od_1.0': 4.0, 'ps4:OH0': -4.0, 'ps5:hsum1': 14.0, 'ps6:tmp0': -2.0, 'hr_1.0': -2.2, 'send_0_zg': 2.0,
+        'gx_1': 2.5, 'fx_0': 4.0, 'P_0': -11.0, 'zexp_1.0': 10.0, 'u5_0': -2.0, 'acc_0': 5.0, 'ho16_1': -14.0, 'zbuf_0': -10.0, 'S2_0': -2.0,
+        'spoh_1': -8.4, 'm_0': -3.0, 'ps7:incs0': -2.0, 'fx_1': -8.0, 'cabs_1.1': -4.0, 'hr_1.1': -5.6, 'sp_0': 8.0, 'rec_1': -9.0,
+        'zexp_1.1': -9.0, 'hr_0.1': 5.0, 'inc_0': 8.0, 'ps4:H0': 1.5, 'orl_1.0': 3.0, 'cabs_1.0': -5.0, 'ch_0.1': -3.0, 'kset_0': -6.0,
+        'zexp_0.1': -6.4, 'od_1.1': -5.0, 'acc_1': -14.0, 'ps5:L1': -1.6, 'ps5:O11': 10.0, 'dhs_0': 6.0, 'ad_0': -11.0, 'cd_1.1': -7.0,
+        'orl_0.1': 8.0, 'cho_1': 4.0, 'ps7:Gs1': 18.0, 'u16_0': -4.0, 'orl_0.0': -3.0}
+HOP = 5.2
+
+
+def build():
+    ops = []
+    cur = {"h": None, "t": -1}
+
+    def add(q, cost, fn, r, w, **kw):
+        ops.append(dict(q=q, cost=cost, fn=fn, r=list(r), w=list(w), h=cur["h"], t=cur["t"], **kw))
+
+    def ps(name, h, T):
+        b, i = PS[name, h]
+        return T["ps%d" % b][:, 64 * i:64 * i + 64]
+
+    def full(name):
+        return (name, lambda T: T[name][:])
+
+    def pk(name, h):
+        return ("ps%d:%s%d" % (PS[name, h][0], name, h), lambda T: ps(name, h, T))
+
+    def sb(name, h):
+        n = "%s_%d" % (name, h)
+        if n in SMALL:
+            b, c = SMALL[n]
+            return (n, lambda T: T[b][:, c:c + 64])
+        return (n, lambda T: T[n][:])
+
+    def cols(name, a, b, step=1, key=None):
+        return (key or name, lambda T: T[name][:, a:b:step] if step != 1 else T[name][:, a:b])
+
+    def inps(x):
+        return x[0].startswith("ps")
+
+    def tt(out, a, b, op, n=64):
+        c = max(64, n * (1 if inps(a) or inps(b) else 2))
+        add("v", c * CY, lambda g, T: g.vector.tensor_tensor(out[1](T), a[1](T), b[1](T), op), [a[0], b[0]], [out[0]])
+
+    def ts(out, a, s1, op0, s2=None, op1=None, n=64, half=False, extra=()):
+        c = max(64, n * (0.5 if half else 1))
+
+        def fn(g, T):
+            sc = s1(T) if callable_(s1) else s1
+            if op1 is None:
+                return g.vector.tensor_scalar(out[1](T), a[1](T), sc, None, op0)
+            return g.vector.tensor_scalar(out[1](T), a[1](T), sc, s2, op0, op1)
+        add("v", c * CY, fn, [a[0]] + list(extra), [out[0]])
+
+    def callable_(x):
+        return not isinstance(x, (int, float))
+
+    def cp(out, a, n=64):
+        add("v", max(64, n) * CY, lambda g, T: g.vector.tensor_copy(out[1](T), a[1](T)), [a[0]], [out[0]])
+
+    def act(out, a, func, scale=1.0, bias=0.0, n=64, extra=(), accum=None):
+        def fn(g, T):
+            kw = {}
+            if scale != 1.0 or callable_(scale):
+                kw["scale"] = scale(T) if callable_(scale) else scale
+            if bias != 0.0:
+                kw["bias"] = bias
+            if accum is not None:
+                kw["accum_out"] = accum[1](T)
+            return g.scalar.activation(out[1](T), a[1](T), func, **kw)
+        add("a", max(64, n) * CY + 0.02, fn, [a[0]] + list(extra), [out[0]] + ([accum[0]] if accum is not None else []))
+
+    def mm(out, terms):
+        def fn(g, T):
+            r = None
+            for k, (l, x, n, f) in enumerate(terms):
+                r = g.tensor.matmul(out[1](T), l[1](T), x[1](T), k == 0, k == len(terms) - 1)
+            return r
+        keys = []
+        for l, x, n, f in terms:
+            for y in (l, x):
+                for kk in (y[0] if isinstance(y[0], (list, tuple)) else [y[0]]):
+                    if kk not in keys:
+                        keys.append(kk)
+        add("t", sum(max(64, n) * f for l, x, n, f in terms) * PCY, fn, keys, [out[0]])
+
+    def f1(l, x, n=64):
+        return (full(l), x, n, 1)
+
+    def f4(l, x, n=64):
+        return (full(l), x, n, 4)
+
+    def gather_v(out, lst, z, n):
+        add("v", 0.05 + n * GA * CY, lambda g, T: g.vector.tensor_tensor(out[1](T), T.X[:, 0:4096].indirect(lst[1](T)), z[1](T), OP.subtract),
+            ["X0", "X1", lst[0], z[0]], [out[0]])
+
+    def gather_a(out, lst, n):
+        add("a", 0.065 + n * GA * CY, lambda g, T: g.scalar.activation(out[1](T), T.X[:, 0:4096].indirect(lst[1](T)), AF.Copy),
+            ["X0", "X1", lst[0]], [out[0]])
+
+    def memset(name, val, n, sl=None, key=None):
+        add("v", max(64, n) * CY, lambda g, T: g.vector.memset(sl(T) if sl is not None else T[name][:], val), [], [key or name])
+
+    def dma(q, sem, out, src, cost):
+        def fn(g, T):
+            return (g.sync if q == "s" else g.scalar).dma_start(out[1](T), src[1](T))
+        add(q, 0.1, fn, [src[0]] if src[0] else [], [out[0]], sem=sem, lat=cost)
+
+    def piece(name, h, p):
+        n = "%s_%d" % (name, h)
+        return ("%s.%d" % (n, p), lambda T: T[n][:, p * PCB:(p + 1) * PCB])
+
+    def col16(name, h, j):
+        n = "%s_%d" % (name, h)
+        return (["%s.%d" % (n, p) for p in range(NPC)], lambda T: T[n][:, j:NB:16])
+
+    dma("s", "in0", full("ia"), (None, lambda T: T.ba[:]), 2.0)
+    dma("a", "in1", full("ib"), (None, lambda T: T.bb[:]), 2.0)
+    dma("s", "in2", ("X0", lambda T: T.X[:, 0:2048]), (None, lambda T: T.xt[:, 0:2048]), 5.0)
+    dma("a", "in3", ("X1", lambda T: T.X[:, 2048:4096]), (None, lambda T: T.xt[:, 2048:4096]), 5.0)
+    for h in range(NH):
+        dma("s", "in%d" % (4 + h), cols("Z0", 192 * h, 192 * h + 64, key="z0_%d" % h), (None, lambda T, h=h: T.zp[:, 64 * h:64 * h + 64]), 2.2)
+    dma("s", "in6", full("wc"), (None, lambda T: T.wl[:]), 2.2)
+    gp = lambda fn, r, w: add("g", 0.5, fn, r, w, sem="qg")
+    memset("ones", 1.0, 128)
+    gp(lambda g, T: g.affine_select(T.I[:], T.ones[:], [[-1, 128]], OP.is_equal, 0.0, 0, 1), ["ones"], ["I"])
+    gp(lambda g, T: g.affine_select(T.bt[:], T.ones[:], [[-16, 8], [0, 16]], OP.is_ge, 0.0, 0, 1), ["ones"], ["bt"])
+    gp(lambda g, T: g.affine_select(T.BM[:], T.bt[:], [[16, 8], [0, 16]], OP.is_ge, 0.0, 15, -1), ["bt"], ["BM"])
+    gp(lambda g, T: g.affine_select(T.TRI[:], T.BM[:], [[1, 128]], OP.is_gt, 0.0, 0, -1), ["BM"], ["TRI"])
+    for h in range(NH):
+        memset("zbuf_%d" % h, 0.0, NB // 2)
+        memset("Z0", 0.0, 64, sl=lambda T, h=h: T.Z0[:, 192 * h + 64:192 * h + 192], key="ig0_%d" % h)
+    memset("zmask", 1.0, NB // 2)
+    memset("zmask", 0.0, 64, sl=lambda T: T.zmask[:, 0:NB:16])
+    ops[-1]["r"].append("zmask")
+    memset("Q", 0.0, 144)
+    add("v", 64 * CY, lambda g, T: g.vector.tensor_copy(T.Q[:, 15:143:16], T.BM[:, 0:128:16]), ["BM", "Q"], ["Q"])
+    act(full("nI"), full("I"), AF.Copy, scale=-1.0, n=128)
+    act(full("n8I"), full("I"), AF.Copy, scale=-8192.0, n=128)
+    ts(full("TRI16"), full("I"), -16.0, OP.mult, n=128, half=True)
+    tt(full("TRI16"), full("TRI16"), full("TRI"), OP.add, n=128)
+    act(full("c91"), full("I"), AF.Copy, scale=91.0, n=128)
+    act(full("c200"), full("I"), AF.Copy, scale=200.0, n=128)
+    act(full("n300"), full("I"), AF.Copy, scale=-300.0, n=128)
+    act(full("n3I"), full("I"), AF.Copy, scale=-3.0, n=128)
+    ts(full("Wb"), full("BM"), lambda T: T.wc[:], OP.mult, n=128, half=True, extra=["wc"])
+    gp(lambda g, T: g.iota(T.mi[:], [[-1, 64]], 64, 1), [], ["mi"])
+    gp(lambda g, T: g.iota(T.ri[:], [[0, 1]], 0, 1), [], ["ri"])
+    gp(lambda g, T: g.iota(T.base0[:], [[512, 4], [0, 16]], 0, 0, allow_small_or_imprecise_dtypes=True), [], ["base0"])
+    ts(full("mj"), full("mi"), 15, OP.bitwise_and)
+    ts(pk("mask", 0), full("mj"), 0.0, OP.is_equal)
+    ts(full("rj"), full("ri"), 15, OP.bitwise_and)
+    ts(full("r32"), full("rj"), 32.0, OP.mult)
+    memset("o16f", 0.0625, 128)
+
+    for h in range(NH):
+        cp(cols("L0", 128 * h, 128 * h + 64, key="l0_%d" % h), cols("ia", 64 * h, 64 * h + 64))
+        cp(cols("L0", 128 * h + 64, 128 * h + 128, key="l0_%d" % h), cols("ib", 64 * h, 64 * h + 64))
+
+    for t in range(NT):
+        last = t == NT - 1
+        scat = []
+        for h in range(NH):
+            cur["h"], cur["t"] = h, t
+            lk, zk, ik = "l%d_%d" % (t, h), "z%d_%d" % (t, h), "ig%d_%d" % (t, h)
+            ca, cb = 128 * h + 64 * (t % 2), 128 * h + 64 * (1 - t % 2)
+            LH, LO = cols("L%d" % t, ca, ca + 64, key=lk), cols("L%d" % t, cb, cb + 64, key=lk)
+            z = cols("Z%d" % t, 192 * h, 192 * h + 64, key=zk)
+            Iold = cols("Z%d" % t, 192 * h + 64, 192 * h + 128, key=ik)
+            Gold = cols("Z%d" % t, 192 * h + 128, 192 * h + 192, key=ik)
+            if t > 0:
+                add(None, 0.0, None, ["send_%d_%d_L" % (t - 1, h)], [lk], arr="arr_%d_%d_L" % (t, h), lat=HOP)
+                add(None, 0.0, None, ["send_%d_%d_Z" % (t - 1, h)], [zk], arr="arr_%d_%d_Z" % (t, h), lat=HOP)
+                add(None, 0.0, None, ["send_%d_%d_N" % (t - 1, h)], [ik], arr="arr_%d_%d_N" % (t, h), lat=HOP)
+            cp(sb("ho16", h), cols("L%d" % t, 128 * h, 128 * h + 128, key=lk), n=128)
+            add("a", 64 * CY, lambda g, T, h=h, z=z: g.scalar.activation(T["zbuf_%d" % h][:, 0:NB:16], z[1](T), AF.Copy), [zk, "zbuf_%d" % h], ["zbuf_%d" % h])
+            act(sb("Hc", h), LH, AF.Copy, bias=-2048.0)
+            act(pk("O1", h), LO, AF.Copy, bias=32.0)
+            act(pk("L", h), LO, AF.Copy, scale=3232.0, bias=65536.0 - 8388608.0)
+            act(pk("H", h), LH, AF.Copy)
+            tt(sb("P", h), sb("Hc", h), pk("O1", h), OP.mult)
+            tt(sb("S", h), sb("P", h), pk("L", h), OP.add)
+            tt(pk("OH", h), LO, pk("H", h), OP.subtract)
+            ts(sb("ci", h), sb("S", h), 5, OP.arith_shift_right, 4095, OP.bitwise_and)
+            cp(sb("c16", h), sb("ci", h))
+            ts(sb("set", h), pk("OH", h), 0.0, OP.is_equal)
+            for p in range(NPC):
+                ze = piece("zexp", h, p)
+                add("v", PCB / 2 * CY, lambda g, T, h=h, p=p: g.vector.tensor_tensor_scan(
+                    T["zexp_%d" % h][:, p * PCB:(p + 1) * PCB], T.zmask[:, 0:PCB], T["zbuf_%d" % h][:, p * PCB:(p + 1) * PCB], 0.0, OP.mult, OP.add),
+                    ["zmask", "zbuf_%d" % h], [ze[0]])
+            lst = lambda name, a, h=h: (lambda p: ("%s_%d" % (name, h), lambda T: T["%s_%d" % (name, h)][:, a + p * PCK:a + (p + 1) * PCK]))
+            lh, lo, lc, lch = lst("ho16", 64 * (t % 2)), lst("ho16", 64 * (1 - t % 2)), lst("c16", 0), lst("ch16", 0)
+            for p in range(NPC):
+                gather_a(piece("hr", h, p), lh(p), PCB)
+                yb = ("ps%d:y" % p, lambda T, p=p: T["ps%d" % p][:, 0:PCB])
+                mm(yb, [f1("I", piece("hr", h, p), PCB), f1("nI", piece("zexp", h, p), PCB)])
+                act(piece("ha", h, p), yb, AF.Abs, n=PCB)
+            for p in range(NPC):
+                gather_v(piece("od", h, p), lo(p), piece("zexp", h, p), PCB)
+                act(piece("orl", h, p), piece("od", h, p), AF.Abs, n=PCB)
+            for p in range(NPC):
+                gather_v(piece("cd", h, p), lc(p), piece("zexp", h, p), PCB)
+                act(piece("cabs", h, p), piece("cd", h, p), AF.Abs, n=PCB)
+            q = lambda j: ("Q", lambda T, j=j: T.Q[:, 15 - j:143 - j])
+            mm(pk("dh", h), [(q(j), col16("ha", h, j), 64, 1) for j in range(16)])
+            mm(pk("do", h), [(q(j), col16("orl", h, j), 64, 1) for j in range(16)])
+            mm(pk("dc", h), [(q(j), col16("cabs", h, j), 64, 1) for j in range(16)])
+            act(sb("dhs", h), pk("dh", h), AF.Copy)
+            mm(pk("dhp", h), [f1("n8I", Gold), f1("n8I", sb("set", h))])
+            tt(sb("thr", h), sb("dhs", h), pk("do", h), OP.min)
+            tt(sb("thr", h), sb("thr", h), pk("dhp", h), OP.add)
+            tt(sb("w", h), pk("dc", h), sb("thr", h), OP.is_lt)
+            mm(pk("cnt", h), [f1("TRI16", sb("w", h))])
+            tt(sb("m", h), sb("dhs", h), pk("dc", h), OP.min)
+            tt(sb("rec", h), pk("do", h), sb("m", h), OP.is_le)
+            tt(pk("CH", h), sb("ci", h), pk("H", h), OP.subtract)
+            tt(pk("tmp", h), sb("rec", h), pk("OH", h), OP.mult)
+            tt(sb("s1", h), LH, pk("tmp", h), OP.add)
+            ts(sb("am", h), pk("cnt", h), -13.0, OP.is_lt)
+            tt(pk("d", h), sb("am", h), pk("CH", h), OP.mult)
+            tt(sb("cho", h), sb("s1", h), pk("d", h), OP.add)
+            tt(pk("d", h), sb("cho", h), pk("H", h), OP.subtract)
+            cp(sb("ch16", h), sb("cho", h))
+            for p in range(NPC):
+                gather_a(piece("ch", h, p), lch(p), PCB)
+                add("v", PCB / 2 * CY, lambda g, T, h=h, p=p: g.vector.tensor_tensor_scan(
+                    T["Mf_%d" % h][:, p * PCB:(p + 1) * PCB], T.zmask[:, 0:PCB], T["ch_%d" % h][:, p * PCB:(p + 1) * PCB], 0.0, OP.mult, OP.max),
+                    ["zmask", "ch_%d.%d" % (h, p)], ["Mf_%d.%d" % (h, p)])
+            M = (["Mf_%d.%d" % (h, p) for p in range(NPC)], lambda T, h=h: T["Mf_%d" % h][:, 15:NB:16])
+            mm(pk("u", h), [f1("Wb", M)])
+            cp(sb("ui", h), pk("u", h))
+            if not last:
+                ts(sb("u5", h), sb("ui", h), 31, OP.bitwise_and)
+                tt(sb("um", h), sb("u5", h), pk("mask", 0), OP.mult)
+                add("v", 64 * CY, lambda g, T, sc=sb("sc", h)[1], um=sb("um", h)[1]: g.vector.tensor_tensor_scan(
+                    sc(T), T.base0[:], um(T), 0.0, OP.max, OP.add), ["base0", "um_%d" % h], ["sc_%d" % h])
+                fb, fc = SMALL["sc_%d" % h]
+                ts(sb("u16", h), ("sc_%d" % h, lambda T, fb=fb, fc=fc: T[fb][:, fc + 15:fc + 64:16]), lambda T: T.r32[:], OP.add, extra=["r32"])
+                win = lambda T, h=h: T.X[:, 2048 * h:2048 * h + 2048].indirect(T["u16_%d" % h][:, 0:4])
+                add("v", 0.05 + 64 * GA * CY, lambda g, T, gx=sb("gx", h)[1], win=win, M=M: g.vector.tensor_tensor(gx(T), win(T), M[1](T), OP.add),
+                    ["X%d" % h, "u16_%d" % h] + M[0], ["gx_%d" % h])
+                ts(sb("gs", h), sb("gx", h), 1, OP.arith_shift_right)
+                scat.append(("v", 0.05 + 64 * 4 * CY, lambda g, T, gs=sb("gs", h)[1], win=win: g.vector.tensor_copy(win(T), gs(T)),
+                             ["gs_%d" % h, "u16_%d" % h, "X%d" % h], ["X%d" % h]))
+            mm(pk("hsum", h), [(full("I"), col16("hr", h, j), 64, 1) for j in range(16)])
+            act(sb("hsb", h), pk("hsum", h), AF.Copy)
+            mm(pk("V", h), [(full("I"), col16("ch", h, j), 64, 1) for j in range(16)])
+            tt(sb("yv", h), pk("V", h), sb("hsb", h), OP.is_ge)
+            mm(pk("cntv", h), [f1("BM", sb("yv", h))])
+            ts(sb("acc", h), pk("cntv", h), 9.0, OP.is_ge)
+            grow = [f1("c91", sb("rec", h)), f1("c91", sb("am", h)), f1("c200", sb("set", h)), f1("BM", sb("yv", h))]
+            mm(pk("dhp", h), [f1("n300", Iold)] + grow)
+            ts(sb("sp", h), pk("dhp", h), -500.0, OP.is_lt)
+            mm(pk("cnt2", h), [f1("TRI", sb("sp", h))])
+            mm(pk("incs", h), grow)
+            ts(sb("inc", h), pk("incs", h), 100.0, OP.is_lt)
+            sl, sz = "SL%d" % t, "SZ%d" % t
+            sh = "send_%d_%d" % (t, h)
+            tt(pk("tmp", h), sb("set", h), pk("H", h), OP.mult)
+            ts(sb("u12", h), sb("ui", h), 4095, OP.bitwise_and)
+            tt(sb("P2", h), sb("u12", h), pk("tmp", h), OP.mult)
+            tt(sb("spoh", h), sb("sp", h), pk("OH", h), OP.mult)
+            tt(pk("CH", h), sb("sp", h), pk("CH", h), OP.mult)
+            cp(sb("pc", h), pk("cnt2", h))
+            ts(sb("od2", h), sb("pc", h), 1, OP.bitwise_and)
+            tt(pk("CH", h), sb("od2", h), pk("CH", h), OP.mult)
+            tt(pk("tmp", h), pk("CH", h), sb("spoh", h), OP.subtract)
+            tt(pk("d", h), sb("acc", h), pk("d", h), OP.mult)
+            act(pk("L2", h), LO, AF.Copy, scale=32.0, bias=-8388608.0)
+            if t > 0:
+                act(sb("kset", h), sb("set", h), AF.Identity, scale=lambda T, t=t: T.K32[:, t - 1:t], extra=["K32.%d" % (t - 1)])
+                tt(pk("L2", h), sb("kset", h), pk("L2", h), OP.add)
+            tt(sb("S2", h), sb("P2", h), pk("L2", h), OP.add)
+            ts(sb("fx", h), sb("S2", h), 5, OP.arith_shift_right, 4095, OP.bitwise_and)
+            tt(cols(sl, cb, cb + 64, key=sh + "_lo"), sb("fx", h), pk("tmp", h), OP.add)
+            tt(sb("ad", h), LH, pk("d", h), OP.add)
+            tt(cols(sl, ca, ca + 64, key=sh + "_lh"), sb("ad", h), pk("CH", h), OP.add)
+            mm(pk("I2", h), [f1("I", Iold), f1("I", sb("inc", h)), f1("n3I", sb("sp", h))])
+            mm(pk("Gs", h), [f1("c91", sb("am", h)), f1("c200", Gold), f1("BM", sb("yv", h))])
+            if last:
+                act(cols("SI", 128 * h, 128 * h + 64, key="si%d" % h), pk("I2", h), AF.Copy)
+                ts(cols("SI", 128 * h + 64, 128 * h + 128, key="sg%d" % h), pk("Gs", h), 100.0, OP.is_ge)
+                ka, kb = sh + "_lh", sh + "_lo"
+                dma("s", "out%d" % (4 * h), (None, lambda T, h=h: T.yi[:, 64 * h:64 * h + 64]), cols("SI", 128 * h, 128 * h + 64, key="si%d" % h), 2.0)
+                dma("s", "out%d" % (4 * h + 1), (None, lambda T, h=h: T.yg[:, 64 * h:64 * h + 64]), cols("SI", 128 * h + 64, 128 * h + 128, key="sg%d" % h), 2.0)
+                dma("s", "out%d" % (4 * h + 2), (None, lambda T, h=h: T.ya[:, 64 * h:64 * h + 64]), cols(sl, ca, ca + 64, key=ka), 2.0)
+                dma("s", "out%d" % (4 * h + 3), (None, lambda T, h=h: T.yb[:, 64 * h:64 * h + 64]), cols(sl, cb, cb + 64, key=kb), 2.0)
+            else:
+                act(cols(sz, 192 * h + 64, 192 * h + 128, key=sh + "_zi"), pk("I2", h), AF.Copy)
+                ts(cols(sz, 192 * h + 128, 192 * h + 192, key=sh + "_zg"), pk("Gs", h), 100.0, OP.is_ge)
+                mm(pk("zd", h), [f1("I", z), f1("nI", M)])
+                act(cols(sz, 192 * h, 192 * h + 64, key=sh + "_zz"), pk("zd", h), AF.Abs)
+                act(sb("dm", h), sb("acc", h), AF.Copy, accum=cols("ks", 2 * t + h, 2 * t + h + 1, key="ks%d_%d" % (t, h)))
+                add("g", 0.3, None, [sh + "_zz"], [sh + "_Z"], send=(t, h, "Z"))
+                add("g", 0.3, None, [sh + "_zi", sh + "_zg"], [sh + "_N"], send=(t, h, "N"))
+                add("g", 0.3, None, [sh + "_lo", sh + "_lh"], [sh + "_L"], send=(t, h, "L"))
+        for x in scat:
+            add(*x)
+        if not last:
+            kp = ("ps4:zd0", lambda T: T.ps4[:, 320:321])
+            mm(kp, [f4("o16f", cols("ks", 2 * t + h, 2 * t + h + 1, key="ks%d_%d" % (t, h)), 1) for h in range(NH)])
+            act(cols("K32", t, t + 1, key="K32.%d" % t), kp, AF.Copy, scale=-32.0, bias=32768.0)
+    return ops
+
+
+def opclass(o):
+    c = o["w"][0] if o["w"] else ""
+    for p in ("l", "z", "ig", "send_", "K32.", "ks"):
+        if o["t"] >= 0 and c.startswith(p + str(o["t"])):
+            c = p + c[len(p) + 1:].lstrip("_")
+    return c
+
+
+def graph():
+    ops = build()
+    n = len(ops)
+    deps = [set() for _ in range(n)]
+    lastw, readers = {}, {}
+
+    def keys(l):
+        out = []
+        for k in l:
+            out += keys(k) if isinstance(k, (list, tuple)) else ([k] if k else [])
+        return out
+    for i, o in enumerate(ops):
+        o["r"], o["w"] = keys(o["r"]), keys(o["w"])
+        for k in o["r"]:
+            if k in lastw:
+                deps[i].add(lastw[k])
+        for k in o["w"]:
+            if k in lastw:
+                deps[i].add(lastw[k])
+            deps[i].update(readers.get(k, ()))
+        for k in o["r"]:
+            readers.setdefault(k, []).append(i)
+        for k in o["w"]:
+            lastw[k] = i
+            readers[k] = []
+        deps[i].discard(i)
+        o["banks"] = sorted(set(k.split(":")[0] for k in o["r"] + o["w"] if k.startswith("ps")))
+        o["cls"] = opclass(o)
+    succ = [[] for _ in range(n)]
+    for i in range(n):
+        for j in deps[i]:
+            succ[j].append(i)
+    pri = [0.0] * n
+    for i in range(n - 1, -1, -1):
+        o = ops[i]
+        pri[i] = o["cost"] + o.get("lat", 0.0) + 0.08 + max([pri[s] for s in succ[i]] or [0.0])
+    return ops, deps, succ, pri
+
+
+def schedule(gr, offs, bonus, window):
+    ops, deps, succ, pri = gr
+    n = len(ops)
+    deps = [set(d) for d in deps]
+    pri = [pri[i] + (bonus if ops[i]["h"] == 0 else 0.0) + offs.get(ops[i]["cls"], 0.0) for i in range(n)]
+    left = [len(d) for d in deps]
+    end = [0.0] * n
+    free, bank, order = {}, {}, []
+    rdy = {}
+    for i in range(n):
+        if left[i] == 0:
+            rdy[i] = 0.0
+    while rdy:
+        est, mins = {}, {}
+        for i, s in rdy.items():
+            o = ops[i]
+            q = o["q"]
+            f = free.get(q, 0.0) if q else 0.0
+            if f > s:
+                s = f
+            for b in o["banks"]:
+                for e, j in bank.get(b, {}).items():
+                    if e != q and end[j] + WAKE > s:
+                        s = end[j] + WAKE
+            est[i] = s
+            if s < mins.get(q, 1e9):
+                mins[q] = s
+        q = min(mins, key=lambda k: mins[k])
+        i = min([k for k in est if ops[k]["q"] == q], key=lambda k: est[k] - window * pri[k])
+        o, s = ops[i], est[i]
+        for b in o["banks"]:
+            for e, j in bank.get(b, {}).items():
+                if e != q:
+                    deps[i].add(j)
+            bank.setdefault(b, {})[q] = i
+        if q:
+            free[q] = s + o["cost"]
+        end[i] = s + o["cost"] + o.get("lat", 0.0)
+        o["start"] = s
+        order.append(i)
+        del rdy[i]
+        for k in succ[i]:
+            left[k] -= 1
+            if left[k] == 0:
+                rdy[k] = max(end[j] + (OWN if ops[j]["q"] == ops[k]["q"] else WAKE) for j in deps[k])
+    assert len(order) == n
+    return deps, order, max(end)
+
+
+def plan(offs=None, bonus=None, window=None):
+    gr = graph()
+    ops = gr[0]
+    deps, order, span = schedule(gr, OFFS if offs is None else offs, BONUS if bonus is None else bonus, WINDOW if window is None else window)
+    count = {}
+    for i in order:
+        o = ops[i]
+        if o.get("sem", "").startswith(("in", "out")):
+            o["ev"] = (o["sem"], 16)
+        elif "arr" in o:
+            o["ev"] = (o["arr"], None)
+        elif "send" in o:
+            o["ev"] = None
+        else:
+            s = "q" + o["q"]
+            count[s] = count.get(s, 0) + 1
+            o["ev"] = (s, count[s])
+    return ops, deps, order, count, span
+
+
+_PLAN = []
+
+
+def rank_program(g, core, T, topo):
+    rank = T.rank_of(core)
+    if rank is None:
+        return
+    if not _PLAN:
+        _PLAN.append(plan())
+    ops, deps, order, count, _ = _PLAN[0]
+    n = len(T.cores)
+    nxt, prv = T.cores[(rank + 1) % n], T.cores[(rank - 1) % n]
+
+    def engines(a, b):
+        return topo.engines(a, b)
+    mask = topo.mask(core, nxt)
+    n_in, n_out = len(engines(prv, core)), len(engines(core, nxt))
+    rid, pid = topo.addr(nxt)[:2]
+    queues = {"v": g.vector, "a": g.scalar, "t": g.tensor, "g": g, "s": g.sync}
+    seen = {}
+    sent = 0
+    for i in order:
+        o = ops[i]
+        if o["q"] is None:
+            continue
+        q = queues[o["q"]]
+        need = {}
+        for j in deps[i]:
+            ev = ops[j]["ev"]
+            if ev is not None:
+                need[ev[0]] = max(need.get(ev[0], 0), n_in if ev[1] is None else ev[1])
+        for s in sorted(need):
+            if seen.get((o["q"], s), 0) < need[s]:
+                q.wait_ge(T.sem[s], need[s])
+                seen[o["q"], s] = need[s]
+        if "send" in o:
+            t, h, k = o["send"]
+            a, b, w = {"L": (128 * h, 128 * h + 128, "L"), "Z": (192 * h, 192 * h + 64, "Z"), "N": (192 * h + 64, 192 * h + 192, "Z")}[k]
+            g.remote_dma(T["%s%d" % (w, t + 1)][:, a:b], T["S%s%d" % (w, t)][:, a:b], T.sem["arr_%d_%d_%s" % (t + 1, h, k)], T.sem.loc, pid, rid, mask)
+            sent += n_out
+            continue
+        r = o["fn"](g, T)
+        r.then_inc(T.sem[o["ev"][0]], 16 if o["ev"][0].startswith(("in", "out")) else 1)
+    for s in sorted(count):
+        g.wait_ge(T.sem[s], count[s])
+    for k in range(8):
+        g.wait_ge(T.sem["out%d" % k], 16)
+    g.wait_ge(T.sem.loc, sent)

@@ -2,384 +2,554 @@ import numpy as np
 from concourse.mybir import AluOpType as OP, ActivationFunctionType as AF
 
 NT = 5
-NH = 2
+NS = 2
 NPK = 64
 NB = 16 * NPK
 NPC = 2
 PCB = NB // NPC
 PCK = NPK // NPC
+ROUND32 = 1.5 * 2.0 ** 28
 
-SCRATCH = {"X": ("sbuf", [128, 4096], "bfloat16"), "ia": ("sbuf", [128, 128], "int32"), "ib": ("sbuf", [128, 128], "int32"),
-           "wc": ("sbuf", [128, 1], "bfloat16"), "r32": ("sbuf", [128, 1], "float32"), "ri": ("sbuf", [128, 1], "int32"),
-           "rj": ("sbuf", [128, 1], "int32"), "mi": ("sbuf", [128, 64], "int32"), "mj": ("sbuf", [128, 64], "int32"),
-           "base0": ("sbuf", [128, 64], "float32"), "Q": ("sbuf", [128, 144], "bfloat16"),
-           "zmask": ("sbuf", [128, NB], "bfloat16"), "K32": ("sbuf", [128, NT], "float32"), "ks": ("sbuf", [128, 2 * NT], "float32"),
-           "SI": ("sbuf", [128, 256], "float32")}
-F32 = ("P", "dhs", "Hc", "thr", "m", "s1", "cho", "um", "sc", "P2", "ad", "hsb", "spoh", "kset")
-I32 = ("S", "ci", "ui", "u12", "u5", "gx", "gs", "S2", "fx", "pc", "od2")
+OPT = {"h": "R2 R2", "o": "F1 F1 F1 F1", "c": "F1 F1 F1 F1", "cabs": "A", "ch": "a2 v2", "zexp": "v2 v2", "zlast": "g2 g2", "cmp": "s", "tmp": "v", "zbuf": "g", "yv": "v", "spoh": "v", "fin": "v", "tsplit": 16, "m": "v", "dup": (0, 0), "msg": 3, "cho": "v"}
+QB = NB // 4
+
+SCALED = {"nI": -1.0, "p8I": 8192.0, "n8I": -8192.0, "n4I": -4096.0, "p4I": 4096.0, "c2080": 2080.0, "c1184": 1184.0, "c32": 32.0,
+          "c32768": 32768.0, "c100": 100.0 / 128, "c200": 200.0 / 128, "cB": 61440.0, "hI": 0.5, "n3I": -3.0, "cG": 1.0 / 8192}
+MATS = ["n2", "ones", "bt", "I", "BM", "TRI", "TRIm", "TRIp", "BMs", "Sw", "hSw", "Wb0", "Wb1"] + sorted(SCALED)
+TILES = {"k2048": 2048.0, "kL2": 65536.0 - 8388608.0, "k155": -15.5, "kys": 155.0 / 128, "kn4": -4096.0}
+SCRATCH = {"MAT": ("sbuf", [128, 128 * len(MATS)], "bfloat16"), "KT": ("sbuf", [128, 64 * (len(TILES) + 1)], "bfloat16"),
+           "I32": ("sbuf", [128, 128], "float32"), "nI32": ("sbuf", [128, 128], "float32"), "SO2": ("sbuf", [128, 128], "float32"),
+           "KI": ("sbuf", [128, 128], "float16"), "ri": ("sbuf", [128, 4], "int32"), "rf": ("sbuf", [128, 4], "float32"),
+           "mi": ("sbuf", [128, 64], "int32"), "mj": ("sbuf", [128, 64], "int32"), "bi": ("sbuf", [128, 8], "float32"),
+           "base": ("sbuf", [128, 8], "bfloat16"), "zmask": ("sbuf", [128, PCB], "bfloat16"), "ks": ("sbuf", [128, 2 * NT], "float32"),
+           "SO": ("sbuf", [128, 512], "float32"), "iab": ("sbuf", [128, 256], "int32"), "abn": ("sbuf", [128, 256], "float16"),
+           "zn": ("sbuf", [128, 128], "bfloat16"), "wn": ("sbuf", [128, 1], "bfloat16")}
+for _n in ("Q", "Q2", "nQ"):
+    SCRATCH[_n] = ("sbuf", [128, 144], "bfloat16")
+F32 = ("P", "dhs", "thr", "m", "tmp", "d", "accd", "q", "spoh", "P2")
+I32 = ("S", "ci", "ui", "u12", "S2", "fx", "pc", "so")
+B16 = ("set", "rec", "w", "am", "yv", "acc", "inc", "sp", "dm", "sc")
 SMALL = {}
-for _n in ("ones", "bt", "BM", "I", "nI", "n8I", "c91", "c200", "n300", "n3I", "TRI", "TRI16", "Wb"):
-    SCRATCH[_n] = ("sbuf", [128, 128], "bfloat16")
-SCRATCH["o16f"] = ("sbuf", [128, 128], "float32")
 for _t in range(NT):
-    SCRATCH["L%d" % _t] = ("sbuf", [128, 256], "float32")
+    SCRATCH["L%d" % _t] = ("sbuf", [128, 256], "uint16")
     SCRATCH["Z%d" % _t] = ("sbuf", [128, 384], "bfloat16")
-    SCRATCH["SL%d" % _t] = ("sbuf", [128, 256], "float32")
-    SCRATCH["SZ%d" % _t] = ("sbuf", [128, 384], "bfloat16")
-for _h in range(NH):
-    for _n in ("zbuf", "zexp", "hr", "ha", "od", "orl", "cd", "cabs", "ch", "Mf"):
-        SCRATCH["%s_%d" % (_n, _h)] = ("sbuf", [128, NB], "bfloat16")
-    SCRATCH["ho16_%d" % _h] = ("sbuf", [128, 128], "uint16")
+    if _t < NT - 1:
+        SCRATCH["SL%d" % _t] = ("sbuf", [128, 256], "uint16")
+        SCRATCH["SZ%d" % _t] = ("sbuf", [128, 384], "bfloat16")
+for _s in range(NS):
+    SCRATCH["X%d" % _s] = ("sbuf", [128, 4096], "bfloat16")
+    for _n in ("zbuf", "zexp", "hr", "ha", "od", "oa", "cd", "ca", "ch", "Mf"):
+        SCRATCH["%s_%d" % (_n, _s)] = ("sbuf", [128, NB], "bfloat16")
+    if OPT["zexp"] == "":
+        SCRATCH["zexp_%d" % _s] = ("sbuf", [128, NPK, 16], "bfloat16")
+    SCRATCH["HO_%d" % _s] = ("sbuf", [128, 128], "float16")
+    for _n in ("t32", "fxc"):
+        SCRATCH["%s_%d" % (_n, _s)] = ("sbuf", [128, 64], "float16")
     for _n in ("c16", "ch16"):
-        SCRATCH["%s_%d" % (_n, _h)] = ("sbuf", [128, 64], "uint16")
-    SCRATCH["u16_%d" % _h] = ("sbuf", [128, 4], "uint16")
-    for _i, _n in enumerate(F32):
-        SMALL["%s_%d" % (_n, _h)] = ("F_%d" % _h, 64 * _i)
-    SCRATCH["F_%d" % _h] = ("sbuf", [128, 64 * len(F32)], "float32")
-    for _i, _n in enumerate(I32):
-        SMALL["%s_%d" % (_n, _h)] = ("J_%d" % _h, 64 * _i)
-    SCRATCH["J_%d" % _h] = ("sbuf", [128, 64 * len(I32)], "int32")
-    for _n in ("set", "rec", "w", "am", "yv", "acc", "inc", "sp", "dm"):
-        SCRATCH["%s_%d" % (_n, _h)] = ("sbuf", [128, 64], "bfloat16")
+        SCRATCH["%s_%d" % (_n, _s)] = ("sbuf", [128, 64], "uint16")
+    SCRATCH["u16_%d" % _s] = ("sbuf", [128, 8], "uint16")
+    SCRATCH["gx_%d" % _s] = ("sbuf", [128, 128], "float32")
+    SCRATCH["gs_%d" % _s] = ("sbuf", [128, 128], "int32")
+    for _b, _l, _d in (("F", F32, "float32"), ("J", I32, "int32"), ("B", B16, "bfloat16")):
+        for _i, _n in enumerate(_l):
+            SMALL["%s_%d" % (_n, _s)] = ("%s_%d" % (_b, _s), 64 * _i)
+        SCRATCH["%s_%d" % (_b, _s)] = ("sbuf", [128, 64 * len(_l)], _d)
 for _b in range(8):
     SCRATCH["ps%d" % _b] = ("psum", [128, 512], "float32")
 
-SEMAPHORES = ["qv", "qa", "qt", "qg", "loc"] + ["in%d" % _i for _i in range(7)] + ["out%d" % _i for _i in range(8)] + \
-    ["arr_%d_%d_%s" % (_t, _h, _k) for _t in range(1, NT) for _h in range(NH) for _k in "LZN"]
+NIN, NOUT = 20, 16
+SEMAPHORES = ["qv", "qa", "qt", "qg", "loc"] + ["in%d" % _i for _i in range(NIN)] + ["out%d" % _i for _i in range(NOUT)] + \
+    ["arr_%d_%d_%s" % (_t, _s, _k) for _t in range(1, NT) for _s in range(NS) for _k in "LZNW"]
 
 PS = {}
-for _h in range(NH):
-    for _i, _n in enumerate(("dh", "do", "dc", "dhp", "V", "cnt", "cntv", "u")):
-        PS[_n, _h] = (2 + _h, _i)
-    for _i, _n in enumerate(("H", "L", "OH", "L2", "O1", "zd", "cnt2", "hsum")):
-        PS[_n, _h] = (4 + _h, _i)
-    for _i, _n in enumerate(("CH", "d", "tmp")):
-        PS[_n, _h] = (6, 3 * _h + _i)
-    for _i, _n in enumerate(("incs", "Gs", "In", "I2")):
-        PS[_n, _h] = (7, 4 * _h + _i)
-PS["mask", 0] = (6, 6)
+for _s in range(NS):
+    for _b, _l in ((2, ("dh u", "do v", "pen r", "cnt off", "cntv", "ys", "Gs", "cnt2")),
+                   (4, ("dc", "V", "zd kp", "I2", "Mh", "Mh2", "H2 k0", "k1")),
+                   (6, ("Hp", "L L2", "OH", "CH", "cho", "d2", "tmpP O2", "spP"))):
+        for _i, _n in enumerate(_l):
+            for _m in _n.split():
+                PS[_m, _s] = (_b + _s, _i)
 
-CY = 0.83e-3 * 1.2
-PCY = 0.55 * 1e-3
-GA = 1.6
-WAKE, OWN = 0.16, 0.16
-BONUS, WINDOW = 0, 0.005
-OFFS = {'zbuf_1': -2.0, 'ps4:L20': -2.2, 'dhs_1': 1.0, 'ps5:H1': -3.1, 'ps5:L21': -2.0, 'hsb_1': -10.0, 'ps5:OH1': 15.0, 'ps6:tmp1': 11.0,
-        'Hc_1': 8.0, 'od_0.0': -3.0, 'od_1.0': 4.0, 'ps4:OH0': -4.0, 'ps5:hsum1': 14.0, 'ps6:tmp0': -2.0, 'hr_1.0': -2.2, 'send_0_zg': 2.0,
-        'gx_1': 2.5, 'fx_0': 4.0, 'P_0': -11.0, 'zexp_1.0': 10.0, 'u5_0': -2.0, 'acc_0': 5.0, 'ho16_1': -14.0, 'zbuf_0': -10.0, 'S2_0': -2.0,
-        'spoh_1': -8.4, 'm_0': -3.0, 'ps7:incs0': -2.0, 'fx_1': -8.0, 'cabs_1.1': -4.0, 'hr_1.1': -5.6, 'sp_0': 8.0, 'rec_1': -9.0,
-        'zexp_1.1': -9.0, 'hr_0.1': 5.0, 'inc_0': 8.0, 'ps4:H0': 1.5, 'orl_1.0': 3.0, 'cabs_1.0': -5.0, 'ch_0.1': -3.0, 'kset_0': -6.0,
-        'zexp_0.1': -6.4, 'od_1.1': -5.0, 'acc_1': -14.0, 'ps5:L1': -1.6, 'ps5:O11': 10.0, 'dhs_0': 6.0, 'ad_0': -11.0, 'cd_1.1': -7.0,
-        'orl_0.1': 8.0, 'cho_1': 4.0, 'ps7:Gs1': 18.0, 'u16_0': -4.0, 'orl_0.0': -3.0}
-HOP = 5.2
+FIG = {"cy": 1.0e-3, "pcy": 0.55e-3, "ga": 1.6, "sca": 4.0, "wake": 0.16, "hop": 5.5, "dma": 400.0, "issue": 0.3}
+PHASE = """S:-1 l0:-0.71 gh0:-0.49 zbuf:-0.32 zexp1:-0.17 zexp0:0.04 look:0.1 HO:0.17 Hp:0.22 P:0.25 OH:0.44 L:0.45 yh0:0.55 ci:0.65 yh1:0.83 gh1:1.01 c16:1.05 gc1:1.18 go0:1.28 ah0:1.33 gc0:1.34 yo0:1.97 ac0:2.13 ah1:2.18 dh:2.26 ao1:2.33 go2:2.36 ac1:2.38 dh2:2.51 set:2.59 ao0:2.61 ao2:2.61 pen:2.61 do:2.62 thr:2.63 go1:2.79 dc:3.52 m:3.52 w:3.79 rec:4.04 CH:4.21 am:4.21 tmp:4.26 cnt:4.31 d:4.44 cho0:4.49 cho:4.57 ch16:4.94 gch1:4.95 gch0:5.09 hsum:5.47 lag:6 M1:6.41 M0:6.61 yv:6.85 u:7.03 ui:7.04 V:7.23 acc:7.25 sp:7.46 u12:7.49 L2:7.63 P2:7.71 cnt2:7.74 pc:7.83 d2:7.93 S2:7.93 fx:8.16 accd:8.16 out1:8.32 pre:8.38 ad:8.38 cntv:8.55 lh:8.61 lo:8.62 zd:8.75 out2:8.75 O16:8.83 H16:8.83 out0:8.83 out3:8.83 out4:8.83 out6:8.83 out7:8.83 so:8.92 zz:8.98 out5:9.04 sendL:9.05 ys:9.15 sendZ:9.31 spoh:9.32 q:10.1 sendN:11.41 Gs:11.44 I2:11.67 out10:11.75 t32:11.87 dm:11.89 kp:11.9 KI:11.91 out11:11.93 out12:11.95 r:12 out13:12 out15:12 out8:12 out9:12 out14:12.27 sc:12.36 v:12.64 I2p:12.65 off:12.67 u16:12.85 G:12.87 gx:13.07 Mh:13.31 Mh2:13.31 gs:13.4 inc:13.47 scat:13.54 period:18.07
+a0:-1 b0:-1 z0:-2 z1:-1.5 wp:9 Wb:9.5 I:-200 set_ones:-201 Sw:-150 abn:-140"""
+PHASE = """a0:-12.24 b0:-12.24 z0:-8.07 zbuf:-7.35 HO:-7.29 gh0:-7.2 zexp1:-6.88 c16:-6.85 S:-6.61 Hp:-5.92 nQ:-5.7 z1:-5.56 ci:-5.48 ri1:-5.1 set_k155:-4.8 L2:-4.46 gc3:-4.39 yh1:-4.36 mi:-4.2 l0:-4.17 L:-4.15 hSw:-4.1 OH:-3.5 set:-3.49 gc1:-3.37 ah1:-3.31 set_n2f:-3.3 yh0:-3.16 P:-2.93 go2:-2.93 zexp0:-2.67 abn:-2.4 dh:-2.17 set_ones:-1.6 go3:-1.28 bi:-1.1 gh1:-0.93 go0:-0.89 ao3:-0.84 set_kys:-0.8 go1:-0.37 CH:-0.32 ah0:-0.31 ao2:-0.12 ac3:-0.12 cho:-0.1 look:0 ao1:0.08 lag3:0.1 gc0:0.11 lag4:0.15 ac0:0.25 ao0:0.26 do:0.28 ac1:0.29 gc2:0.33 ac2:0.36 dc:0.38 ri0:0.4 pen:0.51 I:0.8 lag1:0.83 m:0.91 rec:0.98 d:1.06 yo0:1.09 TRIp:1.2 lag0:1.28 am:1.33 cho0:1.47 gch1:1.49 cnt:1.52 ch16:1.6 set_zmask:1.6 V:1.62 yv:1.63 TRIm:1.9 M0:2.31 lag2:2.34 hI:2.4 tmp:2.46 thr:2.48 M1:2.51 base:2.6 w:2.64 wp:2.8 dh2:2.9 set_kL2:3.4 u:3.55 ui:3.57 Q:3.7 BMs:3.8 cG:4 c2080:4.3 set_zbuf_0:4.3 I32:4.3 c200:4.4 S2:4.43 out4:4.63 c100:4.7 Wb:4.9 hsum:5.32 set_Q:5.8 H16:6.48 u12:6.49 rf0:6.5 mj:6.5 set_k2048:6.5 P2:6.58 pre:6.71 rf2:6.8 sp:6.93 Sw:7 out0:7.07 c32:7.1 TRI:7.3 gch0:7.37 lag:7.48 inc:7.76 d2:7.79 n3I:7.8 bt:7.8 fx:8.03 ys:8.09 cntv:8.11 set_zbuf_1:8.4 out2:8.47 out10:8.63 out8:8.73 out14:8.79 so:8.83 out6:8.94 acc:9.01 q:9.07 accd:9.17 pc:9.18 spoh:9.18 lh:9.19 c32768:9.2 lo:9.29 t32:9.38 nI:9.5 BM:9.8 out3:10 r:10.25 out12:10.27 p8I:10.3 cB:10.4 zz:10.47 out5:10.47 rf1:10.5 sendL:10.74 O16:10.78 out7:10.98 c1184:11 mk:11.1 out11:11.28 ad:11.35 I2:11.67 v:11.91 out1:12.09 u16:12.14 Gs:12.3 cnt2:13.41 sendZ:13.47 off:14.15 gs:14.23 out13:14.71 kp:14.88 out9:15.33 sendN:15.66 KI:15.85 dm:15.94 I2p:16.19 out15:16.91 scat:17.36 Mh2:17.44 Mh:17.54 gx:17.75 zd:17.83 period:18.31 G:19.07 sc:21.92"""
+PHASE = """b0:-18.36 a0:-16.39 HO:-12.38 P:-12.37 zbuf:-11.2 z0:-10.53 z1:-9.56 l0:-9.41 S:-8.84 L:-7.8 zexp0:-7.55 go3:-7.39 ci:-7.29 zexp1:-7 Hp:-6.8 set_zbuf_1:-5.9 gh0:-5.76 ri0:-5.6 go1:-5.4 TRIm:-5.1 nQ:-4.8 c16:-4.74 mj:-4.5 n3I:-4.5 lag4:-4.15 yh1:-4.12 yh0:-3.8 c200:-3.8 mi:-3.5 set_zmask:-2.7 set_ones:-2.5 w:-2.21 Sw:-2.2 OH:-2.17 ah1:-1.8 ah0:-1.56 gc1:-1.53 dc:-1.49 go2:-1.48 gc3:-1.42 am:-1.29 gh1:-1.12 gc0:-1 base:-1 L2:-0.97 set:-0.96 go0:-0.95 yo0:-0.94 ao3:-0.94 cnt:-0.94 abn:-0.9 gch0:-0.86 set_kys:-0.8 ao2:-0.76 ao0:-0.71 set_n2f:-0.7 ao1:-0.61 ac1:-0.6 BMs:-0.6 ac3:-0.55 hSw:-0.4 dh2:-0.28 do:-0.28 dh:-0.27 CH:-0.22 ch16:-0.22 Q:-0.2 yv:-0.18 tmp:-0.07 cho0:-0.06 look:0 rec:0.07 gc2:0.34 Gs:0.38 cntv:0.48 gch1:0.54 cho:0.58 acc:0.88 ys:0.88 m:0.97 I:1 rf2:1.1 BM:1.1 M1:1.3 G:1.33 sp:1.43 set_zbuf_0:1.5 I32:1.9 lag0:1.91 lag3:2.27 bt:2.3 hI:2.4 ac0:2.42 pen:2.44 ac2:2.82 d2:3.03 lag1:3.16 thr:3.23 set_k155:3.3 TRIp:3.6 out4:3.61 S2:3.97 lag2:3.98 cG:4 ad:4.07 p8I:4.7 H16:5.59 u12:5.8 set_Q:5.8 set_k2048:5.9 out0:5.93 d:5.97 Wb:6.3 M0:6.45 rf0:6.5 c32:7.1 accd:7.23 TRI:7.3 fx:7.51 pc:7.66 set_kL2:7.7 pre:7.72 out5:7.74 c1184:8.1 out10:8.54 lag:8.58 out8:8.72 c100:8.9 out6:8.94 P2:8.99 u:9.03 so:9.13 c32768:9.2 ri1:9.3 hsum:9.4 nI:9.5 bi:9.6 c2080:9.7 out2:9.76 spoh:9.98 r:10.14 cB:10.4 dm:10.41 rf1:10.5 O16:10.51 cnt2:10.54 out7:10.55 q:10.61 out14:10.73 lo:10.78 ui:10.93 V:11 wp:11 mk:11.1 lh:11.12 out12:11.12 sendL:11.34 inc:11.56 out3:11.81 out11:11.82 out1:11.83 ri2:11.9 gs:12.93 u16:13.07 t32:13.47 sendZ:13.47 v:14.29 out13:14.58 out9:14.75 kp:15.63 KI:15.85 sendN:16.41 period:16.56 sc:16.88 zd:17.38 I2p:17.38 Mh2:17.44 gx:17.6 out15:17.64 scat:18.05 I2:19.02 off:19.91 zz:20.02 Mh:20.42"""
+PHASE = """HO:-18.85 l0:-18.37 OH:-17.42 b0:-16.71 z1:-16.48 Hp:-16.06 L:-16.01 a0:-15.57 z0:-14.45 ci:-10.65 c16:-10.6 zbuf:-9.63 gh0:-9.63 zexp1:-9.28 gc3:-7.91 gc2:-7.89 go1:-7.41 S:-7.21 lag4:-6.68 go3:-5.94 set_zbuf_1:-5.9 bt:-5.8 rf1:-5.7 CH:-5.6 TRIp:-5.5 TRI:-5.5 wp:-5.5 nQ:-4.8 set_k2048:-4.6 mj:-4.5 BMs:-4.4 Sw:-4.3 p8I:-4.3 P:-3.64 Wb:-3.6 ri0:-3 go2:-2.88 ao3:-2.72 set_ones:-2.5 Q:-2.2 dh:-1.91 c1184:-1.9 cG:-1.7 base:-1.4 gh1:-1.12 gc1:-1.09 abn:-1 ao2:-0.96 gc0:-0.87 lag0:-0.8 ao1:-0.76 ao0:-0.75 ah0:-0.7 gch0:-0.59 zexp0:-0.55 V:-0.45 ch16:-0.24 ah1:-0.14 ac1:-0.03 look:0 lag3:0.28 dc:0.31 c200:0.6 pen:0.79 hsum:0.88 mk:1 go0:1.1 BM:1.1 set:1.32 do:1.39 set_zbuf_0:1.5 L2:1.64 thr:1.86 set_Q:2 hSw:2.1 yh1:2.13 hI:2.4 c100:2.5 yh0:2.57 w:2.73 cnt:2.74 rec:2.76 thr2:2.8 gch1:3.05 am:3.16 n3I:3.4 ac3:4.01 cho:4.07 ac0:4.41 dhs:4.41 lag2:4.42 m:4.89 yv:5.36 ac2:5.55 out4:5.67 set_kL2:5.8 out0:5.83 TRIm:6 c32:6.1 ys:6.71 Gs:6.71 sp:6.72 cntv:6.76 t32:6.92 S2:6.95 dm:7.3 u:7.37 mi:7.7 ui:7.77 out5:7.86 tmp:7.91 cho0:7.92 cnt2:8.23 out6:8.48 out10:8.57 u12:8.6 fx:8.63 pc:8.64 so:8.65 spoh:8.75 P2:8.83 I:8.9 bi:9 kp:9.41 G:9.46 nI:9.5 out8:9.52 set_zmask:9.7 c2080:9.7 d:9.83 out2:9.97 pre:9.99 ri1:10.1 d2:10.15 cB:10.4 rf0:10.6 lag:10.95 M0:11.15 lag1:11.25 zd:11.3 rf2:11.4 out7:11.46 zz:11.68 set_k155:11.8 ri2:11.9 q:11.95 out11:12.11 M1:12.12 v:12.51 period:12.75 out1:12.86 accd:12.91 ad:12.92 KI:12.92 out12:12.94 out14:13.15 out3:13.92 sendZ:14.15 H16:14.24 out9:14.95 O16:15.24 Mh2:16.5 sendL:16.59 r:16.61 I2p:16.69 sendN:16.75 gs:17.04 off:17.22 out13:17.72 out15:18 lh:19.13 u16:19.53 acc:19.95 Mh:20.56 sc:20.68 I2:20.87 gx:21.06 lo:21.78 inc:21.83 scat:24.89"""
 
 
-def build():
+def build(opt):
     ops = []
-    cur = {"h": None, "t": -1}
+    cur = {"s": None, "t": -1}
 
-    def add(q, cost, fn, r, w, **kw):
-        ops.append(dict(q=q, cost=cost, fn=fn, r=list(r), w=list(w), h=cur["h"], t=cur["t"], **kw))
-
-    def ps(name, h, T):
-        b, i = PS[name, h]
-        return T["ps%d" % b][:, 64 * i:64 * i + 64]
+    def add(q, fn, r, w, fx=0.0, cy=0.0, ga=0, sca=0, tc=0, **kw):
+        ops.append(dict(q=q, fn=fn, r=list(r), w=list(w), s=cur["s"], t=cur["t"], c=(fx, cy, ga, sca, tc), **kw))
 
     def full(name):
         return (name, lambda T: T[name][:])
 
-    def pk(name, h):
-        return ("ps%d:%s%d" % (PS[name, h][0], name, h), lambda T: ps(name, h, T))
-
-    def sb(name, h):
-        n = "%s_%d" % (name, h)
-        if n in SMALL:
-            b, c = SMALL[n]
-            return (n, lambda T: T[b][:, c:c + 64])
-        return (n, lambda T: T[n][:])
-
     def cols(name, a, b, step=1, key=None):
         return (key or name, lambda T: T[name][:, a:b:step] if step != 1 else T[name][:, a:b])
 
+    def mat(name, a=0, b=128):
+        i = 128 * MATS.index(name)
+        return cols("MAT", i + a, i + b, key=name)
+
+    def tile(name):
+        i = 64 * (sorted(TILES) + ["mk"]).index(name)
+        return cols("KT", i, i + 64, key=name)
+
+    def pk(name, s, a=0, b=64):
+        bank, i = PS[name, s]
+        return ("ps%d:%d" % (bank, i), lambda T: T["ps%d" % bank][:, 64 * i + a:64 * i + b])
+
+    def sb(name, s):
+        n = "%s_%d" % (name, s)
+        if n in SMALL:
+            return cols(SMALL[n][0], SMALL[n][1], SMALL[n][1] + 64, key=n)
+        return full(n)
+
     def inps(x):
-        return x[0].startswith("ps")
+        return (x[0] if isinstance(x[0], str) else x[0][0]).startswith("ps")
 
-    def tt(out, a, b, op, n=64):
-        c = max(64, n * (1 if inps(a) or inps(b) else 2))
-        add("v", c * CY, lambda g, T: g.vector.tensor_tensor(out[1](T), a[1](T), b[1](T), op), [a[0], b[0]], [out[0]])
+    def num(x):
+        return isinstance(x, (int, float))
 
-    def ts(out, a, s1, op0, s2=None, op1=None, n=64, half=False, extra=()):
-        c = max(64, n * (0.5 if half else 1))
+    def tt(name, out, a, b, op, n=64):
+        add("v", lambda g, T: g.vector.tensor_tensor(out[1](T), a[1](T), b[1](T), op), [a[0], b[0]], [out[0]],
+            cy=max(64, n * (1 if inps(a) or inps(b) else 2)), name=name)
 
+    def ts(name, out, a, s1, op0, s2=None, op1=None, n=64):
         def fn(g, T):
-            sc = s1(T) if callable_(s1) else s1
+            sc = s1 if num(s1) else s1[1](T)
             if op1 is None:
                 return g.vector.tensor_scalar(out[1](T), a[1](T), sc, None, op0)
             return g.vector.tensor_scalar(out[1](T), a[1](T), sc, s2, op0, op1)
-        add("v", c * CY, fn, [a[0]] + list(extra), [out[0]])
+        add("v", fn, [a[0]] + ([] if num(s1) else [s1[0]]), [out[0]], cy=max(64, n), name=name)
 
-    def callable_(x):
-        return not isinstance(x, (int, float))
+    def cp(name, out, a, n=64):
+        add("v", lambda g, T: g.vector.tensor_copy(out[1](T), a[1](T)), [a[0]], [out[0]], cy=max(64, n), name=name)
 
-    def cp(out, a, n=64):
-        add("v", max(64, n) * CY, lambda g, T: g.vector.tensor_copy(out[1](T), a[1](T)), [a[0]], [out[0]])
+    def scan(name, out, d0, d1, op1, n):
+        add("v", lambda g, T: g.vector.tensor_tensor_scan(out[1](T), d0[1](T), d1[1](T), 0.0, OP.mult, op1), [d0[0], d1[0]], [out[0]],
+            cy=max(64, n), name=name)
 
-    def act(out, a, func, scale=1.0, bias=0.0, n=64, extra=(), accum=None):
+    def act(name, out, a, func, scale=1.0, bias=0.0, n=64, accum=None, ga=0):
         def fn(g, T):
             kw = {}
-            if scale != 1.0 or callable_(scale):
-                kw["scale"] = scale(T) if callable_(scale) else scale
+            if scale != 1.0:
+                kw["scale"] = scale
             if bias != 0.0:
                 kw["bias"] = bias
             if accum is not None:
                 kw["accum_out"] = accum[1](T)
             return g.scalar.activation(out[1](T), a[1](T), func, **kw)
-        add("a", max(64, n) * CY + 0.02, fn, [a[0]] + list(extra), [out[0]] + ([accum[0]] if accum is not None else []))
+        add("a", fn, [a[0]], [out[0]] + ([accum[0]] if accum is not None else []), fx=0.065 if ga else 0.02, cy=0 if ga else max(64, n),
+            ga=ga, name=name)
 
-    def mm(out, terms):
+    def mm(name, out, terms, first=True, last=True, after=()):
         def fn(g, T):
             r = None
-            for k, (l, x, n, f) in enumerate(terms):
-                r = g.tensor.matmul(out[1](T), l[1](T), x[1](T), k == 0, k == len(terms) - 1)
+            for k, x in enumerate(terms):
+                o = x[4] if len(x) > 4 else out
+                r = g.tensor.matmul(o[1](T), x[0][1](T), x[1][1](T), first and k == 0, last and k == len(terms) - 1)
             return r
-        keys = []
-        for l, x, n, f in terms:
-            for y in (l, x):
-                for kk in (y[0] if isinstance(y[0], (list, tuple)) else [y[0]]):
-                    if kk not in keys:
-                        keys.append(kk)
-        add("t", sum(max(64, n) * f for l, x, n, f in terms) * PCY, fn, keys, [out[0]])
+        tc = sum(max(64, x[3] if len(x) > 3 else 64) * (x[2] if len(x) > 2 else 1) for x in terms)
+        add("t", fn, [y[0] for x in terms for y in x[:2]] + list(after), [out[0]], tc=tc, name=name, first=first, last=last)
 
-    def f1(l, x, n=64):
-        return (full(l), x, n, 1)
+    def f32(l, x):
+        return (full(l), x, 4)
 
-    def f4(l, x, n=64):
-        return (full(l), x, n, 4)
+    def window(s, lst):
+        return (["X%d" % s, lst[0]], lambda T: T["X%d" % s][:, 0:4096].indirect(lst[1](T)))
 
-    def gather_v(out, lst, z, n):
-        add("v", 0.05 + n * GA * CY, lambda g, T: g.vector.tensor_tensor(out[1](T), T.X[:, 0:4096].indirect(lst[1](T)), z[1](T), OP.subtract),
-            ["X0", "X1", lst[0], z[0]], [out[0]])
+    def memset(out, val, n, again=False):
+        add("v", lambda g, T: g.vector.memset(out[1](T), val), [out[0]] if again else [], [out[0]], cy=max(64, n), name="set_" + out[0])
 
-    def gather_a(out, lst, n):
-        add("a", 0.065 + n * GA * CY, lambda g, T: g.scalar.activation(out[1](T), T.X[:, 0:4096].indirect(lst[1](T)), AF.Copy),
-            ["X0", "X1", lst[0]], [out[0]])
+    nd = {"in": 0, "out": 0}
 
-    def memset(name, val, n, sl=None, key=None):
-        add("v", max(64, n) * CY, lambda g, T: g.vector.memset(sl(T) if sl is not None else T[name][:], val), [], [key or name])
-
-    def dma(q, sem, out, src, cost):
+    def dma(q, kind, out, src, lat):
         def fn(g, T):
-            return (g.sync if q == "s" else g.scalar).dma_start(out[1](T), src[1](T))
-        add(q, 0.1, fn, [src[0]] if src[0] else [], [out[0]], sem=sem, lat=cost)
+            return {"s": g.sync, "a": g.scalar, "g": g}[q].dma_start(out[1](T), src[1](T))
+        add(q, fn, [src[0]], [out[0]], fx=0.1, sem="%s%d" % (kind, nd[kind]), lat=lat, name=kind + str(nd[kind]))
+        nd[kind] += 1
 
-    def piece(name, h, p):
-        n = "%s_%d" % (name, h)
-        return ("%s.%d" % (n, p), lambda T: T[n][:, p * PCB:(p + 1) * PCB])
+    def piece(name, s, p):
+        if name == "zexp" and opt["zexp"] == "":
+            return (["%s_%d.%d" % (name, s, k) for k in range(*p)], lambda T: T["zexp_%d" % s][:, 16 * p[0]:16 * p[1], :])
+        return cols("%s_%d" % (name, s), p[0] * QB, p[1] * QB, key=["%s_%d.%d" % (name, s, k) for k in range(*p)])
 
-    def col16(name, h, j):
-        n = "%s_%d" % (name, h)
-        return (["%s.%d" % (n, p) for p in range(NPC)], lambda T: T[n][:, j:NB:16])
+    def col16(name, s, j):
+        n = "%s_%d" % (name, s)
+        return (["%s.%d" % (n, p) for p in range(4)], lambda T: T[n][:, j:NB:16])
 
-    dma("s", "in0", full("ia"), (None, lambda T: T.ba[:]), 2.0)
-    dma("a", "in1", full("ib"), (None, lambda T: T.bb[:]), 2.0)
-    dma("s", "in2", ("X0", lambda T: T.X[:, 0:2048]), (None, lambda T: T.xt[:, 0:2048]), 5.0)
-    dma("a", "in3", ("X1", lambda T: T.X[:, 2048:4096]), (None, lambda T: T.xt[:, 2048:4096]), 5.0)
-    for h in range(NH):
-        dma("s", "in%d" % (4 + h), cols("Z0", 192 * h, 192 * h + 64, key="z0_%d" % h), (None, lambda T, h=h: T.zp[:, 64 * h:64 * h + 64]), 2.2)
-    dma("s", "in6", full("wc"), (None, lambda T: T.wl[:]), 2.2)
-    gp = lambda fn, r, w: add("g", 0.5, fn, r, w, sem="qg")
-    memset("ones", 1.0, 128)
-    gp(lambda g, T: g.affine_select(T.I[:], T.ones[:], [[-1, 128]], OP.is_equal, 0.0, 0, 1), ["ones"], ["I"])
-    gp(lambda g, T: g.affine_select(T.bt[:], T.ones[:], [[-16, 8], [0, 16]], OP.is_ge, 0.0, 0, 1), ["ones"], ["bt"])
-    gp(lambda g, T: g.affine_select(T.BM[:], T.bt[:], [[16, 8], [0, 16]], OP.is_ge, 0.0, 15, -1), ["bt"], ["BM"])
-    gp(lambda g, T: g.affine_select(T.TRI[:], T.BM[:], [[1, 128]], OP.is_gt, 0.0, 0, -1), ["BM"], ["TRI"])
-    for h in range(NH):
-        memset("zbuf_%d" % h, 0.0, NB // 2)
-        memset("Z0", 0.0, 64, sl=lambda T, h=h: T.Z0[:, 192 * h + 64:192 * h + 192], key="ig0_%d" % h)
-    memset("zmask", 1.0, NB // 2)
-    memset("zmask", 0.0, 64, sl=lambda T: T.zmask[:, 0:NB:16])
-    ops[-1]["r"].append("zmask")
-    memset("Q", 0.0, 144)
-    add("v", 64 * CY, lambda g, T: g.vector.tensor_copy(T.Q[:, 15:143:16], T.BM[:, 0:128:16]), ["BM", "Q"], ["Q"])
-    act(full("nI"), full("I"), AF.Copy, scale=-1.0, n=128)
-    act(full("n8I"), full("I"), AF.Copy, scale=-8192.0, n=128)
-    ts(full("TRI16"), full("I"), -16.0, OP.mult, n=128, half=True)
-    tt(full("TRI16"), full("TRI16"), full("TRI"), OP.add, n=128)
-    act(full("c91"), full("I"), AF.Copy, scale=91.0, n=128)
-    act(full("c200"), full("I"), AF.Copy, scale=200.0, n=128)
-    act(full("n300"), full("I"), AF.Copy, scale=-300.0, n=128)
-    act(full("n3I"), full("I"), AF.Copy, scale=-3.0, n=128)
-    ts(full("Wb"), full("BM"), lambda T: T.wc[:], OP.mult, n=128, half=True, extra=["wc"])
-    gp(lambda g, T: g.iota(T.mi[:], [[-1, 64]], 64, 1), [], ["mi"])
-    gp(lambda g, T: g.iota(T.ri[:], [[0, 1]], 0, 1), [], ["ri"])
-    gp(lambda g, T: g.iota(T.base0[:], [[512, 4], [0, 16]], 0, 0, allow_small_or_imprecise_dtypes=True), [], ["base0"])
-    ts(full("mj"), full("mi"), 15, OP.bitwise_and)
-    ts(pk("mask", 0), full("mj"), 0.0, OP.is_equal)
-    ts(full("rj"), full("ri"), 15, OP.bitwise_and)
-    ts(full("r32"), full("rj"), 32.0, OP.mult)
-    memset("o16f", 0.0625, 128)
+    def cuts(text):
+        out, a = [], 0
+        for x in text.split():
+            out.append((x[0], (a, a + int(x[1])), int(x[1]) * QB))
+            a += int(x[1])
+        return out
 
-    for h in range(NH):
-        cp(cols("L0", 128 * h, 128 * h + 64, key="l0_%d" % h), cols("ia", 64 * h, 64 * h + 64))
-        cp(cols("L0", 128 * h + 64, 128 * h + 128, key="l0_%d" % h), cols("ib", 64 * h, 64 * h + 64))
+    def part(name, c, a, b, key):
+        return (key, lambda T: T[name][64 * c:64 * c + 64, a:b])
+
+    dma("s", "in", cols("iab", 0, 128, key="ia"), (None, lambda T: T.ba[:]), 100)
+    dma("a", "in", cols("iab", 128, 256, key="ib"), (None, lambda T: T.bb[:]), 200)
+    dma("s", "in", full("zn"), (None, lambda T: T.zp[:]), 270)
+    xin = [[], []]
+    kb = 270
+    for s in range(NS):
+        for c in range(0 if opt["dup"][s] else 2):
+            kb += 512
+            xin[s].append("Xin%d.%d" % (s, c))
+            dma("as"[c], "in", part("X%d" % s, c, 0, 4096, xin[s][-1]), part("xt", s, 0, 4096, None), kb + 512 * (1 - c))
+        for k in range(4 if opt["dup"][s] else 0):
+            for c in ([s] if k < opt["dup"][s] else [s, 1 - s]):
+                kb += 128
+                xin[s].append("Xin%d.%d.%d" % (s, k, c))
+                dma("a" if len(xin[0] + xin[1]) in (1, 3) else "s", "in", part("X%d" % s, c, 1024 * k, 1024 * k + 1024, xin[s][-1]),
+                    part("xt", s, 1024 * k, 1024 * k + 1024, None), kb)
+        if s == 0:
+            dma("s", "in", full("wn"), (None, lambda T: T.wl[:]), kb + 30)
+    def gp(fn, r, w, n):
+        add("g", fn, r, w, fx=0.17, cy=2 * n, name=w[0])
+    memset(mat("ones"), 1.0, 64)
+    sel = lambda o, i, pat, cmp, b, ch: gp(lambda g, T: g.affine_select(mat(o)[1](T), mat(i)[1](T), pat, cmp, 0.0, b, ch), [i], [o], 128)
+    sel("I", "ones", [[-1, 128]], OP.is_equal, 0, 1)
+    sel("bt", "ones", [[-16, 8], [0, 16]], OP.is_ge, 0, 1)
+    sel("BM", "bt", [[16, 8], [0, 16]], OP.is_ge, 15, -1)
+    sel("TRI", "BM", [[1, 128]], OP.is_gt, 0, -1)
+    gp(lambda g, T: g.iota(T.mi[:], [[-1, 64]], 64, 1), [], ["mi"], 64)
+    gp(lambda g, T: g.iota(T.ri[:, 0:1], [[0, 1]], 0, 1), [], ["ri0"], 1)
+    gp(lambda g, T: g.iota(T.bi[:], [[2048, 2], [512, 4]], 0, 0, allow_small_or_imprecise_dtypes=True), [], ["bi"], 8)
+    for s in range(NS):
+        memset(full("zbuf_%d" % s), 0.0, NB // 2)
+    memset(full("zmask"), 1.0, PCB // 2)
+    memset(cols("zmask", 0, PCB, 16), 0.0, 64, again=True)
+    for n in sorted(TILES):
+        memset(tile(n), TILES[n], 64)
+    for n in sorted(SCALED):
+        ts(n, mat(n), mat("I"), SCALED[n], OP.mult)
+    memset(full("Q"), 0.0, 72)
+    i0 = 128 * MATS.index("BM")
+    cp("Q", cols("Q", 15, 143, 16), cols("MAT", i0, i0 + 128, 16, key="BM"))
+    ops[-1]["r"].append("Q")
+    ts("Q2", full("Q2"), full("Q"), -2.0, OP.mult, n=72)
+    ts("nQ", full("nQ"), full("Q"), -1.0, OP.mult, n=72)
+    for n, v in (("TRIm", -16.0), ("TRIp", 16.0)):
+        ts(n, mat(n), mat("I"), v, OP.mult)
+        tt(n, mat(n), mat(n), mat("TRI"), OP.add, n=128)
+    ts("BMs", mat("BMs"), mat("BM"), (1.0 if opt["yv"] == "a" else 2.0) / 128, OP.mult)
+    cp("Sw", mat("Sw", 0, 64), mat("I", 64, 128))
+    cp("Sw", mat("Sw", 64, 128), mat("I", 0, 64))
+    ts("hSw", mat("hSw"), mat("Sw"), 0.5, OP.mult)
+    act("I32", full("I32"), mat("I"), AF.Copy, n=128)
+    act("nI32", full("nI32"), mat("I"), AF.Copy, scale=-1.0, n=128)
+    memset(mat("n2"), -2.0, 64)
+
+    def rows(x, s):
+        return (x[0], lambda T: x[1](T)[64 * s:64 * s + 64, :])
+
+    def spread(s, src, a):
+        return [(rows(mat("I" if c == s else "Sw"), s), rows(cols(src, a + 64 * c, a + 64 * c + 64), s)) for c in range(2)]
+    for s in range(NS):
+        wp = pk("spP", 1, s, s + 1)
+        mm("wp", wp, [(rows(mat(n), s), rows(full("wn"), s)) for n in ("I", "Sw")])
+        ts("Wb", mat("Wb%d" % s), mat("BM"), wp, OP.mult)
+    ts("abn", full("abn"), (["ia", "ib"], lambda T: T.iab[:]), -2048.0, OP.add, n=256)
+    nb = 0
+    for s in range(NS):
+        for k in range(2 * opt["dup"][s]):
+            b = ((0, 1, 3, 5) if s == 0 else (0, 1))[nb % (4 - 2 * s)]
+            nb += 1
+            bank = (["ps%d:y" % b] if b < 2 else ["ps%d:%d" % (b, i) for i in range(8)], lambda T, b=b, s=s: T["ps%d" % b][64 - 64 * s:128 - 64 * s, :])
+            src = part("X%d" % s, s, 512 * k, 512 * k + 512, "Xin%d.%d.%d" % (s, k // 2, s))
+            mm("dup", bank, [(rows(mat("I", 64 * s, 64 * s + 64), s), src, 1, 512)])
+            xin[s].append("Xd%d.%d" % (s, k))
+            dst = part("X%d" % s, 1 - s, 512 * k, 512 * k + 512, xin[s][-1])
+            if k % 2:
+                act("dupa", dst, bank, AF.Copy, n=512)
+            else:
+                cp("dupv", dst, bank, n=512)
+    ts("mj", full("mj"), full("mi"), 15, OP.bitwise_and)
+    ts("mk", tile("mk"), full("mj"), 0.0, OP.not_equal, -64.0, OP.mult)
+    ts("ri1", cols("ri", 1, 2, key="ri1"), cols("ri", 0, 1, key="ri0"), 15, OP.bitwise_and)
+    ts("ri2", cols("ri", 2, 3, key="ri2"), cols("ri", 0, 1, key="ri0"), 64, OP.bitwise_and)
+    tt("rf0", cols("rf", 0, 1, key="rf0"), cols("ri", 1, 2, key="ri1"), cols("ri", 2, 3, key="ri2"), OP.add, n=1)
+    tt("rf1", cols("rf", 1, 2, key="rf1"), cols("ri", 1, 2, key="ri1"), cols("ri", 2, 3, key="ri2"), OP.subtract, n=1)
+    ts("rf2", cols("rf", 2, 4, key="rf2"), (["rf0", "rf1"], lambda T: T.rf[:, 0:2]), 32.0, OP.mult)
+    for c in range(2):
+        ts("base", cols("base", 4 * c, 4 * c + 4), cols("bi", 4 * c, 4 * c + 4), cols("rf", 2 + c, 3 + c, key="rf2"), OP.add)
+    I, nI = mat("I"), mat("nI")
 
     for t in range(NT):
-        last = t == NT - 1
-        scat = []
-        for h in range(NH):
-            cur["h"], cur["t"] = h, t
-            lk, zk, ik = "l%d_%d" % (t, h), "z%d_%d" % (t, h), "ig%d_%d" % (t, h)
-            ca, cb = 128 * h + 64 * (t % 2), 128 * h + 64 * (1 - t % 2)
-            LH, LO = cols("L%d" % t, ca, ca + 64, key=lk), cols("L%d" % t, cb, cb + 64, key=lk)
-            z = cols("Z%d" % t, 192 * h, 192 * h + 64, key=zk)
-            Iold = cols("Z%d" % t, 192 * h + 64, 192 * h + 128, key=ik)
-            Gold = cols("Z%d" % t, 192 * h + 128, 192 * h + 192, key=ik)
+        last, splice = t == NT - 1, t >= 2
+        for s in range(NS):
+            cur["s"], cur["t"] = s, t
+            lk, zk, ik, X = "l%d_%d" % (t, s), "z%d_%d" % (t, s), "ig%d_%d" % (t, s), "X%d" % s
+            ca, cb = 64 * (t % 2), 64 * (1 - t % 2)
+            Hc, Oc = cols("HO_%d" % s, ca, ca + 64), cols("HO_%d" % s, cb, cb + 64)
+            z = cols("Z%d" % t, 192 * s, 192 * s + 64, key=zk)
+            Iold = cols("Z%d" % t, 192 * s + 64, 192 * s + 128, key=ik)
+            Gold = cols("Z%d" % t, 192 * s + 128, 192 * s + 192, key=ik)
+            lists = cols("L%d" % t, 128 * s, 128 * s + 128, key=lk)
             if t > 0:
-                add(None, 0.0, None, ["send_%d_%d_L" % (t - 1, h)], [lk], arr="arr_%d_%d_L" % (t, h), lat=HOP)
-                add(None, 0.0, None, ["send_%d_%d_Z" % (t - 1, h)], [zk], arr="arr_%d_%d_Z" % (t, h), lat=HOP)
-                add(None, 0.0, None, ["send_%d_%d_N" % (t - 1, h)], [ik], arr="arr_%d_%d_N" % (t, h), lat=HOP)
-            cp(sb("ho16", h), cols("L%d" % t, 128 * h, 128 * h + 128, key=lk), n=128)
-            add("a", 64 * CY, lambda g, T, h=h, z=z: g.scalar.activation(T["zbuf_%d" % h][:, 0:NB:16], z[1](T), AF.Copy), [zk, "zbuf_%d" % h], ["zbuf_%d" % h])
-            act(sb("Hc", h), LH, AF.Copy, bias=-2048.0)
-            act(pk("O1", h), LO, AF.Copy, bias=32.0)
-            act(pk("L", h), LO, AF.Copy, scale=3232.0, bias=65536.0 - 8388608.0)
-            act(pk("H", h), LH, AF.Copy)
-            tt(sb("P", h), sb("Hc", h), pk("O1", h), OP.mult)
-            tt(sb("S", h), sb("P", h), pk("L", h), OP.add)
-            tt(pk("OH", h), LO, pk("H", h), OP.subtract)
-            ts(sb("ci", h), sb("S", h), 5, OP.arith_shift_right, 4095, OP.bitwise_and)
-            cp(sb("c16", h), sb("ci", h))
-            ts(sb("set", h), pk("OH", h), 0.0, OP.is_equal)
-            for p in range(NPC):
-                ze = piece("zexp", h, p)
-                add("v", PCB / 2 * CY, lambda g, T, h=h, p=p: g.vector.tensor_tensor_scan(
-                    T["zexp_%d" % h][:, p * PCB:(p + 1) * PCB], T.zmask[:, 0:PCB], T["zbuf_%d" % h][:, p * PCB:(p + 1) * PCB], 0.0, OP.mult, OP.add),
-                    ["zmask", "zbuf_%d" % h], [ze[0]])
-            lst = lambda name, a, h=h: (lambda p: ("%s_%d" % (name, h), lambda T: T["%s_%d" % (name, h)][:, a + p * PCK:a + (p + 1) * PCK]))
-            lh, lo, lc, lch = lst("ho16", 64 * (t % 2)), lst("ho16", 64 * (1 - t % 2)), lst("c16", 0), lst("ch16", 0)
-            for p in range(NPC):
-                gather_a(piece("hr", h, p), lh(p), PCB)
-                yb = ("ps%d:y" % p, lambda T, p=p: T["ps%d" % p][:, 0:PCB])
-                mm(yb, [f1("I", piece("hr", h, p), PCB), f1("nI", piece("zexp", h, p), PCB)])
-                act(piece("ha", h, p), yb, AF.Abs, n=PCB)
-            for p in range(NPC):
-                gather_v(piece("od", h, p), lo(p), piece("zexp", h, p), PCB)
-                act(piece("orl", h, p), piece("od", h, p), AF.Abs, n=PCB)
-            for p in range(NPC):
-                gather_v(piece("cd", h, p), lc(p), piece("zexp", h, p), PCB)
-                act(piece("cabs", h, p), piece("cd", h, p), AF.Abs, n=PCB)
-            q = lambda j: ("Q", lambda T, j=j: T.Q[:, 15 - j:143 - j])
-            mm(pk("dh", h), [(q(j), col16("ha", h, j), 64, 1) for j in range(16)])
-            mm(pk("do", h), [(q(j), col16("orl", h, j), 64, 1) for j in range(16)])
-            mm(pk("dc", h), [(q(j), col16("cabs", h, j), 64, 1) for j in range(16)])
-            act(sb("dhs", h), pk("dh", h), AF.Copy)
-            mm(pk("dhp", h), [f1("n8I", Gold), f1("n8I", sb("set", h))])
-            tt(sb("thr", h), sb("dhs", h), pk("do", h), OP.min)
-            tt(sb("thr", h), sb("thr", h), pk("dhp", h), OP.add)
-            tt(sb("w", h), pk("dc", h), sb("thr", h), OP.is_lt)
-            mm(pk("cnt", h), [f1("TRI16", sb("w", h))])
-            tt(sb("m", h), sb("dhs", h), pk("dc", h), OP.min)
-            tt(sb("rec", h), pk("do", h), sb("m", h), OP.is_le)
-            tt(pk("CH", h), sb("ci", h), pk("H", h), OP.subtract)
-            tt(pk("tmp", h), sb("rec", h), pk("OH", h), OP.mult)
-            tt(sb("s1", h), LH, pk("tmp", h), OP.add)
-            ts(sb("am", h), pk("cnt", h), -13.0, OP.is_lt)
-            tt(pk("d", h), sb("am", h), pk("CH", h), OP.mult)
-            tt(sb("cho", h), sb("s1", h), pk("d", h), OP.add)
-            tt(pk("d", h), sb("cho", h), pk("H", h), OP.subtract)
-            cp(sb("ch16", h), sb("cho", h))
-            for p in range(NPC):
-                gather_a(piece("ch", h, p), lch(p), PCB)
-                add("v", PCB / 2 * CY, lambda g, T, h=h, p=p: g.vector.tensor_tensor_scan(
-                    T["Mf_%d" % h][:, p * PCB:(p + 1) * PCB], T.zmask[:, 0:PCB], T["ch_%d" % h][:, p * PCB:(p + 1) * PCB], 0.0, OP.mult, OP.max),
-                    ["zmask", "ch_%d.%d" % (h, p)], ["Mf_%d.%d" % (h, p)])
-            M = (["Mf_%d.%d" % (h, p) for p in range(NPC)], lambda T, h=h: T["Mf_%d" % h][:, 15:NB:16])
-            mm(pk("u", h), [f1("Wb", M)])
-            cp(sb("ui", h), pk("u", h))
-            if not last:
-                ts(sb("u5", h), sb("ui", h), 31, OP.bitwise_and)
-                tt(sb("um", h), sb("u5", h), pk("mask", 0), OP.mult)
-                add("v", 64 * CY, lambda g, T, sc=sb("sc", h)[1], um=sb("um", h)[1]: g.vector.tensor_tensor_scan(
-                    sc(T), T.base0[:], um(T), 0.0, OP.max, OP.add), ["base0", "um_%d" % h], ["sc_%d" % h])
-                fb, fc = SMALL["sc_%d" % h]
-                ts(sb("u16", h), ("sc_%d" % h, lambda T, fb=fb, fc=fc: T[fb][:, fc + 15:fc + 64:16]), lambda T: T.r32[:], OP.add, extra=["r32"])
-                win = lambda T, h=h: T.X[:, 2048 * h:2048 * h + 2048].indirect(T["u16_%d" % h][:, 0:4])
-                add("v", 0.05 + 64 * GA * CY, lambda g, T, gx=sb("gx", h)[1], win=win, M=M: g.vector.tensor_tensor(gx(T), win(T), M[1](T), OP.add),
-                    ["X%d" % h, "u16_%d" % h] + M[0], ["gx_%d" % h])
-                ts(sb("gs", h), sb("gx", h), 1, OP.arith_shift_right)
-                scat.append(("v", 0.05 + 64 * 4 * CY, lambda g, T, gs=sb("gs", h)[1], win=win: g.vector.tensor_copy(win(T), gs(T)),
-                             ["gs_%d" % h, "u16_%d" % h, "X%d" % h], ["X%d" % h]))
-            mm(pk("hsum", h), [(full("I"), col16("hr", h, j), 64, 1) for j in range(16)])
-            act(sb("hsb", h), pk("hsum", h), AF.Copy)
-            mm(pk("V", h), [(full("I"), col16("ch", h, j), 64, 1) for j in range(16)])
-            tt(sb("yv", h), pk("V", h), sb("hsb", h), OP.is_ge)
-            mm(pk("cntv", h), [f1("BM", sb("yv", h))])
-            ts(sb("acc", h), pk("cntv", h), 9.0, OP.is_ge)
-            grow = [f1("c91", sb("rec", h)), f1("c91", sb("am", h)), f1("c200", sb("set", h)), f1("BM", sb("yv", h))]
-            mm(pk("dhp", h), [f1("n300", Iold)] + grow)
-            ts(sb("sp", h), pk("dhp", h), -500.0, OP.is_lt)
-            mm(pk("cnt2", h), [f1("TRI", sb("sp", h))])
-            mm(pk("incs", h), grow)
-            ts(sb("inc", h), pk("incs", h), 100.0, OP.is_lt)
-            sl, sz = "SL%d" % t, "SZ%d" % t
-            sh = "send_%d_%d" % (t, h)
-            tt(pk("tmp", h), sb("set", h), pk("H", h), OP.mult)
-            ts(sb("u12", h), sb("ui", h), 4095, OP.bitwise_and)
-            tt(sb("P2", h), sb("u12", h), pk("tmp", h), OP.mult)
-            tt(sb("spoh", h), sb("sp", h), pk("OH", h), OP.mult)
-            tt(pk("CH", h), sb("sp", h), pk("CH", h), OP.mult)
-            cp(sb("pc", h), pk("cnt2", h))
-            ts(sb("od2", h), sb("pc", h), 1, OP.bitwise_and)
-            tt(pk("CH", h), sb("od2", h), pk("CH", h), OP.mult)
-            tt(pk("tmp", h), pk("CH", h), sb("spoh", h), OP.subtract)
-            tt(pk("d", h), sb("acc", h), pk("d", h), OP.mult)
-            act(pk("L2", h), LO, AF.Copy, scale=32.0, bias=-8388608.0)
-            if t > 0:
-                act(sb("kset", h), sb("set", h), AF.Identity, scale=lambda T, t=t: T.K32[:, t - 1:t], extra=["K32.%d" % (t - 1)])
-                tt(pk("L2", h), sb("kset", h), pk("L2", h), OP.add)
-            tt(sb("S2", h), sb("P2", h), pk("L2", h), OP.add)
-            ts(sb("fx", h), sb("S2", h), 5, OP.arith_shift_right, 4095, OP.bitwise_and)
-            tt(cols(sl, cb, cb + 64, key=sh + "_lo"), sb("fx", h), pk("tmp", h), OP.add)
-            tt(sb("ad", h), LH, pk("d", h), OP.add)
-            tt(cols(sl, ca, ca + 64, key=sh + "_lh"), sb("ad", h), pk("CH", h), OP.add)
-            mm(pk("I2", h), [f1("I", Iold), f1("I", sb("inc", h)), f1("n3I", sb("sp", h))])
-            mm(pk("Gs", h), [f1("c91", sb("am", h)), f1("c200", Gold), f1("BM", sb("yv", h))])
-            if last:
-                act(cols("SI", 128 * h, 128 * h + 64, key="si%d" % h), pk("I2", h), AF.Copy)
-                ts(cols("SI", 128 * h + 64, 128 * h + 128, key="sg%d" % h), pk("Gs", h), 100.0, OP.is_ge)
-                ka, kb = sh + "_lh", sh + "_lo"
-                dma("s", "out%d" % (4 * h), (None, lambda T, h=h: T.yi[:, 64 * h:64 * h + 64]), cols("SI", 128 * h, 128 * h + 64, key="si%d" % h), 2.0)
-                dma("s", "out%d" % (4 * h + 1), (None, lambda T, h=h: T.yg[:, 64 * h:64 * h + 64]), cols("SI", 128 * h + 64, 128 * h + 128, key="sg%d" % h), 2.0)
-                dma("s", "out%d" % (4 * h + 2), (None, lambda T, h=h: T.ya[:, 64 * h:64 * h + 64]), cols(sl, ca, ca + 64, key=ka), 2.0)
-                dma("s", "out%d" % (4 * h + 3), (None, lambda T, h=h: T.yb[:, 64 * h:64 * h + 64]), cols(sl, cb, cb + 64, key=kb), 2.0)
+                for k, key in (("L", lk), ("Z", zk), ("N", ik)) if opt["msg"] == 3 else (("L", lk), ("W", [zk, ik])):
+                    add(None, None, ["send_%d_%d_%s" % (t - 1, s, k)], [key], arr="arr_%d_%d_%s" % (t, s, k), name="arr" + k)
+                ts("HO", sb("HO", s), lists, -2048.0, OP.add)
             else:
-                act(cols(sz, 192 * h + 64, 192 * h + 128, key=sh + "_zi"), pk("I2", h), AF.Copy)
-                ts(cols(sz, 192 * h + 128, 192 * h + 192, key=sh + "_zg"), pk("Gs", h), 100.0, OP.is_ge)
-                mm(pk("zd", h), [f1("I", z), f1("nI", M)])
-                act(cols(sz, 192 * h, 192 * h + 64, key=sh + "_zz"), pk("zd", h), AF.Abs)
-                act(sb("dm", h), sb("acc", h), AF.Copy, accum=cols("ks", 2 * t + h, 2 * t + h + 1, key="ks%d_%d" % (t, h)))
-                add("g", 0.3, None, [sh + "_zz"], [sh + "_Z"], send=(t, h, "Z"))
-                add("g", 0.3, None, [sh + "_zi", sh + "_zg"], [sh + "_N"], send=(t, h, "N"))
-                add("g", 0.3, None, [sh + "_lo", sh + "_lh"], [sh + "_L"], send=(t, h, "L"))
-        for x in scat:
-            add(*x)
+                mm("a0", pk("Mh", s), spread(s, "abn", 0))
+                mm("b0", pk("Mh2", s), spread(s, "abn", 128))
+                mm("z0", pk("zd", s), spread(s, "zn", 0))
+                ab = ([pk("Mh", s)[0], pk("Mh2", s)[0]], pk("Mh", s, 0, 128)[1])
+                ts("l0", lists, ab, 2048.0, OP.add, n=128)
+                cp("HO", sb("HO", s), ab, n=128)
+                act("z1", z, pk("zd", s), AF.Copy)
+                add(None, None, xin[s], [X], name="X0")
+            zb = cols("zbuf_%d" % s, 0, NB, 16)
+            if opt["zexp"] == "":
+                zx = "zexp_%d" % s
+                zq = ["%s.%d" % (zx, k) for k in range(4)]
+                for j in range(2):
+                    add("g", lambda g, T, zx=zx, z=z, j=j: g.affine_select(T[zx][:, :, j], z[1](T), [[0, 64]], OP.is_equal, 0.0, 0, 0),
+                        [zk], zq, fx=0.17, cy=128, name="zx%d" % j)
+                for j in (2, 4):
+                    add("g", lambda g, T, zx=zx, j=j: g.affine_select(T[zx][:, :, j:2 * j], T[zx][:, :, 0:j], [[0, 64], [0, j]], OP.is_equal, 0.0, 0, 0),
+                        zq, zq, fx=0.17, cy=128 * j, name="zx%d" % j)
+                for k, (e, p, n) in enumerate(cuts(opt["zlast"])):
+                    a, b = 16 * p[0], 16 * p[1]
+                    if e == "g":
+                        add("g", lambda g, T, zx=zx, a=a, b=b: g.affine_select(T[zx][:, a:b, 8:16], T[zx][:, a:b, 0:8], [[0, b - a], [0, 8]], OP.is_equal, 0.0, 0, 0),
+                            zq[p[0]:p[1]], zq[p[0]:p[1]], fx=0.17, cy=n, name="zy%d" % k)
+                    else:
+                        cp("zy%d" % k, (zq[p[0]:p[1]], lambda T, zx=zx, a=a, b=b: T[zx][:, a:b, 8:16]), (zq[p[0]:p[1]], lambda T, zx=zx, a=a, b=b: T[zx][:, a:b, 0:8]), n=n // 4)
+            elif opt["zbuf"] == "g":
+                add("g", lambda g, T, zb=zb, z=z: g.affine_select(zb[1](T), z[1](T), [[0, 64]], OP.is_equal, 0.0, 0, 0), [zk, zb[0]], [zb[0]],
+                    fx=0.17, cy=128, name="zbuf")
+            else:
+                act("zbuf", zb, z, AF.Copy)
+                ops[-1]["r"].append(zb[0])
+            for k, (e, p, n) in enumerate(cuts(opt["zexp"])):
+                scan("zexp%d" % k, piece("zexp", s, p), cols("zmask", 0, n), cols("zbuf_%d" % s, p[0] * QB, p[1] * QB), OP.add, n // 2)
+            mm("Hp", pk("Hp", s), [(I, Hc), (I, tile("k2048"))])
+            mm("L", pk("L", s), [(mat("c2080"), Hc), (mat("c1184"), Oc)])
+            mm("OH", pk("OH", s), [(I, Oc), (nI, Hc)])
+            tt("P", sb("P", s), Oc, pk("Hp", s), OP.mult)
+            tt("S", sb("S", s), sb("P", s), pk("L", s), OP.add)
+            ts("ci", sb("ci", s), sb("S", s), 5, OP.arith_shift_right, 4095, OP.bitwise_and)
+            cp("c16", sb("c16", s), sb("ci", s))
+            ts("set", sb("set", s), pk("OH", s), 0.0, OP.is_equal)
+            tt("CH", pk("CH", s), sb("ci", s), pk("Hp", s), OP.subtract)
+
+            def lst(name, a, p, key=None):
+                return cols(name, a + p[0] * 16, a + p[1] * 16, key=key)
+            ny = 0
+            for nm, raw, ab, l in (("h", "hr", "ha", lambda p: lst("L%d" % t, 128 * s + ca, p, lk)),
+                                   ("o", "od", "oa", lambda p: lst("L%d" % t, 128 * s + cb, p, lk)),
+                                   ("c", "cd", "ca", lambda p: lst("c16_%d" % s, 0, p))):
+                for k, (e, p, n) in enumerate(cuts(opt[nm])):
+                    w, o, ze = window(s, l(p)), piece(raw, s, p), piece("zexp", s, p)
+                    if e == "R":
+                        act("g%s%d" % (nm, k), o, w, AF.Copy, ga=n)
+                        yb = ("ps%d:y" % (ny % 2), lambda T, b=ny % 2, n=n: T["ps%d" % b][:, 0:n])
+                        ny += 1
+                        mm("y%s%d" % (nm, k), yb, [(I, o, 1, n), (nI, ze, 1, n)])
+                        act("a%s%d" % (nm, k), piece(ab, s, p), yb, AF.Abs, n=n)
+                    else:
+                        add("v", lambda g, T, o=o, w=w, ze=ze: g.vector.tensor_tensor(o[1](T), w[1](T), ze[1](T), OP.subtract),
+                            [w[0], ze[0]], [o[0]], fx=0.05, ga=n, name="g%s%d" % (nm, k))
+                        if nm == "c" and opt["cabs"] == "R":
+                            ts("a%s%d" % (nm, k), piece(ab, s, p), o, 0.0, OP.max, n=n // 2)
+                        else:
+                            act("a%s%d" % (nm, k), piece(ab, s, p), o, AF.Abs, n=n)
+            qs = lambda q, name: [((q, lambda T, j=j: T[q][:, 15 - j:143 - j]), col16(name, s, j)) for j in range(16)]
+
+            def long(name, out, terms, first=True, last=True, after=()):
+                k = opt["tsplit"]
+                for a in range(0, 16, k):
+                    mm(name if a + k == 16 else "%s_%d" % (name, a), out, terms[a:a + k], first and a == 0, last and a + k == 16, after)
+            df = opt["cmp"] == "d"
+            if df:
+                long("dh", pk("do", s), qs("Q", "ha"), last=False)
+                long("dh2", pk("dc", s), qs("Q", "ha"), last=False)
+                mm("pen", pk("do", s), [(mat("p8I"), sb("set", s))], first=False, last=False)
+            else:
+                long("dh", pk("dh", s), qs("nQ", "ha"))
+                act("dhs", sb("dhs", s), pk("dh", s), AF.Copy)
+                mm("pen", pk("do", s), [(mat("p8I"), sb("set", s))], last=False)
+            long("do", pk("do", s), qs("nQ", "oa"), first=False)
+            if opt["cabs"] == "R":
+                long("dc0", pk("dc", s), qs("Q", "cd"), first=not df, last=False)
+                long("dc", pk("dc", s), qs("Q2", "ca"), first=False)
+            else:
+                long("dc", pk("dc", s), qs("nQ", "ca"), first=not df)
+            if not df:
+                tt("thr", pk("pen", s) if t else sb("thr", s), pk("do", s), sb("dhs", s), OP.max)
+                if t:
+                    tt("thr2", sb("thr", s), pk("pen", s), Gold, OP.add)
+            elif t:
+                tt("thr", sb("thr", s), pk("do", s), Gold, OP.max)
+            else:
+                ts("thr", sb("thr", s), pk("do", s), 0.0, OP.max)
+            tt("w", sb("w", s), pk("dc", s), sb("thr", s), OP.is_gt)
+            mm("cnt", pk("cnt", s), [(mat("TRIm"), sb("w", s))])
+            if not df:
+                tt("m", sb("m", s), pk("dc", s), sb("dhs", s), OP.max)
+            elif opt["m"] == "a":
+                act("m", sb("m", s), pk("dc", s), AF.Relu)
+            else:
+                ts("m", sb("m", s), pk("dc", s), 0.0, OP.max)
+            tt("rec", sb("rec", s), pk("do", s), sb("m", s), OP.is_ge)
+            if opt["tmp"] == "a":
+                mm("tmpP", pk("tmpP", s), [(I, Oc), (nI, Hc), (mat("p8I"), sb("rec", s))])
+                act("tmp", sb("tmp", s), pk("tmpP", s), AF.Relu, bias=-4096.0)
+                mm("cho0", pk("cho", s), [(I, Hc), (mat("n4I"), sb("rec", s)), f32("I32", sb("tmp", s))], last=False)
+            elif opt["cho"] == "t":
+                tt("tmp", sb("tmp", s), sb("rec", s), pk("OH", s), OP.mult)
+                mm("cho0", pk("cho", s), [(I, Hc), f32("I32", sb("tmp", s))], last=False)
+            ts("am", sb("am", s), pk("cnt", s), -13.0, OP.is_lt)
+            if opt["cho"] == "t":
+                tt("d", sb("d", s), sb("am", s), pk("CH", s), OP.mult)
+                mm("cho", pk("cho", s), [f32("I32", sb("d", s))], first=False)
+                ts("ch16", sb("ch16", s), pk("cho", s), 2048.0, OP.add)
+                tt("d2", pk("d2", s), pk("cho", s), Hc, OP.subtract)
+            else:
+                tt("tmp", sb("tmp", s), sb("rec", s), pk("OH", s), OP.mult)
+                tt("cho0", pk("cho", s), sb("tmp", s), pk("Hp", s), OP.add)
+                tt("d", sb("d", s), sb("am", s), pk("CH", s), OP.mult)
+                tt("cho", sb("m", s), sb("d", s), pk("cho", s), OP.add)
+                cp("ch16", sb("ch16", s), sb("m", s))
+                tt("d2", pk("d2", s), sb("m", s), pk("Hp", s), OP.subtract)
+            long("hsum", pk("V", s), [(nI, col16("hr", s, j)) for j in range(16)], last=False, after=["ch16_%d" % s])
+            for k, (e, p, n) in enumerate(cuts(opt["ch"])):
+                w, o = window(s, lst("ch16_%d" % s, 0, p)), piece("ch", s, p)
+                if e == "a":
+                    act("gch%d" % k, o, w, AF.Copy, ga=n)
+                else:
+                    add("v", lambda g, T, o=o, w=w: g.vector.tensor_copy(o[1](T), w[1](T)), [w[0]], [o[0]], fx=0.05, ga=n, name="gch%d" % k)
+                scan("M%d" % k, piece("Mf", s, p), cols("zmask", 0, n), o, OP.max, n // 2)
+            long("V", pk("V", s), [(I, col16("ch", s, j)) for j in range(16)], first=False)
+            M = (["Mf_%d.%d" % (s, p) for p in range(4)], lambda T, s=s: T["Mf_%d" % s][:, 15:NB:16])
+            Wb = mat("Wb%d" % s)
+            mm("u", pk("u", s), [(Wb, M), (mat("cB"), sb("set", s))])
+            ts("ui", sb("ui", s), pk("u", s), -61440.0, OP.add, 0.0, OP.max)
+            ts("u12", sb("u12", s), sb("ui", s), 4095, OP.bitwise_and)
+            tt("P2", sb("P2", s), sb("u12", s), pk("Hp", s), OP.mult)
+            mm("L2", pk("L2", s), [(mat("c32"), Oc), (I, tile("kL2"))] + ([(full("KI"), sb("set", s))] if t else []))
+            tt("S2", sb("S2", s), sb("P2", s), pk("L2", s), OP.add)
+            ts("fx", sb("fx", s), sb("S2", s), 5, OP.arith_shift_right, 4095, OP.bitwise_and)
+            sl, sz, sh = "SL%d" % t, "SZ%d" % t, "send_%d_%d" % (t, s)
+            if not last:
+                mm("zd", pk("zd", s), [(I, z), (nI, M)])
+                act("zz", cols(sz, 192 * s, 192 * s + 64, key=sh + "_zz"), pk("zd", s), AF.Abs)
+                if opt["msg"] == 3:
+                    add("g", None, [sh + "_zz"], [sh + "_Z"], fx=0.3, send=(t, s, "Z"), name="sendZ")
+                mm("v", pk("v", s), [(Wb, M), (I, tile("k155"))])
+                ts("t32", sb("t32", s), pk("v", s), ROUND32, OP.add, -ROUND32, OP.add)
+                mm("r", pk("r", s), [(Wb, M), (nI, sb("t32", s)), (I, tile("mk"))])
+                scan("sc", sb("sc", s), cols("zmask", 0, 64), pk("r", s), OP.max, 64)
+                b, c0 = SMALL["sc_%d" % s]
+                pick = cols(b, c0 + 15, c0 + 64, 16, key="sc_%d" % s)
+                mm("off", pk("off", s, 0, 8), [(I, full("base")), (I, pick, 1, 4, pk("off", s, 0, 4)), (mat("Sw"), pick, 1, 4, pk("off", s, 4, 8))])
+                cp("u16", sb("u16", s), pk("off", s, 0, 8))
+                mm("Mh", pk("Mh", s), [(mat("hI"), M)])
+                mm("Mh2", pk("Mh2", s), [(mat("hSw"), M)])
+                w = window(s, sb("u16", s))
+                act("gx", sb("gx", s), w, AF.Copy, scale=0.5, bias=-0.25, ga=128)
+                tt("gs", sb("gs", s), sb("gx", s), ([pk("Mh", s)[0], pk("Mh2", s)[0]], pk("Mh", s, 0, 128)[1]), OP.add, n=128)
+                add("v", lambda g, T, w=w, s=s: g.vector.tensor_copy(w[1](T), T["gs_%d" % s][:]), [w[0], "gs_%d" % s], [X], fx=0.05, sca=128, name="scat")
+            yv, votes = sb("yv", s), (mat("BMs"), sb("yv", s))
+            if opt["yv"] == "a":
+                act("yv", yv, pk("V", s), AF.Sign, bias=0.5)
+            else:
+                ts("yv", yv, pk("V", s), 0.0, OP.is_ge, 0.5, OP.subtract)
+            mm("cntv", pk("cntv", s), [votes])
+            ts("acc", sb("acc", s), pk("cntv", s), 1.0 / 128, OP.is_ge)
+            tt("accd", sb("accd", s), sb("acc", s), pk("d2", s), OP.mult)
+            mm("ys", pk("ys", s), [(mat("c100"), sb("rec", s)), (mat("c100"), sb("am", s)), (mat("c200"), sb("set", s)), votes])
+            mm("Gs", pk("Gs", s), [(mat("c100"), sb("am", s)), votes] + ([(mat("cG"), Gold)] if t else []))
+            oh = cols("SO", 256 * s + ca, 256 * s + ca + 64, key=sh + "_lh") if last else cols(sl, 128 * s + ca, 128 * s + ca + 64, key=sh + "_lh")
+            oo = cols("SO", 256 * s + cb, 256 * s + cb + 64, key=sh + "_lo") if last else cols(sl, 128 * s + cb, 128 * s + cb + 64, key=sh + "_lo")
+            oi = cols("SO", 256 * s + 128, 256 * s + 192, key=sh + "_zi") if last else cols(sz, 192 * s + 64, 192 * s + 128, key=sh + "_zi")
+            og = cols("SO", 256 * s + 192, 256 * s + 256, key=sh + "_zg") if last else cols(sz, 192 * s + 128, 192 * s + 192, key=sh + "_zg")
+            if splice:
+                sp = sb("sp", s)
+                tt("sp", sp, pk("ys", s), Iold, OP.is_lt)
+                mm("cnt2", pk("cnt2", s), [(mat("TRIp"), sp)])
+                ts("pc", sb("pc", s), pk("cnt2", s), -16.0, OP.add, 0.0, OP.max)
+                ts("so", sb("so", s), sb("pc", s), 1, OP.bitwise_and)
+                tt("q", sb("q", s), sb("so", s), pk("CH", s), OP.mult)
+                if opt["spoh"] == "a":
+                    mm("spP", pk("spP", s), [(I, Oc), (nI, Hc), (mat("p8I"), sp)])
+                    act("spoh", sb("spoh", s), pk("spP", s), AF.Relu, bias=-4096.0)
+                elif opt["fin"] == "t":
+                    tt("spoh", sb("spoh", s), sp, pk("OH", s), OP.mult)
+                else:
+                    tt("spoh", pk("spP", s), sp, pk("OH", s), OP.mult)
+                if opt["fin"] == "t":
+                    ts("fxc", sb("fxc", s), sb("fx", s), -2048.0, OP.add)
+                    mm("H20", pk("H2", s), [(I, Hc), f32("I32", sb("accd", s))], last=False)
+                    mm("H2", pk("H2", s), [f32("I32", sb("q", s))], first=False)
+                    mm("O20", pk("O2", s), [f32("nI32", sb("spoh", s)), (I, sb("fxc", s))] + ([(mat("p4I"), sp)] if opt["spoh"] == "a" else []), last=False)
+                    mm("O2", pk("O2", s), [f32("I32", sb("q", s))], first=False)
+                    ts("O16", oo, pk("O2", s), 2048.0, OP.add)
+                    ts("H16", oh, pk("H2", s), 2048.0, OP.add)
+                else:
+                    tt("pre", pk("spP", s), sb("fx", s), pk("spP", s), OP.subtract)
+                    tt("ad", pk("d2", s), sb("accd", s), pk("Hp", s), OP.add)
+                    tt("lo", oo if last else sb("P2", s), sb("q", s), pk("spP", s), OP.add)
+                    tt("lh", oh if last else sb("accd", s), sb("q", s), pk("d2", s), OP.add)
+                    if not last:
+                        cp("O16", oo, sb("P2", s))
+                        cp("H16", oh, sb("accd", s))
+            else:
+                cp("O16", oo, sb("fx", s))
+                if opt["fin"] == "t":
+                    mm("H2", pk("H2", s), [(I, Hc), f32("I32", sb("accd", s))])
+                    ts("H16", oh, pk("H2", s), 2048.0, OP.add)
+                else:
+                    tt("ad", pk("d2", s), sb("accd", s), pk("Hp", s), OP.add)
+                    cp("H16", oh, pk("d2", s))
+            if t == 0:
+                ts("inc", oi, pk("ys", s), 101.0 / 128, OP.is_lt, -155.0 / 128, OP.add)
+            else:
+                act("inc", sb("inc", s), pk("ys", s), AF.Sign, scale=-1.0, bias=101.0 / 128)
+                mm("I2p", pk("I2", s), [(I, Iold), (mat("hI"), sb("inc", s))] + ([(mat("n3I"), sb("sp", s))] if splice else []))
+                act("I2", oi, pk("I2", s), AF.Copy, bias=0.5 + (155.0 / 128 if last else 0.0))
+            if last:
+                ts("G", og, pk("Gs", s), 101.0 / 128, OP.is_ge)
+                for x, y, qq in ((oi, "yi", "ss"), (og, "yg", "ss"), (oh, "ya", "sa"), (oo, "yb", "sa")):
+                    a = 256 * s + {"ya": ca, "yb": cb, "yi": 128, "yg": 192}[y]
+                    for c in range(2):
+                        dma(qq[c], "out", part(y, s, 64 * c, 64 * c + 64, None), part("SO", c, a, a + 64, x[0]), 30)
+            else:
+                act("G", og, pk("Gs", s), AF.Relu, scale=2.0 ** 20, bias=-101.0 * 8192)
+                mm("dm", pk("k%d" % s, 1), [(mat("n2"), sb("acc", s))])
+                add("g", None, [sh + "_lo", sh + "_lh"], [sh + "_L"], fx=0.3, send=(t, s, "L"), name="sendL")
+                if opt["msg"] == 3:
+                    add("g", None, [sh + "_zi", sh + "_zg", sh + "_L"], [sh + "_N"], fx=0.3, send=(t, s, "N"), name="sendN")
+                else:
+                    add("g", None, [sh + "_zi", sh + "_zg", sh + "_zz"] + ([sh + "_L"] if opt["msg"] == 2 else []), [sh + "_W"], fx=0.3, send=(t, s, "W"), name="sendN")
         if not last:
-            kp = ("ps4:zd0", lambda T: T.ps4[:, 320:321])
-            mm(kp, [f4("o16f", cols("ks", 2 * t + h, 2 * t + h + 1, key="ks%d_%d" % (t, h)), 1) for h in range(NH)])
-            act(cols("K32", t, t + 1, key="K32.%d" % t), kp, AF.Copy, scale=-32.0, bias=32768.0)
+            kp = cols("ks", 0, 1)
+            act("kp", full("SO2"), ([pk("k0", 1)[0], pk("k1", 1)[0]], pk("k0", 1, 0, 128)[1]), AF.Copy, bias=256.0, n=128, accum=kp)
+            ts("KI", full("KI"), I, kp, OP.mult)
     return ops
 
 
-def opclass(o):
-    c = o["w"][0] if o["w"] else ""
-    for p in ("l", "z", "ig", "send_", "K32.", "ks"):
-        if o["t"] >= 0 and c.startswith(p + str(o["t"])):
-            c = p + c[len(p) + 1:].lstrip("_")
-    return c
+def cost(o, fig):
+    fx, cy, ga, sca, tc = o["c"]
+    if "send" in o:
+        return fig["issue"]
+    return fx + fig["cy"] * (cy + fig["ga"] * ga + fig["sca"] * sca) + fig["pcy"] * tc
 
 
-def graph():
-    ops = build()
+def late(o, fig):
+    return fig["hop"] + (0.5 if o["name"] == "arrW" else 0.0) if "arr" in o else 2.0 + o["lat"] / fig["dma"] if "lat" in o else 0.0
+
+
+def graph(opt):
+    ops = build(opt)
     n = len(ops)
     deps = [set() for _ in range(n)]
     lastw, readers = {}, {}
@@ -389,14 +559,17 @@ def graph():
         for k in l:
             out += keys(k) if isinstance(k, (list, tuple)) else ([k] if k else [])
         return out
-    for i, o in enumerate(ops):
+    for o in ops:
         o["r"], o["w"] = keys(o["r"]), keys(o["w"])
-        for k in o["r"]:
+    used = set(k for o in ops for k in o["r"])
+    ops = [o for o in ops if o["t"] >= 0 or used.intersection(o["w"])]
+    n = len(ops)
+    deps = deps[:n]
+    for i, o in enumerate(ops):
+        for k in o["r"] + o["w"]:
             if k in lastw:
                 deps[i].add(lastw[k])
         for k in o["w"]:
-            if k in lastw:
-                deps[i].add(lastw[k])
             deps[i].update(readers.get(k, ()))
         for k in o["r"]:
             readers.setdefault(k, []).append(i)
@@ -405,85 +578,206 @@ def graph():
             readers[k] = []
         deps[i].discard(i)
         o["banks"] = sorted(set(k.split(":")[0] for k in o["r"] + o["w"] if k.startswith("ps")))
-        o["cls"] = opclass(o)
     succ = [[] for _ in range(n)]
     for i in range(n):
         for j in deps[i]:
             succ[j].append(i)
-    pri = [0.0] * n
+    return ops, deps, succ
+
+
+def cyclic(gr, phase, fig):
+    ops, deps, succ = gr
+    n = len(ops)
+    wake = fig["wake"]
+    key = [0.0] * n
     for i in range(n - 1, -1, -1):
         o = ops[i]
-        pri[i] = o["cost"] + o.get("lat", 0.0) + 0.08 + max([pri[s] for s in succ[i]] or [0.0])
-    return ops, deps, succ, pri
-
-
-def schedule(gr, offs, bonus, window):
-    ops, deps, succ, pri = gr
-    n = len(ops)
+        if o["t"] < 0:
+            key[i] = -99.0 + i * 1e-3 if "sem" in o else min([key[k] for k in succ[i]] or [0.0]) - 3.0
+        else:
+            key[i] = o["t"] * phase["period"] + o["s"] * phase["lag"] + phase.get(o["name"], 0.0) if o["q"] else -99.0
     deps = [set(d) for d in deps]
-    pri = [pri[i] + (bonus if ops[i]["h"] == 0 else 0.0) + offs.get(ops[i]["cls"], 0.0) for i in range(n)]
     left = [len(d) for d in deps]
     end = [0.0] * n
-    free, bank, order = {}, {}, []
-    rdy = {}
-    for i in range(n):
-        if left[i] == 0:
-            rdy[i] = 0.0
+    free, bank, order, shut = {}, {}, [], set()
+    rdy = set(i for i in range(n) if left[i] == 0)
     while rdy:
-        est, mins = {}, {}
-        for i, s in rdy.items():
-            o = ops[i]
-            q = o["q"]
-            f = free.get(q, 0.0) if q else 0.0
-            if f > s:
-                s = f
-            for b in o["banks"]:
-                for e, j in bank.get(b, {}).items():
-                    if e != q and end[j] + WAKE > s:
-                        s = end[j] + WAKE
-            est[i] = s
-            if s < mins.get(q, 1e9):
-                mins[q] = s
-        q = min(mins, key=lambda k: mins[k])
-        i = min([k for k in est if ops[k]["q"] == q], key=lambda k: est[k] - window * pri[k])
-        o, s = ops[i], est[i]
+        i = min((key[k], k) for k in rdy if not (shut and ops[k]["q"] == "t" and ops[k]["first"] and ops[k]["banks"][0] in shut))[1]
+        o = ops[i]
+        q = o["q"]
         for b in o["banks"]:
             for e, j in bank.get(b, {}).items():
                 if e != q:
                     deps[i].add(j)
             bank.setdefault(b, {})[q] = i
+        if q == "t":
+            if o["last"]:
+                shut.discard(o["banks"][0])
+            else:
+                shut.add(o["banks"][0])
+        s = max([end[j] for j in deps[i]] or [0.0]) + (wake if q and deps[i] else 0.0)
         if q:
-            free[q] = s + o["cost"]
-        end[i] = s + o["cost"] + o.get("lat", 0.0)
+            s = max(s, free.get(q, 0.0))
+            free[q] = s + cost(o, fig)
+        end[i] = s + cost(o, fig) + late(o, fig)
+        o["start"] = s
+        order.append(i)
+        rdy.discard(i)
+        for k in succ[i]:
+            left[k] -= 1
+            if left[k] == 0:
+                rdy.add(k)
+    assert len(order) == n
+    return deps, order, max(end)
+
+
+def schedule(gr, offs, window, fig):
+    ops, deps, succ = gr
+    n = len(ops)
+    wake = fig["wake"]
+    cs = [cost(o, fig) for o in ops]
+    lt = [late(o, fig) for o in ops]
+    pri = [0.0] * n
+    for i in range(n - 1, -1, -1):
+        pri[i] = cs[i] + lt[i] + (wake if ops[i]["q"] else 0.0) + max([pri[k] for k in succ[i]] or [0.0])
+    pri = [window * (pri[i] + offs.get(ops[i]["name"], 0.0) + (offs.get("lead", 0.0) if ops[i]["s"] == 0 else 0.0)) for i in range(n)]
+    deps = [set(d) for d in deps]
+    left = [len(d) for d in deps]
+    end = [0.0] * n
+    free, bank, order, shut = {}, {}, [], set()
+    rdy = dict((i, 0.0) for i in range(n) if left[i] == 0)
+    while rdy:
+        best = {}
+        for i, s in rdy.items():
+            o = ops[i]
+            q = o["q"]
+            if q == "t" and o["first"] and o["banks"][0] in shut:
+                continue
+            f = free.get(q, 0.0)
+            if f > s:
+                s = f
+            for b in o["banks"]:
+                for e, j in bank.get(b, {}).items():
+                    if e != q and end[j] + wake > s:
+                        s = end[j] + wake
+            x = best.get(q)
+            if x is None:
+                best[q] = [s, s - pri[i], i, s]
+            else:
+                if s < x[0]:
+                    x[0] = s
+                if s - pri[i] < x[1]:
+                    x[1], x[2], x[3] = s - pri[i], i, s
+        q = min(best, key=lambda k: best[k][0])
+        i, s = best[q][2], best[q][3]
+        o = ops[i]
+        for b in o["banks"]:
+            for e, j in bank.get(b, {}).items():
+                if e != q:
+                    deps[i].add(j)
+            bank.setdefault(b, {})[q] = i
+        if q == "t":
+            if o["last"]:
+                shut.discard(o["banks"][0])
+            else:
+                shut.add(o["banks"][0])
+        if q:
+            free[q] = s + cs[i]
+        end[i] = s + cs[i] + lt[i]
         o["start"] = s
         order.append(i)
         del rdy[i]
         for k in succ[i]:
             left[k] -= 1
             if left[k] == 0:
-                rdy[k] = max(end[j] + (OWN if ops[j]["q"] == ops[k]["q"] else WAKE) for j in deps[k])
+                rdy[k] = max(end[j] for j in deps[k]) + (wake if ops[k]["q"] else 0.0)
     assert len(order) == n
     return deps, order, max(end)
 
 
-def plan(offs=None, bonus=None, window=None):
-    gr = graph()
+def events(gr, ph, fig):
+    ops, deps, succ = gr
+    n, w = len(ops), fig["wake"]
+    key = [0.0] * n
+    for i in range(n - 1, -1, -1):
+        o = ops[i]
+        if o["t"] < 0:
+            key[i] = -99.0 + i * 1e-3 if "sem" in o else ph.get(o["name"], min(min(key[k] for k in succ[i]) - 3.0, 5.0))
+        else:
+            key[i] = o["t"] * ph["period"] + (o["s"] or 0) * (ph["lag"] + ph.get("lag%d" % o["t"], 0.0)) + ph.get(o["name"], 12.0) if o["q"] else -99.0
+    left, end, order = [len(d) for d in deps], [0.0] * n, []
+    rdy, free, bank, shut = dict((q, {}) for q in "vatgs"), dict.fromkeys("vatgs", 0.0), {}, set()
+    deps = [set(d) for d in deps]
+
+    def done(i, st):
+        o = ops[i]
+        end[i] = st + cost(o, fig) + (-w if o["q"] == "t" and not o["last"] else late(o, fig))
+        order.append(i)
+        for k in succ[i]:
+            left[k] -= 1
+            if not left[k]:
+                m = max(end[j] for j in deps[k])
+                if ops[k]["q"]:
+                    rdy[ops[k]["q"]][k] = m + w
+                else:
+                    done(k, m)
+    for i in range(n):
+        if not deps[i]:
+            rdy[ops[i]["q"]][i] = 0.0
+    while len(order) < n:
+        best = None
+        for q in rdy:
+            es = []
+            for i, st in rdy[q].items():
+                if q == "t" and ops[i]["first"] and ops[i]["banks"][0] in shut:
+                    continue
+                es.append((max([st, free[q]] + [end[j] + w for b in ops[i]["banks"] for p, j in bank.get(b, {}).items() if p != q]), i))
+            if es:
+                m = min(es)[0]
+                if best is None or m < best[0]:
+                    best = (m, q) + min((key[i], st, i) for st, i in es if st <= m + ph["look"])[1:]
+        m, q, st, i = best
+        del rdy[q][i]
+        for b in ops[i]["banks"]:
+            deps[i].update(j for p, j in bank.get(b, {}).items() if p != q)
+            bank.setdefault(b, {})[q] = i
+        if q == "t":
+            if ops[i]["last"]:
+                shut.discard(ops[i]["banks"][0])
+            else:
+                shut.add(ops[i]["banks"][0])
+        free[q] = st + cost(ops[i], fig)
+        done(i, st)
+    return deps, order, max(end)
+
+
+def plan(opt=None, phase=None):
+    gr = graph(opt or OPT)
     ops = gr[0]
-    deps, order, span = schedule(gr, OFFS if offs is None else offs, BONUS if bonus is None else bonus, WINDOW if window is None else window)
+    deps, order, span = events(gr, phase or dict((x.split(":")[0], float(x.split(":")[1])) for x in PHASE.split()), FIG)
     count = {}
     for i in order:
         o = ops[i]
-        if o.get("sem", "").startswith(("in", "out")):
-            o["ev"] = (o["sem"], 16)
+        if "sem" in o:
+            o["ev"] = [(o["sem"], 16)]
         elif "arr" in o:
-            o["ev"] = (o["arr"], None)
+            o["ev"] = [(o["arr"], None)]
         elif "send" in o:
-            o["ev"] = None
+            o["ev"] = []
+        elif o["q"] is None:
+            o["ev"] = [e for j in deps[i] for e in ops[j]["ev"]]
         else:
             s = "q" + o["q"]
             count[s] = count.get(s, 0) + 1
-            o["ev"] = (s, count[s])
+            o["ev"] = [(s, count[s])]
     return ops, deps, order, count, span
+
+
+def send_aps(o, far, near):
+    t, s, k = o["send"]
+    a, b, w = {"L": (128 * s, 128 * s + 128, "L"), "Z": (192 * s, 192 * s + 64, "Z"), "N": (192 * s + 64, 192 * s + 192, "Z"),
+               "W": (192 * s, 192 * s + 192, "Z")}[k]
+    return [(far["%s%d" % (w, t + 1)][:, a:b], near["S%s%d" % (w, t)][:, a:b])]
 
 
 _PLAN = []
@@ -498,11 +792,8 @@ def rank_program(g, core, T, topo):
     ops, deps, order, count, _ = _PLAN[0]
     n = len(T.cores)
     nxt, prv = T.cores[(rank + 1) % n], T.cores[(rank - 1) % n]
-
-    def engines(a, b):
-        return topo.engines(a, b)
     mask = topo.mask(core, nxt)
-    n_in, n_out = len(engines(prv, core)), len(engines(core, nxt))
+    n_in, n_out = len(topo.engines(prv, core)), len(topo.engines(core, nxt))
     rid, pid = topo.addr(nxt)[:2]
     queues = {"v": g.vector, "a": g.scalar, "t": g.tensor, "g": g, "s": g.sync}
     seen = {}
@@ -514,23 +805,23 @@ def rank_program(g, core, T, topo):
         q = queues[o["q"]]
         need = {}
         for j in deps[i]:
-            ev = ops[j]["ev"]
-            if ev is not None:
-                need[ev[0]] = max(need.get(ev[0], 0), n_in if ev[1] is None else ev[1])
+            if o["q"] == "t" and ops[j]["q"] == "t" and not ops[j]["last"] and ops[j]["w"] == o["w"]:
+                continue
+            for s, v in ops[j]["ev"]:
+                need[s] = max(need.get(s, 0), n_in if v is None else v)
         for s in sorted(need):
             if seen.get((o["q"], s), 0) < need[s]:
                 q.wait_ge(T.sem[s], need[s])
                 seen[o["q"], s] = need[s]
         if "send" in o:
-            t, h, k = o["send"]
-            a, b, w = {"L": (128 * h, 128 * h + 128, "L"), "Z": (192 * h, 192 * h + 64, "Z"), "N": (192 * h + 64, 192 * h + 192, "Z")}[k]
-            g.remote_dma(T["%s%d" % (w, t + 1)][:, a:b], T["S%s%d" % (w, t)][:, a:b], T.sem["arr_%d_%d_%s" % (t + 1, h, k)], T.sem.loc, pid, rid, mask)
+            t, s, k = o["send"]
+            dst, src = send_aps(o, T, T)[0]
+            g.remote_dma(dst, src, T.sem["arr_%d_%d_%s" % (t + 1, s, k)], T.sem.loc, pid, rid, mask)
             sent += n_out
             continue
-        r = o["fn"](g, T)
-        r.then_inc(T.sem[o["ev"][0]], 16 if o["ev"][0].startswith(("in", "out")) else 1)
+        o["fn"](g, T).then_inc(T.sem[o["ev"][0][0]], 16 if "sem" in o else 1)
     for s in sorted(count):
         g.wait_ge(T.sem[s], count[s])
-    for k in range(8):
+    for k in range(NOUT):
         g.wait_ge(T.sem["out%d" % k], 16)
     g.wait_ge(T.sem.loc, sent)

@@ -1,34 +1,27 @@
-import numpy as np
 from concourse.mybir import AluOpType as OP, ActivationFunctionType as AF
 
 NT = 5
 NS = 2
-NPK = 64
-NB = 16 * NPK
-NPC = 2
-PCB = NB // NPC
-PCK = NPK // NPC
-ROUND32 = 1.5 * 2.0 ** 28
-
-OPT = {"h": "R2 R2", "o": "F1 F1 F1 F1", "c": "F1 F1 F1 F1", "cabs": "A", "ch": "a2 v2", "zexp": "v2 v2", "zlast": "g2 g2", "cmp": "s", "tmp": "v", "zbuf": "g", "yv": "v", "spoh": "v", "fin": "v", "tsplit": 16, "m": "v", "dup": (0, 0), "msg": 3, "cho": "v"}
+NB = 1024
 QB = NB // 4
 
-SCALED = {"nI": -1.0, "p8I": 8192.0, "n8I": -8192.0, "n4I": -4096.0, "p4I": 4096.0, "c2080": 2080.0, "c1184": 1184.0, "c32": 32.0,
-          "c32768": 32768.0, "c100": 100.0 / 128, "c200": 200.0 / 128, "cB": 61440.0, "hI": 0.5, "n3I": -3.0, "cG": 1.0 / 8192}
-MATS = ["n2", "ones", "bt", "I", "BM", "TRI", "TRIm", "TRIp", "BMs", "Sw", "hSw", "Wb0", "Wb1"] + sorted(SCALED)
-TILES = {"k2048": 2048.0, "kL2": 65536.0 - 8388608.0, "k155": -15.5, "kys": 155.0 / 128, "kn4": -4096.0}
-SCRATCH = {"MAT": ("sbuf", [128, 128 * len(MATS)], "bfloat16"), "KT": ("sbuf", [128, 64 * (len(TILES) + 1)], "bfloat16"),
-           "I32": ("sbuf", [128, 128], "float32"), "nI32": ("sbuf", [128, 128], "float32"), "SO2": ("sbuf", [128, 128], "float32"),
-           "KI": ("sbuf", [128, 128], "float16"), "ri": ("sbuf", [128, 4], "int32"), "rf": ("sbuf", [128, 4], "float32"),
-           "mi": ("sbuf", [128, 64], "int32"), "mj": ("sbuf", [128, 64], "int32"), "bi": ("sbuf", [128, 8], "float32"),
-           "base": ("sbuf", [128, 8], "bfloat16"), "zmask": ("sbuf", [128, PCB], "bfloat16"), "ks": ("sbuf", [128, 2 * NT], "float32"),
+OPT = {"h": "R2 R2", "o": "F1 F1 F1 F1", "c": "F1 F1 F1 F1", "ch": "a2 v2", "zexp": "v2 v2", "yv": "v", "off": "t"}
+
+SCALED = {"nI": -1.0, "p8I": 8192.0, "c2080": 2080.0, "c1184": 1184.0, "c32": 32.0, "c100": 100.0 / 128, "n100": -100.0 / 128,
+          "c200": 200.0 / 128, "hI": 0.5, "n3I": -3.0, "cG": 1.0 / 8192, "c63": 63.0}
+MATS = ["p2", "ones", "bt", "I", "BM", "TRI", "TRIm", "TRIo", "BMs", "Sw", "hSw", "Wb0", "Wb1", "nWb0", "nWb1"] + sorted(SCALED)
+TILES = {"k2048": 2048.0, "kL2": 65536.0 - 8388608.0, "k155": -15.5, "k325": 32.5, "r2": 1.5 * 2.0 ** 24, "r4096": 1.5 * 2.0 ** 35}
+ROUND32 = 1.5 * 2.0 ** 28
+SCRATCH = {"MAT": ("sbuf", [128, 128 * len(MATS)], "bfloat16"), "KT": ("sbuf", [128, 64 * len(TILES)], "bfloat16"),
+           "mk": ("sbuf", [128, 64], "bfloat16"), "nQ": ("sbuf", [128, 144], "bfloat16"), "KI": ("sbuf", [128, 128], "float16"),
+           "ri": ("sbuf", [128, 4], "int32"), "rf": ("sbuf", [128, 4], "float32"), "mi": ("sbuf", [128, 64], "int32"),
+           "mj": ("sbuf", [128, 64], "int32"), "bi": ("sbuf", [128, 8], "float32"), "base": ("sbuf", [128, 8], "bfloat16"),
+           "zmask": ("sbuf", [128, NB // 2], "bfloat16"), "ks": ("sbuf", [128, 1], "float32"), "kw": ("sbuf", [128, 128], "float32"),
            "SO": ("sbuf", [128, 512], "float32"), "iab": ("sbuf", [128, 256], "int32"), "abn": ("sbuf", [128, 256], "float16"),
            "zn": ("sbuf", [128, 128], "bfloat16"), "wn": ("sbuf", [128, 1], "bfloat16")}
-for _n in ("Q", "Q2", "nQ"):
-    SCRATCH[_n] = ("sbuf", [128, 144], "bfloat16")
-F32 = ("P", "dhs", "thr", "m", "tmp", "d", "accd", "q", "spoh", "P2")
-I32 = ("S", "ci", "ui", "u12", "S2", "fx", "pc", "so")
-B16 = ("set", "rec", "w", "am", "yv", "acc", "inc", "sp", "dm", "sc")
+F32 = ("P", "dhs", "thr", "m", "setH", "so", "pre", "P2", "lh", "lo")
+I32 = ("S", "ci", "S2", "fx")
+B16 = ("set", "w", "yv", "inc", "sp", "sc")
 SMALL = {}
 for _t in range(NT):
     SCRATCH["L%d" % _t] = ("sbuf", [128, 256], "uint16")
@@ -40,16 +33,10 @@ for _s in range(NS):
     SCRATCH["X%d" % _s] = ("sbuf", [128, 4096], "bfloat16")
     for _n in ("zbuf", "zexp", "hr", "ha", "od", "oa", "cd", "ca", "ch", "Mf"):
         SCRATCH["%s_%d" % (_n, _s)] = ("sbuf", [128, NB], "bfloat16")
-    if OPT["zexp"] == "":
-        SCRATCH["zexp_%d" % _s] = ("sbuf", [128, NPK, 16], "bfloat16")
-    SCRATCH["HO_%d" % _s] = ("sbuf", [128, 128], "float16")
-    for _n in ("t32", "fxc"):
-        SCRATCH["%s_%d" % (_n, _s)] = ("sbuf", [128, 64], "float16")
-    for _n in ("c16", "ch16"):
-        SCRATCH["%s_%d" % (_n, _s)] = ("sbuf", [128, 64], "uint16")
-    SCRATCH["u16_%d" % _s] = ("sbuf", [128, 8], "uint16")
-    SCRATCH["gx_%d" % _s] = ("sbuf", [128, 128], "float32")
-    SCRATCH["gs_%d" % _s] = ("sbuf", [128, 128], "int32")
+    for _n, _c, _d in (("chz", 192, "bfloat16"), ("rjz", 192, "bfloat16"), ("R", 192, "float32"), ("ad", 192, "float32"), ("HO", 128, "float16"),
+                       ("t32", 64, "float16"), ("c16", 64, "uint16"), ("ch16", 64, "uint16"), ("u16", 8, "uint16"), ("gx", 128, "float32"),
+                       ("gs", 128, "int32")):
+        SCRATCH["%s_%d" % (_n, _s)] = ("sbuf", [128, _c], _d)
     for _b, _l, _d in (("F", F32, "float32"), ("J", I32, "int32"), ("B", B16, "bfloat16")):
         for _i, _n in enumerate(_l):
             SMALL["%s_%d" % (_n, _s)] = ("%s_%d" % (_b, _s), 64 * _i)
@@ -57,25 +44,30 @@ for _s in range(NS):
 for _b in range(8):
     SCRATCH["ps%d" % _b] = ("psum", [128, 512], "float32")
 
-NIN, NOUT = 20, 16
+NIN, NOUT = 8, 16
 SEMAPHORES = ["qv", "qa", "qt", "qg", "loc"] + ["in%d" % _i for _i in range(NIN)] + ["out%d" % _i for _i in range(NOUT)] + \
-    ["arr_%d_%d_%s" % (_t, _s, _k) for _t in range(1, NT) for _s in range(NS) for _k in "LZNW"]
+    ["arr_%d_%d_%s" % (_t, _s, _k) for _t in range(1, NT) for _s in range(NS) for _k in "LZN"]
 
 PS = {}
 for _s in range(NS):
     for _b, _l in ((2, ("dh u", "do v", "pen r", "cnt off", "cntv", "ys", "Gs", "cnt2")),
-                   (4, ("dc", "V", "zd kp", "I2", "Mh", "Mh2", "H2 k0", "k1")),
-                   (6, ("Hp", "L L2", "OH", "CH", "cho", "d2", "tmpP O2", "spP"))):
+                   (4, ("dc", "V", "zd", "I2", "Mh", "Mh2", "k0", "k1")),
+                   (6, ("Hp", "L L2", "A", "", "", "spoh", "q", "wp"))):
         for _i, _n in enumerate(_l):
             for _m in _n.split():
                 PS[_m, _s] = (_b + _s, _i)
 
-FIG = {"cy": 1.0e-3, "pcy": 0.55e-3, "ga": 1.6, "sca": 4.0, "wake": 0.16, "hop": 5.5, "dma": 400.0, "issue": 0.3}
-PHASE = """S:-1 l0:-0.71 gh0:-0.49 zbuf:-0.32 zexp1:-0.17 zexp0:0.04 look:0.1 HO:0.17 Hp:0.22 P:0.25 OH:0.44 L:0.45 yh0:0.55 ci:0.65 yh1:0.83 gh1:1.01 c16:1.05 gc1:1.18 go0:1.28 ah0:1.33 gc0:1.34 yo0:1.97 ac0:2.13 ah1:2.18 dh:2.26 ao1:2.33 go2:2.36 ac1:2.38 dh2:2.51 set:2.59 ao0:2.61 ao2:2.61 pen:2.61 do:2.62 thr:2.63 go1:2.79 dc:3.52 m:3.52 w:3.79 rec:4.04 CH:4.21 am:4.21 tmp:4.26 cnt:4.31 d:4.44 cho0:4.49 cho:4.57 ch16:4.94 gch1:4.95 gch0:5.09 hsum:5.47 lag:6 M1:6.41 M0:6.61 yv:6.85 u:7.03 ui:7.04 V:7.23 acc:7.25 sp:7.46 u12:7.49 L2:7.63 P2:7.71 cnt2:7.74 pc:7.83 d2:7.93 S2:7.93 fx:8.16 accd:8.16 out1:8.32 pre:8.38 ad:8.38 cntv:8.55 lh:8.61 lo:8.62 zd:8.75 out2:8.75 O16:8.83 H16:8.83 out0:8.83 out3:8.83 out4:8.83 out6:8.83 out7:8.83 so:8.92 zz:8.98 out5:9.04 sendL:9.05 ys:9.15 sendZ:9.31 spoh:9.32 q:10.1 sendN:11.41 Gs:11.44 I2:11.67 out10:11.75 t32:11.87 dm:11.89 kp:11.9 KI:11.91 out11:11.93 out12:11.95 r:12 out13:12 out15:12 out8:12 out9:12 out14:12.27 sc:12.36 v:12.64 I2p:12.65 off:12.67 u16:12.85 G:12.87 gx:13.07 Mh:13.31 Mh2:13.31 gs:13.4 inc:13.47 scat:13.54 period:18.07
-a0:-1 b0:-1 z0:-2 z1:-1.5 wp:9 Wb:9.5 I:-200 set_ones:-201 Sw:-150 abn:-140"""
-PHASE = """a0:-12.24 b0:-12.24 z0:-8.07 zbuf:-7.35 HO:-7.29 gh0:-7.2 zexp1:-6.88 c16:-6.85 S:-6.61 Hp:-5.92 nQ:-5.7 z1:-5.56 ci:-5.48 ri1:-5.1 set_k155:-4.8 L2:-4.46 gc3:-4.39 yh1:-4.36 mi:-4.2 l0:-4.17 L:-4.15 hSw:-4.1 OH:-3.5 set:-3.49 gc1:-3.37 ah1:-3.31 set_n2f:-3.3 yh0:-3.16 P:-2.93 go2:-2.93 zexp0:-2.67 abn:-2.4 dh:-2.17 set_ones:-1.6 go3:-1.28 bi:-1.1 gh1:-0.93 go0:-0.89 ao3:-0.84 set_kys:-0.8 go1:-0.37 CH:-0.32 ah0:-0.31 ao2:-0.12 ac3:-0.12 cho:-0.1 look:0 ao1:0.08 lag3:0.1 gc0:0.11 lag4:0.15 ac0:0.25 ao0:0.26 do:0.28 ac1:0.29 gc2:0.33 ac2:0.36 dc:0.38 ri0:0.4 pen:0.51 I:0.8 lag1:0.83 m:0.91 rec:0.98 d:1.06 yo0:1.09 TRIp:1.2 lag0:1.28 am:1.33 cho0:1.47 gch1:1.49 cnt:1.52 ch16:1.6 set_zmask:1.6 V:1.62 yv:1.63 TRIm:1.9 M0:2.31 lag2:2.34 hI:2.4 tmp:2.46 thr:2.48 M1:2.51 base:2.6 w:2.64 wp:2.8 dh2:2.9 set_kL2:3.4 u:3.55 ui:3.57 Q:3.7 BMs:3.8 cG:4 c2080:4.3 set_zbuf_0:4.3 I32:4.3 c200:4.4 S2:4.43 out4:4.63 c100:4.7 Wb:4.9 hsum:5.32 set_Q:5.8 H16:6.48 u12:6.49 rf0:6.5 mj:6.5 set_k2048:6.5 P2:6.58 pre:6.71 rf2:6.8 sp:6.93 Sw:7 out0:7.07 c32:7.1 TRI:7.3 gch0:7.37 lag:7.48 inc:7.76 d2:7.79 n3I:7.8 bt:7.8 fx:8.03 ys:8.09 cntv:8.11 set_zbuf_1:8.4 out2:8.47 out10:8.63 out8:8.73 out14:8.79 so:8.83 out6:8.94 acc:9.01 q:9.07 accd:9.17 pc:9.18 spoh:9.18 lh:9.19 c32768:9.2 lo:9.29 t32:9.38 nI:9.5 BM:9.8 out3:10 r:10.25 out12:10.27 p8I:10.3 cB:10.4 zz:10.47 out5:10.47 rf1:10.5 sendL:10.74 O16:10.78 out7:10.98 c1184:11 mk:11.1 out11:11.28 ad:11.35 I2:11.67 v:11.91 out1:12.09 u16:12.14 Gs:12.3 cnt2:13.41 sendZ:13.47 off:14.15 gs:14.23 out13:14.71 kp:14.88 out9:15.33 sendN:15.66 KI:15.85 dm:15.94 I2p:16.19 out15:16.91 scat:17.36 Mh2:17.44 Mh:17.54 gx:17.75 zd:17.83 period:18.31 G:19.07 sc:21.92"""
-PHASE = """b0:-18.36 a0:-16.39 HO:-12.38 P:-12.37 zbuf:-11.2 z0:-10.53 z1:-9.56 l0:-9.41 S:-8.84 L:-7.8 zexp0:-7.55 go3:-7.39 ci:-7.29 zexp1:-7 Hp:-6.8 set_zbuf_1:-5.9 gh0:-5.76 ri0:-5.6 go1:-5.4 TRIm:-5.1 nQ:-4.8 c16:-4.74 mj:-4.5 n3I:-4.5 lag4:-4.15 yh1:-4.12 yh0:-3.8 c200:-3.8 mi:-3.5 set_zmask:-2.7 set_ones:-2.5 w:-2.21 Sw:-2.2 OH:-2.17 ah1:-1.8 ah0:-1.56 gc1:-1.53 dc:-1.49 go2:-1.48 gc3:-1.42 am:-1.29 gh1:-1.12 gc0:-1 base:-1 L2:-0.97 set:-0.96 go0:-0.95 yo0:-0.94 ao3:-0.94 cnt:-0.94 abn:-0.9 gch0:-0.86 set_kys:-0.8 ao2:-0.76 ao0:-0.71 set_n2f:-0.7 ao1:-0.61 ac1:-0.6 BMs:-0.6 ac3:-0.55 hSw:-0.4 dh2:-0.28 do:-0.28 dh:-0.27 CH:-0.22 ch16:-0.22 Q:-0.2 yv:-0.18 tmp:-0.07 cho0:-0.06 look:0 rec:0.07 gc2:0.34 Gs:0.38 cntv:0.48 gch1:0.54 cho:0.58 acc:0.88 ys:0.88 m:0.97 I:1 rf2:1.1 BM:1.1 M1:1.3 G:1.33 sp:1.43 set_zbuf_0:1.5 I32:1.9 lag0:1.91 lag3:2.27 bt:2.3 hI:2.4 ac0:2.42 pen:2.44 ac2:2.82 d2:3.03 lag1:3.16 thr:3.23 set_k155:3.3 TRIp:3.6 out4:3.61 S2:3.97 lag2:3.98 cG:4 ad:4.07 p8I:4.7 H16:5.59 u12:5.8 set_Q:5.8 set_k2048:5.9 out0:5.93 d:5.97 Wb:6.3 M0:6.45 rf0:6.5 c32:7.1 accd:7.23 TRI:7.3 fx:7.51 pc:7.66 set_kL2:7.7 pre:7.72 out5:7.74 c1184:8.1 out10:8.54 lag:8.58 out8:8.72 c100:8.9 out6:8.94 P2:8.99 u:9.03 so:9.13 c32768:9.2 ri1:9.3 hsum:9.4 nI:9.5 bi:9.6 c2080:9.7 out2:9.76 spoh:9.98 r:10.14 cB:10.4 dm:10.41 rf1:10.5 O16:10.51 cnt2:10.54 out7:10.55 q:10.61 out14:10.73 lo:10.78 ui:10.93 V:11 wp:11 mk:11.1 lh:11.12 out12:11.12 sendL:11.34 inc:11.56 out3:11.81 out11:11.82 out1:11.83 ri2:11.9 gs:12.93 u16:13.07 t32:13.47 sendZ:13.47 v:14.29 out13:14.58 out9:14.75 kp:15.63 KI:15.85 sendN:16.41 period:16.56 sc:16.88 zd:17.38 I2p:17.38 Mh2:17.44 gx:17.6 out15:17.64 scat:18.05 I2:19.02 off:19.91 zz:20.02 Mh:20.42"""
-PHASE = """HO:-18.85 l0:-18.37 OH:-17.42 b0:-16.71 z1:-16.48 Hp:-16.06 L:-16.01 a0:-15.57 z0:-14.45 ci:-10.65 c16:-10.6 zbuf:-9.63 gh0:-9.63 zexp1:-9.28 gc3:-7.91 gc2:-7.89 go1:-7.41 S:-7.21 lag4:-6.68 go3:-5.94 set_zbuf_1:-5.9 bt:-5.8 rf1:-5.7 CH:-5.6 TRIp:-5.5 TRI:-5.5 wp:-5.5 nQ:-4.8 set_k2048:-4.6 mj:-4.5 BMs:-4.4 Sw:-4.3 p8I:-4.3 P:-3.64 Wb:-3.6 ri0:-3 go2:-2.88 ao3:-2.72 set_ones:-2.5 Q:-2.2 dh:-1.91 c1184:-1.9 cG:-1.7 base:-1.4 gh1:-1.12 gc1:-1.09 abn:-1 ao2:-0.96 gc0:-0.87 lag0:-0.8 ao1:-0.76 ao0:-0.75 ah0:-0.7 gch0:-0.59 zexp0:-0.55 V:-0.45 ch16:-0.24 ah1:-0.14 ac1:-0.03 look:0 lag3:0.28 dc:0.31 c200:0.6 pen:0.79 hsum:0.88 mk:1 go0:1.1 BM:1.1 set:1.32 do:1.39 set_zbuf_0:1.5 L2:1.64 thr:1.86 set_Q:2 hSw:2.1 yh1:2.13 hI:2.4 c100:2.5 yh0:2.57 w:2.73 cnt:2.74 rec:2.76 thr2:2.8 gch1:3.05 am:3.16 n3I:3.4 ac3:4.01 cho:4.07 ac0:4.41 dhs:4.41 lag2:4.42 m:4.89 yv:5.36 ac2:5.55 out4:5.67 set_kL2:5.8 out0:5.83 TRIm:6 c32:6.1 ys:6.71 Gs:6.71 sp:6.72 cntv:6.76 t32:6.92 S2:6.95 dm:7.3 u:7.37 mi:7.7 ui:7.77 out5:7.86 tmp:7.91 cho0:7.92 cnt2:8.23 out6:8.48 out10:8.57 u12:8.6 fx:8.63 pc:8.64 so:8.65 spoh:8.75 P2:8.83 I:8.9 bi:9 kp:9.41 G:9.46 nI:9.5 out8:9.52 set_zmask:9.7 c2080:9.7 d:9.83 out2:9.97 pre:9.99 ri1:10.1 d2:10.15 cB:10.4 rf0:10.6 lag:10.95 M0:11.15 lag1:11.25 zd:11.3 rf2:11.4 out7:11.46 zz:11.68 set_k155:11.8 ri2:11.9 q:11.95 out11:12.11 M1:12.12 v:12.51 period:12.75 out1:12.86 accd:12.91 ad:12.92 KI:12.92 out12:12.94 out14:13.15 out3:13.92 sendZ:14.15 H16:14.24 out9:14.95 O16:15.24 Mh2:16.5 sendL:16.59 r:16.61 I2p:16.69 sendN:16.75 gs:17.04 off:17.22 out13:17.72 out15:18 lh:19.13 u16:19.53 acc:19.95 Mh:20.56 sc:20.68 I2:20.87 gx:21.06 lo:21.78 inc:21.83 scat:24.89"""
+FIG = {"cy": 0.97e-3, "pcy": 0.6e-3, "ga": 1.56, "sca": 3.8, "wake": 0.21, "hop": 5.5, "dma": 400.0, "issue": 0.3}
+PHASE = """a0:-24.74 z1:-23.45 zbuf:-21.64 z0:-21.52 zexp1:-20.96 L:-20.08 OH:-19.79 gch0:-14.32 sendL:-11.8 HO:-11.54 S2:-10.66
+ch16:-10.13 lag4:-9.93 M1:-8.59 M0:-8.58 fx:-8.48 u:-8.24 rej:-6.33 TRIm:-5.5 TRI:-5.3 H16:-5.01 l0:-5.01 base:-4.8 mi:-4.7 out7:-4.07
+nQ:-3.1 sendZ:-3.08 Sw:-3 zexp0:-1.75 go3:-1.73 S:-1.54 Hp:-1.31 spoh:-1.23 so:-1.13 go1:-1.1 P:-1.07 ao3:-1.06 gh1:-1.05 w:-0.91
+zd:-0.76 m:-0.69 look:0.1 ao0:0.37 out0:0.69 out1:0.79 out6:0.79 lag3:0.88 go2:0.9 ci:0.96 lag2:0.96 gh0:0.97 set:1.27 L2:1.31 pen:1.51
+ao1:1.59 ao2:1.59 do:1.6 out3:1.66 gc1:1.7 lag1:1.73 abn:2.1 c16:2.14 yh0:2.33 lag0:2.61 fill:2.8 ah1:2.84 ac2:2.95 gc0:3.13 ah0:3.66
+go0:3.92 C:3.97 gc3:3.98 dhs:4.16 dc:4.43 sendN:4.52 gc2:4.68 ac0:4.69 cnt:4.8 nam:4.81 ac1:4.83 HC:4.87 thr2:5.12 rec:5.69 out2:5.74
+thr:6.46 wp:6.6 lag:6.74 ac3:7.33 yh1:7.36 dh:7.68 mk:7.7 G:7.76 dm:8.49 V:8.5 setH:8.52 out4:8.53 Wb:8.6 I:8.7 hsum:9.18 yv:9.79
+cntv:9.8 ys:10.42 Gs:10.43 P2:10.72 sp:11.12 gch1:11.16 cho:11.41 d2:11.49 O16:11.84 pre:11.99 ad:12.22 q:12.25 lh:12.32 lo:12.4
+zz:12.45 t32:12.45 gs:12.84 KI:13.64 Mh:14.42 Mh2:14.43 I2:14.78 u16:15.54 gx:15.85 sc:15.98 off:17.87 inc:19.08 kp:19.52 cnt2:19.59
+scat:19.7 v:20.13 I2p:21.06 period:22.17 out5:22.52 r:22.78"""
 
 
 def build(opt):
@@ -96,18 +88,26 @@ def build(opt):
         return cols("MAT", i + a, i + b, key=name)
 
     def tile(name):
-        i = 64 * (sorted(TILES) + ["mk"]).index(name)
+        i = 64 * sorted(TILES).index(name)
         return cols("KT", i, i + 64, key=name)
 
     def pk(name, s, a=0, b=64):
         bank, i = PS[name, s]
         return ("ps%d:%d" % (bank, i), lambda T: T["ps%d" % bank][:, 64 * i + a:64 * i + b])
 
+    def two(name, other, s):
+        return ([pk(name, s)[0], pk(other, s)[0]], pk(name, s, 0, 128)[1])
+
     def sb(name, s):
         n = "%s_%d" % (name, s)
         if n in SMALL:
             return cols(SMALL[n][0], SMALL[n][1], SMALL[n][1] + 64, key=n)
         return full(n)
+
+    def slot(name, s, k=None):
+        n, a = ("ps%d" % PS["A", s][0], 64 * PS["A", s][1]) if name == "A" else ("%s_%d" % (name, s), 0)
+        key = lambda j: "%s:%s%d" % (n, name, j)
+        return cols(n, a, a + 192, key=[key(j) for j in range(3)]) if k is None else cols(n, a + k, a + 192, 3, key=key(k))
 
     def inps(x):
         return (x[0] if isinstance(x[0], str) else x[0][0]).startswith("ps")
@@ -147,41 +147,32 @@ def build(opt):
         add("a", fn, [a[0]], [out[0]] + ([accum[0]] if accum is not None else []), fx=0.065 if ga else 0.02, cy=0 if ga else max(64, n),
             ga=ga, name=name)
 
-    def mm(name, out, terms, first=True, last=True, after=()):
+    def mm(name, out, terms, first=True, last=True, after=(), n=64):
         def fn(g, T):
             r = None
             for k, x in enumerate(terms):
-                o = x[4] if len(x) > 4 else out
-                r = g.tensor.matmul(o[1](T), x[0][1](T), x[1][1](T), first and k == 0, last and k == len(terms) - 1)
+                r = g.tensor.matmul((x[2] if len(x) > 2 else out)[1](T), x[0][1](T), x[1][1](T), first and k == 0, last and k == len(terms) - 1)
             return r
-        tc = sum(max(64, x[3] if len(x) > 3 else 64) * (x[2] if len(x) > 2 else 1) for x in terms)
-        add("t", fn, [y[0] for x in terms for y in x[:2]] + list(after), [out[0]], tc=tc, name=name, first=first, last=last)
-
-    def f32(l, x):
-        return (full(l), x, 4)
+        add("t", fn, [y[0] for x in terms for y in x[:2]] + list(after), [out[0]], tc=n * len(terms), name=name, first=first, last=last)
 
     def window(s, lst):
         return (["X%d" % s, lst[0]], lambda T: T["X%d" % s][:, 0:4096].indirect(lst[1](T)))
 
     def memset(out, val, n, again=False):
-        add("v", lambda g, T: g.vector.memset(out[1](T), val), [out[0]] if again else [], [out[0]], cy=max(64, n), name="set_" + out[0])
+        add("v", lambda g, T: g.vector.memset(out[1](T), val), [out[0]] if again else [], [out[0]], cy=max(64, n), name="fill")
 
     nd = {"in": 0, "out": 0}
 
-    def dma(q, kind, out, src, lat):
-        def fn(g, T):
-            return {"s": g.sync, "a": g.scalar, "g": g}[q].dma_start(out[1](T), src[1](T))
-        add(q, fn, [src[0]], [out[0]], fx=0.1, sem="%s%d" % (kind, nd[kind]), lat=lat, name=kind + str(nd[kind]))
+    def dma(q, kind, out, src, kb):
+        add(q, lambda g, T: (g.sync if q == "s" else g.scalar).dma_start(out[1](T), src[1](T)), [src[0]], [out[0]], fx=0.1,
+            sem="%s%d" % (kind, nd[kind]), lat=kb, name=kind + str(nd[kind] % 8))
         nd[kind] += 1
 
     def piece(name, s, p):
-        if name == "zexp" and opt["zexp"] == "":
-            return (["%s_%d.%d" % (name, s, k) for k in range(*p)], lambda T: T["zexp_%d" % s][:, 16 * p[0]:16 * p[1], :])
         return cols("%s_%d" % (name, s), p[0] * QB, p[1] * QB, key=["%s_%d.%d" % (name, s, k) for k in range(*p)])
 
     def col16(name, s, j):
-        n = "%s_%d" % (name, s)
-        return (["%s.%d" % (n, p) for p in range(4)], lambda T: T[n][:, j:NB:16])
+        return cols("%s_%d" % (name, s), j, NB, 16, key=["%s_%d.%d" % (name, s, p) for p in range(4)])
 
     def cuts(text):
         out, a = [], 0
@@ -193,26 +184,21 @@ def build(opt):
     def part(name, c, a, b, key):
         return (key, lambda T: T[name][64 * c:64 * c + 64, a:b])
 
+    def rows(x, s):
+        return (x[0], lambda T: x[1](T)[64 * s:64 * s + 64, :])
+
     dma("s", "in", cols("iab", 0, 128, key="ia"), (None, lambda T: T.ba[:]), 100)
     dma("a", "in", cols("iab", 128, 256, key="ib"), (None, lambda T: T.bb[:]), 200)
     dma("s", "in", full("zn"), (None, lambda T: T.zp[:]), 270)
-    xin = [[], []]
-    kb = 270
     for s in range(NS):
-        for c in range(0 if opt["dup"][s] else 2):
-            kb += 512
-            xin[s].append("Xin%d.%d" % (s, c))
-            dma("as"[c], "in", part("X%d" % s, c, 0, 4096, xin[s][-1]), part("xt", s, 0, 4096, None), kb + 512 * (1 - c))
-        for k in range(4 if opt["dup"][s] else 0):
-            for c in ([s] if k < opt["dup"][s] else [s, 1 - s]):
-                kb += 128
-                xin[s].append("Xin%d.%d.%d" % (s, k, c))
-                dma("a" if len(xin[0] + xin[1]) in (1, 3) else "s", "in", part("X%d" % s, c, 1024 * k, 1024 * k + 1024, xin[s][-1]),
-                    part("xt", s, 1024 * k, 1024 * k + 1024, None), kb)
+        for c in range(2):
+            dma("as"[c], "in", part("X%d" % s, c, 0, 4096, "Xin%d.%d" % (s, c)), part("xt", s, 0, 4096, None), 1300 + 1024 * s)
         if s == 0:
-            dma("s", "in", full("wn"), (None, lambda T: T.wl[:]), kb + 30)
+            dma("s", "in", full("wn"), (None, lambda T: T.wl[:]), 1330)
+
     def gp(fn, r, w, n):
         add("g", fn, r, w, fx=0.17, cy=2 * n, name=w[0])
+    I, nI = mat("I"), mat("nI")
     memset(mat("ones"), 1.0, 64)
     sel = lambda o, i, pat, cmp, b, ch: gp(lambda g, T: g.affine_select(mat(o)[1](T), mat(i)[1](T), pat, cmp, 0.0, b, ch), [i], [o], 128)
     sel("I", "ones", [[-1, 128]], OP.is_equal, 0, 1)
@@ -224,63 +210,47 @@ def build(opt):
     gp(lambda g, T: g.iota(T.bi[:], [[2048, 2], [512, 4]], 0, 0, allow_small_or_imprecise_dtypes=True), [], ["bi"], 8)
     for s in range(NS):
         memset(full("zbuf_%d" % s), 0.0, NB // 2)
-    memset(full("zmask"), 1.0, PCB // 2)
-    memset(cols("zmask", 0, PCB, 16), 0.0, 64, again=True)
+        memset(slot("chz", s), 0.0, 96)
+        memset(slot("rjz", s), 0.0, 96)
+    memset(full("zmask"), 1.0, NB // 4)
+    memset(cols("zmask", 0, NB // 2, 16), 0.0, 64, again=True)
     for n in sorted(TILES):
         memset(tile(n), TILES[n], 64)
     for n in sorted(SCALED):
-        ts(n, mat(n), mat("I"), SCALED[n], OP.mult)
-    memset(full("Q"), 0.0, 72)
+        ts("scaled", mat(n), I, SCALED[n], OP.mult)
+    memset(full("nQ"), 0.0, 72)
     i0 = 128 * MATS.index("BM")
-    cp("Q", cols("Q", 15, 143, 16), cols("MAT", i0, i0 + 128, 16, key="BM"))
-    ops[-1]["r"].append("Q")
-    ts("Q2", full("Q2"), full("Q"), -2.0, OP.mult, n=72)
-    ts("nQ", full("nQ"), full("Q"), -1.0, OP.mult, n=72)
-    for n, v in (("TRIm", -16.0), ("TRIp", 16.0)):
-        ts(n, mat(n), mat("I"), v, OP.mult)
-        tt(n, mat(n), mat(n), mat("TRI"), OP.add, n=128)
-    ts("BMs", mat("BMs"), mat("BM"), (1.0 if opt["yv"] == "a" else 2.0) / 128, OP.mult)
+    ts("nQ", cols("nQ", 15, 143, 16), cols("MAT", i0, i0 + 128, 16, key="BM"), -1.0, OP.mult)
+    ts("scaled", mat("TRIm"), I, -16.0, OP.mult)
+    tt("TRIm", mat("TRIm"), mat("TRIm"), mat("TRI"), OP.add, n=128)
+    ts("scaled", mat("BMs"), mat("BM"), (1.0 if opt["yv"] == "a" else 2.0) / 128, OP.mult)
+    ts("scaled", mat("TRIo"), mat("TRI"), -31.0 / 32, OP.mult)
     cp("Sw", mat("Sw", 0, 64), mat("I", 64, 128))
     cp("Sw", mat("Sw", 64, 128), mat("I", 0, 64))
-    ts("hSw", mat("hSw"), mat("Sw"), 0.5, OP.mult)
-    act("I32", full("I32"), mat("I"), AF.Copy, n=128)
-    act("nI32", full("nI32"), mat("I"), AF.Copy, scale=-1.0, n=128)
-    memset(mat("n2"), -2.0, 64)
-
-    def rows(x, s):
-        return (x[0], lambda T: x[1](T)[64 * s:64 * s + 64, :])
+    ts("scaled", mat("hSw"), mat("Sw"), 0.5, OP.mult)
+    memset(mat("p2"), 2.0, 64)
+    for s in range(NS):
+        wp = pk("wp", 1, s, s + 1)
+        mm("wp", wp, [(rows(mat(n), s), rows(full("wn"), s)) for n in ("I", "Sw")])
+        ts("Wb", mat("Wb%d" % s), mat("BM"), wp, OP.mult)
+        ts("Wb", mat("nWb%d" % s), mat("Wb%d" % s), -1.0, OP.mult)
+    ts("abn", full("abn"), (["ia", "ib"], lambda T: T.iab[:]), -2048.0, OP.add, n=256)
+    ts("mk", full("mj"), full("mi"), 15, OP.bitwise_and)
+    ts("mk", full("mk"), full("mj"), 0.0, OP.not_equal, -64.0, OP.mult)
+    ri = lambda k: cols("ri", k, k + 1, key="ri%d" % k)
+    ts("base", ri(1), ri(0), 15, OP.bitwise_and)
+    ts("base", ri(2), ri(0), 64, OP.bitwise_and)
+    tt("base", cols("rf", 0, 1, key="rf0"), ri(1), ri(2), OP.add, n=1)
+    tt("base", cols("rf", 1, 2, key="rf1"), ri(1), ri(2), OP.subtract, n=1)
+    ts("base", cols("rf", 2, 4, key="rf2"), (["rf0", "rf1"], lambda T: T.rf[:, 0:2]), 32.0, OP.mult)
+    for c in range(2):
+        ts("base", cols("base", 4 * c, 4 * c + 4), cols("bi", 4 * c, 4 * c + 4), cols("rf", 2 + c, 3 + c, key="rf2"), OP.add)
 
     def spread(s, src, a):
         return [(rows(mat("I" if c == s else "Sw"), s), rows(cols(src, a + 64 * c, a + 64 * c + 64), s)) for c in range(2)]
-    for s in range(NS):
-        wp = pk("spP", 1, s, s + 1)
-        mm("wp", wp, [(rows(mat(n), s), rows(full("wn"), s)) for n in ("I", "Sw")])
-        ts("Wb", mat("Wb%d" % s), mat("BM"), wp, OP.mult)
-    ts("abn", full("abn"), (["ia", "ib"], lambda T: T.iab[:]), -2048.0, OP.add, n=256)
-    nb = 0
-    for s in range(NS):
-        for k in range(2 * opt["dup"][s]):
-            b = ((0, 1, 3, 5) if s == 0 else (0, 1))[nb % (4 - 2 * s)]
-            nb += 1
-            bank = (["ps%d:y" % b] if b < 2 else ["ps%d:%d" % (b, i) for i in range(8)], lambda T, b=b, s=s: T["ps%d" % b][64 - 64 * s:128 - 64 * s, :])
-            src = part("X%d" % s, s, 512 * k, 512 * k + 512, "Xin%d.%d.%d" % (s, k // 2, s))
-            mm("dup", bank, [(rows(mat("I", 64 * s, 64 * s + 64), s), src, 1, 512)])
-            xin[s].append("Xd%d.%d" % (s, k))
-            dst = part("X%d" % s, 1 - s, 512 * k, 512 * k + 512, xin[s][-1])
-            if k % 2:
-                act("dupa", dst, bank, AF.Copy, n=512)
-            else:
-                cp("dupv", dst, bank, n=512)
-    ts("mj", full("mj"), full("mi"), 15, OP.bitwise_and)
-    ts("mk", tile("mk"), full("mj"), 0.0, OP.not_equal, -64.0, OP.mult)
-    ts("ri1", cols("ri", 1, 2, key="ri1"), cols("ri", 0, 1, key="ri0"), 15, OP.bitwise_and)
-    ts("ri2", cols("ri", 2, 3, key="ri2"), cols("ri", 0, 1, key="ri0"), 64, OP.bitwise_and)
-    tt("rf0", cols("rf", 0, 1, key="rf0"), cols("ri", 1, 2, key="ri1"), cols("ri", 2, 3, key="ri2"), OP.add, n=1)
-    tt("rf1", cols("rf", 1, 2, key="rf1"), cols("ri", 1, 2, key="ri1"), cols("ri", 2, 3, key="ri2"), OP.subtract, n=1)
-    ts("rf2", cols("rf", 2, 4, key="rf2"), (["rf0", "rf1"], lambda T: T.rf[:, 0:2]), 32.0, OP.mult)
-    for c in range(2):
-        ts("base", cols("base", 4 * c, 4 * c + 4), cols("bi", 4 * c, 4 * c + 4), cols("rf", 2 + c, 3 + c, key="rf2"), OP.add)
-    I, nI = mat("I"), mat("nI")
+
+    def whole(k):
+        return [(I, tile(k)), (nI, tile(k))]
 
     for t in range(NT):
         last, splice = t == NT - 1, t >= 2
@@ -294,52 +264,33 @@ def build(opt):
             Gold = cols("Z%d" % t, 192 * s + 128, 192 * s + 192, key=ik)
             lists = cols("L%d" % t, 128 * s, 128 * s + 128, key=lk)
             if t > 0:
-                for k, key in (("L", lk), ("Z", zk), ("N", ik)) if opt["msg"] == 3 else (("L", lk), ("W", [zk, ik])):
+                for k, key in (("L", lk), ("Z", zk), ("N", ik)):
                     add(None, None, ["send_%d_%d_%s" % (t - 1, s, k)], [key], arr="arr_%d_%d_%s" % (t, s, k), name="arr" + k)
                 ts("HO", sb("HO", s), lists, -2048.0, OP.add)
             else:
                 mm("a0", pk("Mh", s), spread(s, "abn", 0))
-                mm("b0", pk("Mh2", s), spread(s, "abn", 128))
+                mm("a0", pk("Mh2", s), spread(s, "abn", 128))
                 mm("z0", pk("zd", s), spread(s, "zn", 0))
-                ab = ([pk("Mh", s)[0], pk("Mh2", s)[0]], pk("Mh", s, 0, 128)[1])
-                ts("l0", lists, ab, 2048.0, OP.add, n=128)
-                cp("HO", sb("HO", s), ab, n=128)
+                ts("l0", lists, two("Mh", "Mh2", s), 2048.0, OP.add, n=128)
+                cp("HO", sb("HO", s), two("Mh", "Mh2", s), n=128)
                 act("z1", z, pk("zd", s), AF.Copy)
-                add(None, None, xin[s], [X], name="X0")
+                add(None, None, ["Xin%d.0" % s, "Xin%d.1" % s], [X], name="X0")
             zb = cols("zbuf_%d" % s, 0, NB, 16)
-            if opt["zexp"] == "":
-                zx = "zexp_%d" % s
-                zq = ["%s.%d" % (zx, k) for k in range(4)]
-                for j in range(2):
-                    add("g", lambda g, T, zx=zx, z=z, j=j: g.affine_select(T[zx][:, :, j], z[1](T), [[0, 64]], OP.is_equal, 0.0, 0, 0),
-                        [zk], zq, fx=0.17, cy=128, name="zx%d" % j)
-                for j in (2, 4):
-                    add("g", lambda g, T, zx=zx, j=j: g.affine_select(T[zx][:, :, j:2 * j], T[zx][:, :, 0:j], [[0, 64], [0, j]], OP.is_equal, 0.0, 0, 0),
-                        zq, zq, fx=0.17, cy=128 * j, name="zx%d" % j)
-                for k, (e, p, n) in enumerate(cuts(opt["zlast"])):
-                    a, b = 16 * p[0], 16 * p[1]
-                    if e == "g":
-                        add("g", lambda g, T, zx=zx, a=a, b=b: g.affine_select(T[zx][:, a:b, 8:16], T[zx][:, a:b, 0:8], [[0, b - a], [0, 8]], OP.is_equal, 0.0, 0, 0),
-                            zq[p[0]:p[1]], zq[p[0]:p[1]], fx=0.17, cy=n, name="zy%d" % k)
-                    else:
-                        cp("zy%d" % k, (zq[p[0]:p[1]], lambda T, zx=zx, a=a, b=b: T[zx][:, a:b, 8:16]), (zq[p[0]:p[1]], lambda T, zx=zx, a=a, b=b: T[zx][:, a:b, 0:8]), n=n // 4)
-            elif opt["zbuf"] == "g":
-                add("g", lambda g, T, zb=zb, z=z: g.affine_select(zb[1](T), z[1](T), [[0, 64]], OP.is_equal, 0.0, 0, 0), [zk, zb[0]], [zb[0]],
-                    fx=0.17, cy=128, name="zbuf")
-            else:
-                act("zbuf", zb, z, AF.Copy)
-                ops[-1]["r"].append(zb[0])
+            add("g", lambda g, T, zb=zb, z=z: g.affine_select(zb[1](T), z[1](T), [[0, 64]], OP.is_equal, 0.0, 0, 0), [zk, zb[0]], [zb[0]],
+                fx=0.17, cy=128, name="zbuf")
             for k, (e, p, n) in enumerate(cuts(opt["zexp"])):
                 scan("zexp%d" % k, piece("zexp", s, p), cols("zmask", 0, n), cols("zbuf_%d" % s, p[0] * QB, p[1] * QB), OP.add, n // 2)
-            mm("Hp", pk("Hp", s), [(I, Hc), (I, tile("k2048"))])
+            Hp, OH, HC = pk("Hp", s), slot("A", s, 0), slot("A", s, 1)
+            mm("Hp", Hp, [(I, Hc), (I, tile("k2048"))])
             mm("L", pk("L", s), [(mat("c2080"), Hc), (mat("c1184"), Oc)])
-            mm("OH", pk("OH", s), [(I, Oc), (nI, Hc)])
-            tt("P", sb("P", s), Oc, pk("Hp", s), OP.mult)
+            mm("OH", OH, [(I, Oc), (nI, Hc)])
+            tt("P", sb("P", s), Oc, Hp, OP.mult)
             tt("S", sb("S", s), sb("P", s), pk("L", s), OP.add)
             ts("ci", sb("ci", s), sb("S", s), 5, OP.arith_shift_right, 4095, OP.bitwise_and)
             cp("c16", sb("c16", s), sb("ci", s))
-            ts("set", sb("set", s), pk("OH", s), 0.0, OP.is_equal)
-            tt("CH", pk("CH", s), sb("ci", s), pk("Hp", s), OP.subtract)
+            ts("set", sb("set", s), OH, 0.0, OP.is_equal)
+            tt("HC", HC, Hp, sb("ci", s), OP.subtract)
+            cp("C", slot("A", s, 2), sb("ci", s))
 
             def lst(name, a, p, key=None):
                 return cols(name, a + p[0] * 16, a + p[1] * 16, key=key)
@@ -351,76 +302,33 @@ def build(opt):
                     w, o, ze = window(s, l(p)), piece(raw, s, p), piece("zexp", s, p)
                     if e == "R":
                         act("g%s%d" % (nm, k), o, w, AF.Copy, ga=n)
-                        yb = ("ps%d:y" % (ny % 2), lambda T, b=ny % 2, n=n: T["ps%d" % b][:, 0:n])
+                        yb = cols("ps%d" % (ny % 2), 0, n, key="ps%d:y" % (ny % 2))
                         ny += 1
-                        mm("y%s%d" % (nm, k), yb, [(I, o, 1, n), (nI, ze, 1, n)])
+                        mm("y%s%d" % (nm, k), yb, [(I, o), (nI, ze)], n=n)
                         act("a%s%d" % (nm, k), piece(ab, s, p), yb, AF.Abs, n=n)
                     else:
                         add("v", lambda g, T, o=o, w=w, ze=ze: g.vector.tensor_tensor(o[1](T), w[1](T), ze[1](T), OP.subtract),
                             [w[0], ze[0]], [o[0]], fx=0.05, ga=n, name="g%s%d" % (nm, k))
-                        if nm == "c" and opt["cabs"] == "R":
-                            ts("a%s%d" % (nm, k), piece(ab, s, p), o, 0.0, OP.max, n=n // 2)
-                        else:
-                            act("a%s%d" % (nm, k), piece(ab, s, p), o, AF.Abs, n=n)
-            qs = lambda q, name: [((q, lambda T, j=j: T[q][:, 15 - j:143 - j]), col16(name, s, j)) for j in range(16)]
-
-            def long(name, out, terms, first=True, last=True, after=()):
-                k = opt["tsplit"]
-                for a in range(0, 16, k):
-                    mm(name if a + k == 16 else "%s_%d" % (name, a), out, terms[a:a + k], first and a == 0, last and a + k == 16, after)
-            df = opt["cmp"] == "d"
-            if df:
-                long("dh", pk("do", s), qs("Q", "ha"), last=False)
-                long("dh2", pk("dc", s), qs("Q", "ha"), last=False)
-                mm("pen", pk("do", s), [(mat("p8I"), sb("set", s))], first=False, last=False)
-            else:
-                long("dh", pk("dh", s), qs("nQ", "ha"))
-                act("dhs", sb("dhs", s), pk("dh", s), AF.Copy)
-                mm("pen", pk("do", s), [(mat("p8I"), sb("set", s))], last=False)
-            long("do", pk("do", s), qs("nQ", "oa"), first=False)
-            if opt["cabs"] == "R":
-                long("dc0", pk("dc", s), qs("Q", "cd"), first=not df, last=False)
-                long("dc", pk("dc", s), qs("Q2", "ca"), first=False)
-            else:
-                long("dc", pk("dc", s), qs("nQ", "ca"), first=not df)
-            if not df:
-                tt("thr", pk("pen", s) if t else sb("thr", s), pk("do", s), sb("dhs", s), OP.max)
-                if t:
-                    tt("thr2", sb("thr", s), pk("pen", s), Gold, OP.add)
-            elif t:
-                tt("thr", sb("thr", s), pk("do", s), Gold, OP.max)
-            else:
-                ts("thr", sb("thr", s), pk("do", s), 0.0, OP.max)
+                        act("a%s%d" % (nm, k), piece(ab, s, p), o, AF.Abs, n=n)
+            qs = lambda name: [(cols("nQ", 15 - j, 143 - j), col16(name, s, j)) for j in range(16)]
+            mm("dh", pk("dh", s), qs("ha"))
+            act("dhs", sb("dhs", s), pk("dh", s), AF.Copy)
+            mm("pen", pk("do", s), [(mat("p8I"), sb("set", s))], last=False)
+            mm("do", pk("do", s), qs("oa"), first=False)
+            mm("dc", pk("dc", s), qs("ca"))
+            tt("thr", pk("pen", s) if t else sb("thr", s), pk("do", s), sb("dhs", s), OP.max)
+            if t:
+                tt("thr2", sb("thr", s), pk("pen", s), Gold, OP.add)
             tt("w", sb("w", s), pk("dc", s), sb("thr", s), OP.is_gt)
             mm("cnt", pk("cnt", s), [(mat("TRIm"), sb("w", s))])
-            if not df:
-                tt("m", sb("m", s), pk("dc", s), sb("dhs", s), OP.max)
-            elif opt["m"] == "a":
-                act("m", sb("m", s), pk("dc", s), AF.Relu)
-            else:
-                ts("m", sb("m", s), pk("dc", s), 0.0, OP.max)
-            tt("rec", sb("rec", s), pk("do", s), sb("m", s), OP.is_ge)
-            if opt["tmp"] == "a":
-                mm("tmpP", pk("tmpP", s), [(I, Oc), (nI, Hc), (mat("p8I"), sb("rec", s))])
-                act("tmp", sb("tmp", s), pk("tmpP", s), AF.Relu, bias=-4096.0)
-                mm("cho0", pk("cho", s), [(I, Hc), (mat("n4I"), sb("rec", s)), f32("I32", sb("tmp", s))], last=False)
-            elif opt["cho"] == "t":
-                tt("tmp", sb("tmp", s), sb("rec", s), pk("OH", s), OP.mult)
-                mm("cho0", pk("cho", s), [(I, Hc), f32("I32", sb("tmp", s))], last=False)
-            ts("am", sb("am", s), pk("cnt", s), -13.0, OP.is_lt)
-            if opt["cho"] == "t":
-                tt("d", sb("d", s), sb("am", s), pk("CH", s), OP.mult)
-                mm("cho", pk("cho", s), [f32("I32", sb("d", s))], first=False)
-                ts("ch16", sb("ch16", s), pk("cho", s), 2048.0, OP.add)
-                tt("d2", pk("d2", s), pk("cho", s), Hc, OP.subtract)
-            else:
-                tt("tmp", sb("tmp", s), sb("rec", s), pk("OH", s), OP.mult)
-                tt("cho0", pk("cho", s), sb("tmp", s), pk("Hp", s), OP.add)
-                tt("d", sb("d", s), sb("am", s), pk("CH", s), OP.mult)
-                tt("cho", sb("m", s), sb("d", s), pk("cho", s), OP.add)
-                cp("ch16", sb("ch16", s), sb("m", s))
-                tt("d2", pk("d2", s), sb("m", s), pk("Hp", s), OP.subtract)
-            long("hsum", pk("V", s), [(nI, col16("hr", s, j)) for j in range(16)], last=False, after=["ch16_%d" % s])
+            rec, nam, rej = slot("chz", s, 1), slot("chz", s, 2), slot("rjz", s, 2)
+            tt("m", sb("m", s), pk("dc", s), sb("dhs", s), OP.max)
+            tt("rec", rec, pk("do", s), sb("m", s), OP.is_ge)
+            ts("nam", nam, pk("cnt", s), -13.0, OP.is_ge)
+            scan("cho", slot("R", s), slot("chz", s), slot("A", s), OP.add, 192)
+            cp("ch16", sb("ch16", s), slot("R", s, 2))
+            tt("d2", slot("R", s, 1), Hp, slot("R", s, 2), OP.subtract)
+            mm("hsum", pk("V", s), [(nI, col16("hr", s, j)) for j in range(16)], last=False, after=["ch16_%d" % s])
             for k, (e, p, n) in enumerate(cuts(opt["ch"])):
                 w, o = window(s, lst("ch16_%d" % s, 0, p)), piece("ch", s, p)
                 if e == "a":
@@ -428,13 +336,11 @@ def build(opt):
                 else:
                     add("v", lambda g, T, o=o, w=w: g.vector.tensor_copy(o[1](T), w[1](T)), [w[0]], [o[0]], fx=0.05, ga=n, name="gch%d" % k)
                 scan("M%d" % k, piece("Mf", s, p), cols("zmask", 0, n), o, OP.max, n // 2)
-            long("V", pk("V", s), [(I, col16("ch", s, j)) for j in range(16)], first=False)
-            M = (["Mf_%d.%d" % (s, p) for p in range(4)], lambda T, s=s: T["Mf_%d" % s][:, 15:NB:16])
-            Wb = mat("Wb%d" % s)
-            mm("u", pk("u", s), [(Wb, M), (mat("cB"), sb("set", s))])
-            ts("ui", sb("ui", s), pk("u", s), -61440.0, OP.add, 0.0, OP.max)
-            ts("u12", sb("u12", s), sb("ui", s), 4095, OP.bitwise_and)
-            tt("P2", sb("P2", s), sb("u12", s), pk("Hp", s), OP.mult)
+            mm("V", pk("V", s), [(I, col16("ch", s, j)) for j in range(16)], first=False)
+            M, Wb = col16("Mf", s, 15), mat("Wb%d" % s)
+            tt("setH", sb("setH", s), sb("set", s), Hp, OP.mult)
+            mm("u", pk("u", s), [(mat("c63"), tile("k325")), (mat("nWb%d" % s), M)] + whole("r4096") + [(Wb, M)])
+            tt("P2", sb("P2", s), sb("setH", s), pk("u", s), OP.mult)
             mm("L2", pk("L2", s), [(mat("c32"), Oc), (I, tile("kL2"))] + ([(full("KI"), sb("set", s))] if t else []))
             tt("S2", sb("S2", s), sb("P2", s), pk("L2", s), OP.add)
             ts("fx", sb("fx", s), sb("S2", s), 5, OP.arith_shift_right, 4095, OP.bitwise_and)
@@ -442,116 +348,85 @@ def build(opt):
             if not last:
                 mm("zd", pk("zd", s), [(I, z), (nI, M)])
                 act("zz", cols(sz, 192 * s, 192 * s + 64, key=sh + "_zz"), pk("zd", s), AF.Abs)
-                if opt["msg"] == 3:
-                    add("g", None, [sh + "_zz"], [sh + "_Z"], fx=0.3, send=(t, s, "Z"), name="sendZ")
+                add("g", None, [sh + "_zz"], [sh + "_Z"], send=(t, s, "Z"), name="sendZ")
                 mm("v", pk("v", s), [(Wb, M), (I, tile("k155"))])
                 ts("t32", sb("t32", s), pk("v", s), ROUND32, OP.add, -ROUND32, OP.add)
-                mm("r", pk("r", s), [(Wb, M), (nI, sb("t32", s)), (I, tile("mk"))])
+                mm("r", pk("r", s), [(Wb, M), (nI, sb("t32", s)), (I, full("mk"))])
                 scan("sc", sb("sc", s), cols("zmask", 0, 64), pk("r", s), OP.max, 64)
                 b, c0 = SMALL["sc_%d" % s]
                 pick = cols(b, c0 + 15, c0 + 64, 16, key="sc_%d" % s)
-                mm("off", pk("off", s, 0, 8), [(I, full("base")), (I, pick, 1, 4, pk("off", s, 0, 4)), (mat("Sw"), pick, 1, 4, pk("off", s, 4, 8))])
+                mm("off", pk("off", s, 0, 8), [(I, full("base")), (I, pick, pk("off", s, 0, 4)), (mat("Sw"), pick, pk("off", s, 4, 8))])
                 cp("u16", sb("u16", s), pk("off", s, 0, 8))
                 mm("Mh", pk("Mh", s), [(mat("hI"), M)])
                 mm("Mh2", pk("Mh2", s), [(mat("hSw"), M)])
                 w = window(s, sb("u16", s))
                 act("gx", sb("gx", s), w, AF.Copy, scale=0.5, bias=-0.25, ga=128)
-                tt("gs", sb("gs", s), sb("gx", s), ([pk("Mh", s)[0], pk("Mh2", s)[0]], pk("Mh", s, 0, 128)[1]), OP.add, n=128)
+                tt("gs", sb("gs", s), sb("gx", s), two("Mh", "Mh2", s), OP.add, n=128)
                 add("v", lambda g, T, w=w, s=s: g.vector.tensor_copy(w[1](T), T["gs_%d" % s][:]), [w[0], "gs_%d" % s], [X], fx=0.05, sca=128, name="scat")
             yv, votes = sb("yv", s), (mat("BMs"), sb("yv", s))
             if opt["yv"] == "a":
                 act("yv", yv, pk("V", s), AF.Sign, bias=0.5)
             else:
-                ts("yv", yv, pk("V", s), 0.0, OP.is_ge, 0.5, OP.subtract)
+                ts("yv", yv, pk("V", s), 0.0, OP.is_ge)
+            y0 = 0.0 if opt["yv"] == "a" else 16.0
+            y1, i0 = (1 + y0) / 128, (255 - y0) / 128
             mm("cntv", pk("cntv", s), [votes])
-            ts("acc", sb("acc", s), pk("cntv", s), 1.0 / 128, OP.is_ge)
-            tt("accd", sb("accd", s), sb("acc", s), pk("d2", s), OP.mult)
-            mm("ys", pk("ys", s), [(mat("c100"), sb("rec", s)), (mat("c100"), sb("am", s)), (mat("c200"), sb("set", s)), votes])
-            mm("Gs", pk("Gs", s), [(mat("c100"), sb("am", s)), votes] + ([(mat("cG"), Gold)] if t else []))
-            oh = cols("SO", 256 * s + ca, 256 * s + ca + 64, key=sh + "_lh") if last else cols(sl, 128 * s + ca, 128 * s + ca + 64, key=sh + "_lh")
-            oo = cols("SO", 256 * s + cb, 256 * s + cb + 64, key=sh + "_lo") if last else cols(sl, 128 * s + cb, 128 * s + cb + 64, key=sh + "_lo")
-            oi = cols("SO", 256 * s + 128, 256 * s + 192, key=sh + "_zi") if last else cols(sz, 192 * s + 64, 192 * s + 128, key=sh + "_zi")
-            og = cols("SO", 256 * s + 192, 256 * s + 256, key=sh + "_zg") if last else cols(sz, 192 * s + 128, 192 * s + 192, key=sh + "_zg")
+            ts("rej", rej, pk("cntv", s), y1, OP.is_lt)
+            scan("ad", slot("ad", s), slot("rjz", s), slot("R", s), OP.add, 192)
+            ad = slot("ad", s, 2)
+            mm("ys", pk("ys", s), [(mat("c100"), rec), (mat("n100"), nam), (mat("c200"), sb("set", s)), votes])
+            mm("Gs", pk("Gs", s), [(mat("n100"), nam), votes] + ([(mat("cG"), Gold)] if t else []))
+            out = lambda a, name, b, key: cols("SO", 256 * s + a, 256 * s + a + 64, key=sh + key) if last else cols(name, b, b + 64, key=sh + key)
+            oh, oo = out(ca, sl, 128 * s + ca, "_h"), out(cb, sl, 128 * s + cb, "_o")
+            oi, og = out(128, sz, 192 * s + 64, "_i"), out(192, sz, 192 * s + 128, "_g")
             if splice:
-                sp = sb("sp", s)
+                sp, q = sb("sp", s), pk("q", s)
                 tt("sp", sp, pk("ys", s), Iold, OP.is_lt)
-                mm("cnt2", pk("cnt2", s), [(mat("TRIp"), sp)])
-                ts("pc", sb("pc", s), pk("cnt2", s), -16.0, OP.add, 0.0, OP.max)
-                ts("so", sb("so", s), sb("pc", s), 1, OP.bitwise_and)
-                tt("q", sb("q", s), sb("so", s), pk("CH", s), OP.mult)
-                if opt["spoh"] == "a":
-                    mm("spP", pk("spP", s), [(I, Oc), (nI, Hc), (mat("p8I"), sp)])
-                    act("spoh", sb("spoh", s), pk("spP", s), AF.Relu, bias=-4096.0)
-                elif opt["fin"] == "t":
-                    tt("spoh", sb("spoh", s), sp, pk("OH", s), OP.mult)
-                else:
-                    tt("spoh", pk("spP", s), sp, pk("OH", s), OP.mult)
-                if opt["fin"] == "t":
-                    ts("fxc", sb("fxc", s), sb("fx", s), -2048.0, OP.add)
-                    mm("H20", pk("H2", s), [(I, Hc), f32("I32", sb("accd", s))], last=False)
-                    mm("H2", pk("H2", s), [f32("I32", sb("q", s))], first=False)
-                    mm("O20", pk("O2", s), [f32("nI32", sb("spoh", s)), (I, sb("fxc", s))] + ([(mat("p4I"), sp)] if opt["spoh"] == "a" else []), last=False)
-                    mm("O2", pk("O2", s), [f32("I32", sb("q", s))], first=False)
-                    ts("O16", oo, pk("O2", s), 2048.0, OP.add)
-                    ts("H16", oh, pk("H2", s), 2048.0, OP.add)
-                else:
-                    tt("pre", pk("spP", s), sb("fx", s), pk("spP", s), OP.subtract)
-                    tt("ad", pk("d2", s), sb("accd", s), pk("Hp", s), OP.add)
-                    tt("lo", oo if last else sb("P2", s), sb("q", s), pk("spP", s), OP.add)
-                    tt("lh", oh if last else sb("accd", s), sb("q", s), pk("d2", s), OP.add)
-                    if not last:
-                        cp("O16", oo, sb("P2", s))
-                        cp("H16", oh, sb("accd", s))
-            else:
-                cp("O16", oo, sb("fx", s))
-                if opt["fin"] == "t":
-                    mm("H2", pk("H2", s), [(I, Hc), f32("I32", sb("accd", s))])
-                    ts("H16", oh, pk("H2", s), 2048.0, OP.add)
-                else:
-                    tt("ad", pk("d2", s), sb("accd", s), pk("Hp", s), OP.add)
-                    cp("H16", oh, pk("d2", s))
+                mm("cnt2", pk("cnt2", s), [(mat("TRIo"), sp)] + whole("r2") + [(mat("TRI"), sp)])
+                tt("so", sb("so", s), sp, HC, OP.mult)
+                tt("q", q, sb("so", s), pk("cnt2", s), OP.mult)
+                tt("spoh", pk("spoh", s), sp, OH, OP.mult)
+                tt("pre", sb("pre", s), sb("fx", s), pk("spoh", s), OP.subtract)
+                tt("lo", oo if last else sb("lo", s), sb("pre", s), q, OP.subtract)
+                tt("lh", oh if last else sb("lh", s), ad, q, OP.subtract)
+            if not last:
+                cp("O16", oo, sb("lo" if splice else "fx", s))
+                cp("H16", oh, sb("lh", s) if splice else ad)
             if t == 0:
-                ts("inc", oi, pk("ys", s), 101.0 / 128, OP.is_lt, -155.0 / 128, OP.add)
+                ts("inc", oi, pk("ys", s), y1, OP.is_lt, -i0, OP.add)
             else:
-                act("inc", sb("inc", s), pk("ys", s), AF.Sign, scale=-1.0, bias=101.0 / 128)
+                act("inc", sb("inc", s), pk("ys", s), AF.Sign, scale=-1.0, bias=y1)
                 mm("I2p", pk("I2", s), [(I, Iold), (mat("hI"), sb("inc", s))] + ([(mat("n3I"), sb("sp", s))] if splice else []))
-                act("I2", oi, pk("I2", s), AF.Copy, bias=0.5 + (155.0 / 128 if last else 0.0))
+                act("I2", oi, pk("I2", s), AF.Copy, bias=0.5 + (i0 if last else 0.0))
             if last:
-                ts("G", og, pk("Gs", s), 101.0 / 128, OP.is_ge)
+                ts("G", og, pk("Gs", s), y1, OP.is_ge)
                 for x, y, qq in ((oi, "yi", "ss"), (og, "yg", "ss"), (oh, "ya", "sa"), (oo, "yb", "sa")):
                     a = 256 * s + {"ya": ca, "yb": cb, "yi": 128, "yg": 192}[y]
                     for c in range(2):
                         dma(qq[c], "out", part(y, s, 64 * c, 64 * c + 64, None), part("SO", c, a, a + 64, x[0]), 30)
             else:
-                act("G", og, pk("Gs", s), AF.Relu, scale=2.0 ** 20, bias=-101.0 * 8192)
-                mm("dm", pk("k%d" % s, 1), [(mat("n2"), sb("acc", s))])
-                add("g", None, [sh + "_lo", sh + "_lh"], [sh + "_L"], fx=0.3, send=(t, s, "L"), name="sendL")
-                if opt["msg"] == 3:
-                    add("g", None, [sh + "_zi", sh + "_zg", sh + "_L"], [sh + "_N"], fx=0.3, send=(t, s, "N"), name="sendN")
-                else:
-                    add("g", None, [sh + "_zi", sh + "_zg", sh + "_zz"] + ([sh + "_L"] if opt["msg"] == 2 else []), [sh + "_W"], fx=0.3, send=(t, s, "W"), name="sendN")
+                act("G", og, pk("Gs", s), AF.Relu, scale=2.0 ** 20, bias=-y1 * 2.0 ** 20)
+                mm("dm", pk("k%d" % s, 1), [(mat("p2"), rej)])
+                add("g", None, [sh + "_o", sh + "_h"], [sh + "_L"], send=(t, s, "L"), name="sendL")
+                add("g", None, [sh + "_i", sh + "_g", sh + "_L"], [sh + "_N"], send=(t, s, "N"), name="sendN")
         if not last:
-            kp = cols("ks", 0, 1)
-            act("kp", full("SO2"), ([pk("k0", 1)[0], pk("k1", 1)[0]], pk("k0", 1, 0, 128)[1]), AF.Copy, bias=256.0, n=128, accum=kp)
-            ts("KI", full("KI"), I, kp, OP.mult)
+            act("kp", full("kw"), two("k0", "k1", 1), AF.Copy, n=128, accum=full("ks"))
+            ts("KI", full("KI"), I, full("ks"), OP.mult)
     return ops
 
 
 def cost(o, fig):
     fx, cy, ga, sca, tc = o["c"]
-    if "send" in o:
-        return fig["issue"]
-    return fx + fig["cy"] * (cy + fig["ga"] * ga + fig["sca"] * sca) + fig["pcy"] * tc
+    return fig["issue"] if "send" in o else fx + fig["cy"] * (cy + fig["ga"] * ga + fig["sca"] * sca) + fig["pcy"] * tc
 
 
 def late(o, fig):
-    return fig["hop"] + (0.5 if o["name"] == "arrW" else 0.0) if "arr" in o else 2.0 + o["lat"] / fig["dma"] if "lat" in o else 0.0
+    return fig["hop"] if "arr" in o else 2.0 + o["lat"] / fig["dma"] if "lat" in o else 0.0
 
 
 def graph(opt):
     ops = build(opt)
-    n = len(ops)
-    deps = [set() for _ in range(n)]
+    deps, succ = [set() for _ in ops], [[] for _ in ops]
     lastw, readers = {}, {}
 
     def keys(l):
@@ -559,13 +434,8 @@ def graph(opt):
         for k in l:
             out += keys(k) if isinstance(k, (list, tuple)) else ([k] if k else [])
         return out
-    for o in ops:
-        o["r"], o["w"] = keys(o["r"]), keys(o["w"])
-    used = set(k for o in ops for k in o["r"])
-    ops = [o for o in ops if o["t"] >= 0 or used.intersection(o["w"])]
-    n = len(ops)
-    deps = deps[:n]
     for i, o in enumerate(ops):
+        o["r"], o["w"] = keys(o["r"]), keys(o["w"])
         for k in o["r"] + o["w"]:
             if k in lastw:
                 deps[i].add(lastw[k])
@@ -578,121 +448,9 @@ def graph(opt):
             readers[k] = []
         deps[i].discard(i)
         o["banks"] = sorted(set(k.split(":")[0] for k in o["r"] + o["w"] if k.startswith("ps")))
-    succ = [[] for _ in range(n)]
-    for i in range(n):
-        for j in deps[i]:
+        for j in sorted(deps[i]):
             succ[j].append(i)
     return ops, deps, succ
-
-
-def cyclic(gr, phase, fig):
-    ops, deps, succ = gr
-    n = len(ops)
-    wake = fig["wake"]
-    key = [0.0] * n
-    for i in range(n - 1, -1, -1):
-        o = ops[i]
-        if o["t"] < 0:
-            key[i] = -99.0 + i * 1e-3 if "sem" in o else min([key[k] for k in succ[i]] or [0.0]) - 3.0
-        else:
-            key[i] = o["t"] * phase["period"] + o["s"] * phase["lag"] + phase.get(o["name"], 0.0) if o["q"] else -99.0
-    deps = [set(d) for d in deps]
-    left = [len(d) for d in deps]
-    end = [0.0] * n
-    free, bank, order, shut = {}, {}, [], set()
-    rdy = set(i for i in range(n) if left[i] == 0)
-    while rdy:
-        i = min((key[k], k) for k in rdy if not (shut and ops[k]["q"] == "t" and ops[k]["first"] and ops[k]["banks"][0] in shut))[1]
-        o = ops[i]
-        q = o["q"]
-        for b in o["banks"]:
-            for e, j in bank.get(b, {}).items():
-                if e != q:
-                    deps[i].add(j)
-            bank.setdefault(b, {})[q] = i
-        if q == "t":
-            if o["last"]:
-                shut.discard(o["banks"][0])
-            else:
-                shut.add(o["banks"][0])
-        s = max([end[j] for j in deps[i]] or [0.0]) + (wake if q and deps[i] else 0.0)
-        if q:
-            s = max(s, free.get(q, 0.0))
-            free[q] = s + cost(o, fig)
-        end[i] = s + cost(o, fig) + late(o, fig)
-        o["start"] = s
-        order.append(i)
-        rdy.discard(i)
-        for k in succ[i]:
-            left[k] -= 1
-            if left[k] == 0:
-                rdy.add(k)
-    assert len(order) == n
-    return deps, order, max(end)
-
-
-def schedule(gr, offs, window, fig):
-    ops, deps, succ = gr
-    n = len(ops)
-    wake = fig["wake"]
-    cs = [cost(o, fig) for o in ops]
-    lt = [late(o, fig) for o in ops]
-    pri = [0.0] * n
-    for i in range(n - 1, -1, -1):
-        pri[i] = cs[i] + lt[i] + (wake if ops[i]["q"] else 0.0) + max([pri[k] for k in succ[i]] or [0.0])
-    pri = [window * (pri[i] + offs.get(ops[i]["name"], 0.0) + (offs.get("lead", 0.0) if ops[i]["s"] == 0 else 0.0)) for i in range(n)]
-    deps = [set(d) for d in deps]
-    left = [len(d) for d in deps]
-    end = [0.0] * n
-    free, bank, order, shut = {}, {}, [], set()
-    rdy = dict((i, 0.0) for i in range(n) if left[i] == 0)
-    while rdy:
-        best = {}
-        for i, s in rdy.items():
-            o = ops[i]
-            q = o["q"]
-            if q == "t" and o["first"] and o["banks"][0] in shut:
-                continue
-            f = free.get(q, 0.0)
-            if f > s:
-                s = f
-            for b in o["banks"]:
-                for e, j in bank.get(b, {}).items():
-                    if e != q and end[j] + wake > s:
-                        s = end[j] + wake
-            x = best.get(q)
-            if x is None:
-                best[q] = [s, s - pri[i], i, s]
-            else:
-                if s < x[0]:
-                    x[0] = s
-                if s - pri[i] < x[1]:
-                    x[1], x[2], x[3] = s - pri[i], i, s
-        q = min(best, key=lambda k: best[k][0])
-        i, s = best[q][2], best[q][3]
-        o = ops[i]
-        for b in o["banks"]:
-            for e, j in bank.get(b, {}).items():
-                if e != q:
-                    deps[i].add(j)
-            bank.setdefault(b, {})[q] = i
-        if q == "t":
-            if o["last"]:
-                shut.discard(o["banks"][0])
-            else:
-                shut.add(o["banks"][0])
-        if q:
-            free[q] = s + cs[i]
-        end[i] = s + cs[i] + lt[i]
-        o["start"] = s
-        order.append(i)
-        del rdy[i]
-        for k in succ[i]:
-            left[k] -= 1
-            if left[k] == 0:
-                rdy[k] = max(end[j] for j in deps[k]) + (wake if ops[k]["q"] else 0.0)
-    assert len(order) == n
-    return deps, order, max(end)
 
 
 def events(gr, ph, fig):
@@ -704,7 +462,7 @@ def events(gr, ph, fig):
         if o["t"] < 0:
             key[i] = -99.0 + i * 1e-3 if "sem" in o else ph.get(o["name"], min(min(key[k] for k in succ[i]) - 3.0, 5.0))
         else:
-            key[i] = o["t"] * ph["period"] + (o["s"] or 0) * (ph["lag"] + ph.get("lag%d" % o["t"], 0.0)) + ph.get(o["name"], 12.0) if o["q"] else -99.0
+            key[i] = o["t"] * ph["period"] + o["s"] * (ph["lag"] + ph.get("lag%d" % o["t"], 0.0)) + ph.get(o["name"], 12.0) if o["q"] else -99.0
     left, end, order = [len(d) for d in deps], [0.0] * n, []
     rdy, free, bank, shut = dict((q, {}) for q in "vatgs"), dict.fromkeys("vatgs", 0.0), {}, set()
     deps = [set(d) for d in deps]
@@ -751,10 +509,10 @@ def events(gr, ph, fig):
     return deps, order, max(end)
 
 
-def plan(opt=None, phase=None):
+def plan(opt=None):
     gr = graph(opt or OPT)
     ops = gr[0]
-    deps, order, span = events(gr, phase or dict((x.split(":")[0], float(x.split(":")[1])) for x in PHASE.split()), FIG)
+    deps, order, span = events(gr, dict((x.split(":")[0], float(x.split(":")[1])) for x in PHASE.split()), FIG)
     count = {}
     for i in order:
         o = ops[i]
@@ -775,8 +533,7 @@ def plan(opt=None, phase=None):
 
 def send_aps(o, far, near):
     t, s, k = o["send"]
-    a, b, w = {"L": (128 * s, 128 * s + 128, "L"), "Z": (192 * s, 192 * s + 64, "Z"), "N": (192 * s + 64, 192 * s + 192, "Z"),
-               "W": (192 * s, 192 * s + 192, "Z")}[k]
+    a, b, w = {"L": (128 * s, 128 * s + 128, "L"), "Z": (192 * s, 192 * s + 64, "Z"), "N": (192 * s + 64, 192 * s + 192, "Z")}[k]
     return [(far["%s%d" % (w, t + 1)][:, a:b], near["S%s%d" % (w, t)][:, a:b])]
 
 

@@ -5,13 +5,13 @@ NS = 2
 NB = 1024
 QB = NB // 4
 
-OPT = {"h": "R2 R2", "o": "F1 F1 F1 F1", "c": "F1 F1 F1 F1", "ch": "a2 v2", "zexp": "v2 v2", "yv": "v", "off": "t"}
+OPT = {"h": "R2 R2", "o": "F1 F1 F1 F1", "c": "F1 F1 F1 F1", "ch": "a2 v2", "zexp": "v2 v2", "yv": "v", "t32": "t", "xfirst": 1}
 
 SCALED = {"nI": -1.0, "p8I": 8192.0, "c2080": 2080.0, "c1184": 1184.0, "c32": 32.0, "c100": 100.0 / 128, "n100": -100.0 / 128,
           "c200": 200.0 / 128, "hI": 0.5, "n3I": -3.0, "cG": 1.0 / 8192, "c63": 63.0}
 MATS = ["p2", "ones", "bt", "I", "BM", "TRI", "TRIm", "TRIo", "BMs", "Sw", "hSw", "Wb0", "Wb1", "nWb0", "nWb1"] + sorted(SCALED)
-TILES = {"k2048": 2048.0, "kL2": 65536.0 - 8388608.0, "k155": -15.5, "k325": 32.5, "r2": 1.5 * 2.0 ** 24, "r4096": 1.5 * 2.0 ** 35}
-ROUND32 = 1.5 * 2.0 ** 28
+TILES = {"k2048": 2048.0, "kL2": 65536.0 - 8388608.0, "k155": -15.5, "k325": 32.5, "r2": 1.5 * 2.0 ** 24, "r32": 1.5 * 2.0 ** 28,
+         "r4096": 1.5 * 2.0 ** 35}
 SCRATCH = {"MAT": ("sbuf", [128, 128 * len(MATS)], "bfloat16"), "KT": ("sbuf", [128, 64 * len(TILES)], "bfloat16"),
            "mk": ("sbuf", [128, 64], "bfloat16"), "nQ": ("sbuf", [128, 144], "bfloat16"), "KI": ("sbuf", [128, 128], "float16"),
            "ri": ("sbuf", [128, 4], "int32"), "rf": ("sbuf", [128, 4], "float32"), "mi": ("sbuf", [128, 64], "int32"),
@@ -19,9 +19,10 @@ SCRATCH = {"MAT": ("sbuf", [128, 128 * len(MATS)], "bfloat16"), "KT": ("sbuf", [
            "zmask": ("sbuf", [128, NB // 2], "bfloat16"), "ks": ("sbuf", [128, 1], "float32"), "kw": ("sbuf", [128, 128], "float32"),
            "SO": ("sbuf", [128, 512], "float32"), "iab": ("sbuf", [128, 256], "int32"), "abn": ("sbuf", [128, 256], "float16"),
            "zn": ("sbuf", [128, 128], "bfloat16"), "wn": ("sbuf", [128, 1], "bfloat16")}
-F32 = ("P", "dhs", "thr", "m", "setH", "so", "pre", "P2", "lh", "lo")
-I32 = ("S", "ci", "S2", "fx")
-B16 = ("set", "w", "yv", "inc", "sp", "sc")
+F32 = ("P", "dhs", "thr", "m", "so", "pre", "lh")
+I32 = ("S", "ci", "fx")
+B16 = ("set", "w", "yv", "inc", "sp", "sc", "rej")
+PAIRS = ("U", "sH", "S2")
 SMALL = {}
 for _t in range(NT):
     SCRATCH["L%d" % _t] = ("sbuf", [128, 256], "uint16")
@@ -33,9 +34,9 @@ for _s in range(NS):
     SCRATCH["X%d" % _s] = ("sbuf", [128, 4096], "bfloat16")
     for _n in ("zbuf", "zexp", "hr", "ha", "od", "oa", "cd", "ca", "ch", "Mf"):
         SCRATCH["%s_%d" % (_n, _s)] = ("sbuf", [128, NB], "bfloat16")
-    for _n, _c, _d in (("chz", 192, "bfloat16"), ("rjz", 192, "bfloat16"), ("R", 192, "float32"), ("ad", 192, "float32"), ("HO", 128, "float16"),
+    for _n, _c, _d in (("chz", 192, "bfloat16"), ("R", 192, "float32"), ("HO", 128, "float16"),
                        ("t32", 64, "float16"), ("c16", 64, "uint16"), ("ch16", 64, "uint16"), ("u16", 8, "uint16"), ("gx", 128, "float32"),
-                       ("gs", 128, "int32")):
+                       ("gs", 128, "int32"), ("sH", 128, "float32"), ("S2", 128, "int32")):
         SCRATCH["%s_%d" % (_n, _s)] = ("sbuf", [128, _c], _d)
     for _b, _l, _d in (("F", F32, "float32"), ("J", I32, "int32"), ("B", B16, "bfloat16")):
         for _i, _n in enumerate(_l):
@@ -50,24 +51,24 @@ SEMAPHORES = ["qv", "qa", "qt", "qg", "loc"] + ["in%d" % _i for _i in range(NIN)
 
 PS = {}
 for _s in range(NS):
-    for _b, _l in ((2, ("dh u", "do v", "pen r", "cnt off", "cntv", "ys", "Gs", "cnt2")),
-                   (4, ("dc", "V", "zd", "I2", "Mh", "Mh2", "k0", "k1")),
-                   (6, ("Hp", "L L2", "A", "", "", "spoh", "q", "wp"))):
+    for _b, _l in ((2, ("dh", "do v", "pen r", "cnt off", "cntv", "Gs", "ys", "cnt2")),
+                   (4, ("dc spoh", "V", "zd", "I2", "Mh", "Mh2", "k0", "k1")),
+                   (6, ("Hp", "L d2", "A", "", "", "U", "", "q wp"))):
         for _i, _n in enumerate(_l):
             for _m in _n.split():
                 PS[_m, _s] = (_b + _s, _i)
 
-FIG = {"cy": 0.97e-3, "pcy": 0.6e-3, "ga": 1.56, "sca": 3.8, "wake": 0.21, "hop": 5.5, "dma": 400.0, "issue": 0.3}
-PHASE = """a0:-24.74 z1:-23.45 zbuf:-21.64 z0:-21.52 zexp1:-20.96 L:-20.08 OH:-19.79 gch0:-14.32 sendL:-11.8 HO:-11.54 S2:-10.66
-ch16:-10.13 lag4:-9.93 M1:-8.59 M0:-8.58 fx:-8.48 u:-8.24 rej:-6.33 TRIm:-5.5 TRI:-5.3 H16:-5.01 l0:-5.01 base:-4.8 mi:-4.7 out7:-4.07
-nQ:-3.1 sendZ:-3.08 Sw:-3 zexp0:-1.75 go3:-1.73 S:-1.54 Hp:-1.31 spoh:-1.23 so:-1.13 go1:-1.1 P:-1.07 ao3:-1.06 gh1:-1.05 w:-0.91
-zd:-0.76 m:-0.69 look:0.1 ao0:0.37 out0:0.69 out1:0.79 out6:0.79 lag3:0.88 go2:0.9 ci:0.96 lag2:0.96 gh0:0.97 set:1.27 L2:1.31 pen:1.51
-ao1:1.59 ao2:1.59 do:1.6 out3:1.66 gc1:1.7 lag1:1.73 abn:2.1 c16:2.14 yh0:2.33 lag0:2.61 fill:2.8 ah1:2.84 ac2:2.95 gc0:3.13 ah0:3.66
-go0:3.92 C:3.97 gc3:3.98 dhs:4.16 dc:4.43 sendN:4.52 gc2:4.68 ac0:4.69 cnt:4.8 nam:4.81 ac1:4.83 HC:4.87 thr2:5.12 rec:5.69 out2:5.74
-thr:6.46 wp:6.6 lag:6.74 ac3:7.33 yh1:7.36 dh:7.68 mk:7.7 G:7.76 dm:8.49 V:8.5 setH:8.52 out4:8.53 Wb:8.6 I:8.7 hsum:9.18 yv:9.79
-cntv:9.8 ys:10.42 Gs:10.43 P2:10.72 sp:11.12 gch1:11.16 cho:11.41 d2:11.49 O16:11.84 pre:11.99 ad:12.22 q:12.25 lh:12.32 lo:12.4
-zz:12.45 t32:12.45 gs:12.84 KI:13.64 Mh:14.42 Mh2:14.43 I2:14.78 u16:15.54 gx:15.85 sc:15.98 off:17.87 inc:19.08 kp:19.52 cnt2:19.59
-scat:19.7 v:20.13 I2p:21.06 period:22.17 out5:22.52 r:22.78"""
+FIG = {"cy": 0.97e-3, "pcy": 0.6e-3, "ga": 1.56, "sca": 3.8, "wake": 0.24, "hop": 5.2, "dma": 500.0, "issue": 0.3}
+PHASE = """lag4:-29.97 a0:-25.52 z0:-24.14 z1:-22.84 sendL:-13.83 gch0:-13.31 zbuf:-11.69 ch16:-6.44 BM:-5.6 HO:-4.83 L:-4.69 bt:-4.3
+wp:-4.1 zexp0:-4.07 l0:-3.8 bi:-3.5 S:-3.26 Hp:-3.04 lag1:-3.01 lag3:-2.8 fill:-2.8 OH:-2.78 gh1:-2.33 gch1:-2.19 M1:-2.18 lag2:-1.84
+out3:-1.47 P:-1.31 dhs:-1.14 Sw:-1.1 ao0:-0.76 M0:0.07 look:0.1 scaled:0.4 c16:0.72 ac0:1.57 gh0:1.78 go1:1.87 abn:2.1 u:2.19 lag0:2.26
+TRI:2.5 sendZ:2.7 w:3.26 ac2:3.27 nQ:3.3 ao1:3.51 yh0:3.73 pen:4.09 hsum:4.13 ao3:4.29 m:4.47 gc3:4.5 gc0:4.54 gc1:4.54 ao2:4.62
+ah1:4.72 ah0:4.9 go3:5.07 thr2:5.13 zexp1:5.17 V:5.17 go2:5.21 ac3:5.24 set:5.27 do:5.28 ci:5.46 yv:5.88 gc2:5.92 TRIm:6 L2:6.07
+ri0:6.2 ac1:6.33 yh1:6.35 out2:6.83 I:7 go0:7.2 ys:7.6 lag:7.7 rec:7.89 nam:7.9 C:8.11 setH:8.22 Wb:8.3 spoh:9.14 rej:9.44 sp:9.45
+pre:9.69 mk:9.8 HC:9.93 zd:10.09 back:10.13 d2:10.55 cntv:10.63 mi:10.7 cho:10.8 ad:10.81 dh:10.99 base:11 thr:11.16 cnt2:11.32
+dm:11.36 zz:11.38 lo:11.82 S2:12.12 out1:12.57 O16:12.62 sendN:13.2 dc:13.21 lh:13.42 out0:13.73 out4:13.81 out6:13.83 cnt:14.45
+so:15.57 gx:15.77 q:18.58 u16:19.65 I2p:20.81 kp:21.54 gs:22.94 Gs:23.18 period:23.33 sc:24.31 r:24.48 scat:24.56 Mh:25.08 Mh2:25.09
+out7:25.68 KI:25.91 I2:26.4 out5:27.66 off:28.32 inc:29.69 G:30.02 fx:30.28"""
 
 
 def build(opt):
@@ -105,9 +106,10 @@ def build(opt):
         return full(n)
 
     def slot(name, s, k=None):
-        n, a = ("ps%d" % PS["A", s][0], 64 * PS["A", s][1]) if name == "A" else ("%s_%d" % (name, s), 0)
+        n, a = ("ps%d" % PS[name, s][0], 64 * PS[name, s][1]) if (name, s) in PS else ("%s_%d" % (name, s), 0)
+        m = 2 if name in PAIRS else 3
         key = lambda j: "%s:%s%d" % (n, name, j)
-        return cols(n, a, a + 192, key=[key(j) for j in range(3)]) if k is None else cols(n, a + k, a + 192, 3, key=key(k))
+        return cols(n, a, a + 64 * m, key=[key(j) for j in range(m)]) if k is None else cols(n, a + k, a + 64 * m, m, key=key(k))
 
     def inps(x):
         return (x[0] if isinstance(x[0], str) else x[0][0]).startswith("ps")
@@ -187,9 +189,9 @@ def build(opt):
     def rows(x, s):
         return (x[0], lambda T: x[1](T)[64 * s:64 * s + 64, :])
 
-    dma("s", "in", cols("iab", 0, 128, key="ia"), (None, lambda T: T.ba[:]), 100)
-    dma("a", "in", cols("iab", 128, 256, key="ib"), (None, lambda T: T.bb[:]), 200)
-    dma("s", "in", full("zn"), (None, lambda T: T.zp[:]), 270)
+    dma("s", "in", full("zn"), (None, lambda T: T.zp[:]), 70)
+    dma("a", "in", cols("iab", 128, 256, key="ib"), (None, lambda T: T.bb[:]), 170)
+    dma("s", "in", cols("iab", 0, 128, key="ia"), (None, lambda T: T.ba[:]), 270)
     for s in range(NS):
         for c in range(2):
             dma("as"[c], "in", part("X%d" % s, c, 0, 4096, "Xin%d.%d" % (s, c)), part("xt", s, 0, 4096, None), 1300 + 1024 * s)
@@ -211,11 +213,12 @@ def build(opt):
     for s in range(NS):
         memset(full("zbuf_%d" % s), 0.0, NB // 2)
         memset(slot("chz", s), 0.0, 96)
-        memset(slot("rjz", s), 0.0, 96)
+        memset(slot("sH", s), 0.0, 128)
     memset(full("zmask"), 1.0, NB // 4)
     memset(cols("zmask", 0, NB // 2, 16), 0.0, 64, again=True)
     for n in sorted(TILES):
-        memset(tile(n), TILES[n], 64)
+        if n != "r32" or opt["t32"] == "t":
+            memset(tile(n), TILES[n], 64)
     for n in sorted(SCALED):
         ts("scaled", mat(n), I, SCALED[n], OP.mult)
     memset(full("nQ"), 0.0, 72)
@@ -321,13 +324,13 @@ def build(opt):
                 tt("thr2", sb("thr", s), pk("pen", s), Gold, OP.add)
             tt("w", sb("w", s), pk("dc", s), sb("thr", s), OP.is_gt)
             mm("cnt", pk("cnt", s), [(mat("TRIm"), sb("w", s))])
-            rec, nam, rej = slot("chz", s, 1), slot("chz", s, 2), slot("rjz", s, 2)
+            rec, nam, rej = slot("chz", s, 1), slot("chz", s, 2), sb("rej", s)
             tt("m", sb("m", s), pk("dc", s), sb("dhs", s), OP.max)
             tt("rec", rec, pk("do", s), sb("m", s), OP.is_ge)
             ts("nam", nam, pk("cnt", s), -13.0, OP.is_ge)
             scan("cho", slot("R", s), slot("chz", s), slot("A", s), OP.add, 192)
             cp("ch16", sb("ch16", s), slot("R", s, 2))
-            tt("d2", slot("R", s, 1), Hp, slot("R", s, 2), OP.subtract)
+            tt("d2", pk("d2", s), Hp, slot("R", s, 2), OP.subtract)
             mm("hsum", pk("V", s), [(nI, col16("hr", s, j)) for j in range(16)], last=False, after=["ch16_%d" % s])
             for k, (e, p, n) in enumerate(cuts(opt["ch"])):
                 w, o = window(s, lst("ch16_%d" % s, 0, p)), piece("ch", s, p)
@@ -338,20 +341,22 @@ def build(opt):
                 scan("M%d" % k, piece("Mf", s, p), cols("zmask", 0, n), o, OP.max, n // 2)
             mm("V", pk("V", s), [(I, col16("ch", s, j)) for j in range(16)], first=False)
             M, Wb = col16("Mf", s, 15), mat("Wb%d" % s)
-            tt("setH", sb("setH", s), sb("set", s), Hp, OP.mult)
-            mm("u", pk("u", s), [(mat("c63"), tile("k325")), (mat("nWb%d" % s), M)] + whole("r4096") + [(Wb, M)])
-            tt("P2", sb("P2", s), sb("setH", s), pk("u", s), OP.mult)
-            mm("L2", pk("L2", s), [(mat("c32"), Oc), (I, tile("kL2"))] + ([(full("KI"), sb("set", s))] if t else []))
-            tt("S2", sb("S2", s), sb("P2", s), pk("L2", s), OP.add)
-            ts("fx", sb("fx", s), sb("S2", s), 5, OP.arith_shift_right, 4095, OP.bitwise_and)
+            tt("setH", slot("sH", s, 1), sb("set", s), Hp, OP.mult)
+            mm("L2", slot("U", s, 1), [(mat("c32"), Oc), (I, tile("kL2"))] + ([(full("KI"), sb("set", s))] if t else []))
+            mm("u", slot("U", s, 0), [(mat("c63"), tile("k325")), (mat("nWb%d" % s), M)] + whole("r4096") + [(Wb, M)])
+            scan("S2", slot("S2", s), slot("sH", s), slot("U", s), OP.add, 128)
             sl, sz, sh = "SL%d" % t, "SZ%d" % t, "send_%d_%d" % (t, s)
+            ts("fx", sb("fx", s), slot("S2", s, 1), 5, OP.arith_shift_right, 4095, OP.bitwise_and)
             if not last:
                 mm("zd", pk("zd", s), [(I, z), (nI, M)])
                 act("zz", cols(sz, 192 * s, 192 * s + 64, key=sh + "_zz"), pk("zd", s), AF.Abs)
                 add("g", None, [sh + "_zz"], [sh + "_Z"], send=(t, s, "Z"), name="sendZ")
-                mm("v", pk("v", s), [(Wb, M), (I, tile("k155"))])
-                ts("t32", sb("t32", s), pk("v", s), ROUND32, OP.add, -ROUND32, OP.add)
-                mm("r", pk("r", s), [(Wb, M), (nI, sb("t32", s)), (I, full("mk"))])
+                if opt["t32"] == "v":
+                    mm("v", pk("v", s), [(Wb, M), (I, tile("k155"))])
+                    ts("t32", sb("t32", s), pk("v", s), TILES["r32"], OP.add, -TILES["r32"], OP.add)
+                    mm("r", pk("r", s), [(Wb, M), (nI, sb("t32", s)), (I, full("mk"))])
+                else:
+                    mm("r", pk("r", s), [(nI, tile("k155")), (mat("nWb%d" % s), M)] + whole("r32") + [(Wb, M), (I, full("mk"))])
                 scan("sc", sb("sc", s), cols("zmask", 0, 64), pk("r", s), OP.max, 64)
                 b, c0 = SMALL["sc_%d" % s]
                 pick = cols(b, c0 + 15, c0 + 64, 16, key="sc_%d" % s)
@@ -372,13 +377,14 @@ def build(opt):
             y1, i0 = (1 + y0) / 128, (255 - y0) / 128
             mm("cntv", pk("cntv", s), [votes])
             ts("rej", rej, pk("cntv", s), y1, OP.is_lt)
-            scan("ad", slot("ad", s), slot("rjz", s), slot("R", s), OP.add, 192)
-            ad = slot("ad", s, 2)
+            tt("back", pk("d2", s), rej, pk("d2", s), OP.mult)
             mm("ys", pk("ys", s), [(mat("c100"), rec), (mat("n100"), nam), (mat("c200"), sb("set", s)), votes])
             mm("Gs", pk("Gs", s), [(mat("n100"), nam), votes] + ([(mat("cG"), Gold)] if t else []))
             out = lambda a, name, b, key: cols("SO", 256 * s + a, 256 * s + a + 64, key=sh + key) if last else cols(name, b, b + 64, key=sh + key)
             oh, oo = out(ca, sl, 128 * s + ca, "_h"), out(cb, sl, 128 * s + cb, "_o")
             oi, og = out(128, sz, 192 * s + 64, "_i"), out(192, sz, 192 * s + 128, "_g")
+            ad = sb("lh", s) if splice else oh
+            tt("ad", ad, slot("R", s, 2), pk("d2", s), OP.add)
             if splice:
                 sp, q = sb("sp", s), pk("q", s)
                 tt("sp", sp, pk("ys", s), Iold, OP.is_lt)
@@ -387,11 +393,10 @@ def build(opt):
                 tt("q", q, sb("so", s), pk("cnt2", s), OP.mult)
                 tt("spoh", pk("spoh", s), sp, OH, OP.mult)
                 tt("pre", sb("pre", s), sb("fx", s), pk("spoh", s), OP.subtract)
-                tt("lo", oo if last else sb("lo", s), sb("pre", s), q, OP.subtract)
-                tt("lh", oh if last else sb("lh", s), ad, q, OP.subtract)
-            if not last:
-                cp("O16", oo, sb("lo" if splice else "fx", s))
-                cp("H16", oh, sb("lh", s) if splice else ad)
+                tt("lo", oo, sb("pre", s), q, OP.subtract)
+                tt("lh", oh, ad, q, OP.subtract)
+            else:
+                cp("O16", oo, sb("fx", s))
             if t == 0:
                 ts("inc", oi, pk("ys", s), y1, OP.is_lt, -i0, OP.add)
             else:

from concourse.mybir import AluOpType as OP, ActivationFunctionType as AF

NT = 5
NS = 2
NB = 1024
QB = NB // 4

OPT = {"h": "R2 R2", "o": "F1 F1 F1 F1", "c": "F1 F1 F1 F1", "ch": "a2 v2", "zexp": "v2 v2", "yv": "v", "t32": "t", "xfirst": 1}

SCALED = {"nI": -1.0, "p8I": 8192.0, "c2080": 2080.0, "c1184": 1184.0, "c32": 32.0, "c100": 100.0 / 128, "n100": -100.0 / 128,
          "c200": 200.0 / 128, "hI": 0.5, "n3I": -3.0, "cG": 1.0 / 8192, "c63": 63.0}
MATS = ["p2", "ones", "bt", "I", "BM", "TRI", "TRIm", "TRIo", "BMs", "Sw", "hSw", "Wb0", "Wb1", "nWb0", "nWb1"] + sorted(SCALED)
TILES = {"k2048": 2048.0, "kL2": 65536.0 - 8388608.0, "k155": -15.5, "k325": 32.5, "r2": 1.5 * 2.0 ** 24, "r32": 1.5 * 2.0 ** 28,
         "r4096": 1.5 * 2.0 ** 35}
SCRATCH = {"MAT": ("sbuf", [128, 128 * len(MATS)], "bfloat16"), "KT": ("sbuf", [128, 64 * len(TILES)], "bfloat16"),
           "mk": ("sbuf", [128, 64], "bfloat16"), "nQ": ("sbuf", [128, 144], "bfloat16"), "KI": ("sbuf", [128, 128], "float16"),
           "ri": ("sbuf", [128, 4], "int32"), "rf": ("sbuf", [128, 4], "float32"), "mi": ("sbuf", [128, 64], "int32"),
           "mj": ("sbuf", [128, 64], "int32"), "bi": ("sbuf", [128, 8], "float32"), "base": ("sbuf", [128, 8], "bfloat16"),
           "zmask": ("sbuf", [128, NB // 2], "bfloat16"), "ks": ("sbuf", [128, 1], "float32"), "kw": ("sbuf", [128, 128], "float32"),
           "SO": ("sbuf", [128, 512], "float32"), "iab": ("sbuf", [128, 256], "int32"), "abn": ("sbuf", [128, 256], "float16"),
           "zn": ("sbuf", [128, 128], "bfloat16"), "wn": ("sbuf", [128, 1], "bfloat16")}
F32 = ("P", "dhs", "thr", "m", "so", "pre", "lh")
I32 = ("S", "ci", "fx")
B16 = ("set", "w", "yv", "inc", "sp", "sc", "rej")
PAIRS = ("U", "sH", "S2")
SMALL = {}
for _t in range(NT):
    SCRATCH["L%d" % _t] = ("sbuf", [128, 256], "uint16")
    SCRATCH["Z%d" % _t] = ("sbuf", [128, 384], "bfloat16")
    if _t < NT - 1:
        SCRATCH["SL%d" % _t] = ("sbuf", [128, 256], "uint16")
        SCRATCH["SZ%d" % _t] = ("sbuf", [128, 384], "bfloat16")
for _s in range(NS):
    SCRATCH["X%d" % _s] = ("sbuf", [128, 4096], "bfloat16")
    for _n in ("zbuf", "zexp", "hr", "ha", "od", "oa", "cd", "ca", "ch", "Mf"):
        SCRATCH["%s_%d" % (_n, _s)] = ("sbuf", [128, NB], "bfloat16")
    for _n, _c, _d in (("chz", 192, "bfloat16"), ("R", 192, "float32"), ("HO", 128, "float16"),
                       ("t32", 64, "float16"), ("c16", 64, "uint16"), ("ch16", 64, "uint16"), ("u16", 8, "uint16"), ("gx", 128, "float32"),
                       ("gs", 128, "int32"), ("sH", 128, "float32"), ("S2", 128, "int32")):
        SCRATCH["%s_%d" % (_n, _s)] = ("sbuf", [128, _c], _d)
    for _b, _l, _d in (("F", F32, "float32"), ("J", I32, "int32"), ("B", B16, "bfloat16")):
        for _i, _n in enumerate(_l):
            SMALL["%s_%d" % (_n, _s)] = ("%s_%d" % (_b, _s), 64 * _i)
        SCRATCH["%s_%d" % (_b, _s)] = ("sbuf", [128, 64 * len(_l)], _d)
for _b in range(8):
    SCRATCH["ps%d" % _b] = ("psum", [128, 512], "float32")

NIN, NOUT = 8, 16
SEMAPHORES = ["qv", "qa", "qt", "qg", "loc"] + ["in%d" % _i for _i in range(NIN)] + ["out%d" % _i for _i in range(NOUT)] + \
    ["arr_%d_%d_%s" % (_t, _s, _k) for _t in range(1, NT) for _s in range(NS) for _k in "LZN"]

PS = {}
for _s in range(NS):
    for _b, _l in ((2, ("dh", "do v", "pen r", "cnt off", "cntv", "Gs", "ys", "cnt2")),
                   (4, ("dc spoh", "V", "zd", "I2", "Mh", "Mh2", "k0", "k1")),
                   (6, ("Hp", "L d2", "A", "", "", "U", "", "q wp"))):
        for _i, _n in enumerate(_l):
            for _m in _n.split():
                PS[_m, _s] = (_b + _s, _i)

FIG = {"cy": 0.97e-3, "pcy": 0.6e-3, "ga": 1.56, "sca": 3.8, "wake": 0.24, "hop": 5.2, "dma": 500.0, "issue": 0.3}
PHASE = """lag4:-29.97 a0:-25.52 z0:-24.14 z1:-22.84 sendL:-13.83 gch0:-13.31 zbuf:-11.69 ch16:-6.44 BM:-5.6 HO:-4.83 L:-4.69 bt:-4.3
wp:-4.1 zexp0:-4.07 l0:-3.8 bi:-3.5 S:-3.26 Hp:-3.04 lag1:-3.01 lag3:-2.8 fill:-2.8 OH:-2.78 gh1:-2.33 gch1:-2.19 M1:-2.18 lag2:-1.84
out3:-1.47 P:-1.31 dhs:-1.14 Sw:-1.1 ao0:-0.76 M0:0.07 look:0.1 scaled:0.4 c16:0.72 ac0:1.57 gh0:1.78 go1:1.87 abn:2.1 u:2.19 lag0:2.26
TRI:2.5 sendZ:2.7 w:3.26 ac2:3.27 nQ:3.3 ao1:3.51 yh0:3.73 pen:4.09 hsum:4.13 ao3:4.29 m:4.47 gc3:4.5 gc0:4.54 gc1:4.54 ao2:4.62
ah1:4.72 ah0:4.9 go3:5.07 thr2:5.13 zexp1:5.17 V:5.17 go2:5.21 ac3:5.24 set:5.27 do:5.28 ci:5.46 yv:5.88 gc2:5.92 TRIm:6 L2:6.07
ri0:6.2 ac1:6.33 yh1:6.35 out2:6.83 I:7 go0:7.2 ys:7.6 lag:7.7 rec:7.89 nam:7.9 C:8.11 setH:8.22 Wb:8.3 spoh:9.14 rej:9.44 sp:9.45
pre:9.69 mk:9.8 HC:9.93 zd:10.09 back:10.13 d2:10.55 cntv:10.63 mi:10.7 cho:10.8 ad:10.81 dh:10.99 base:11 thr:11.16 cnt2:11.32
dm:11.36 zz:11.38 lo:11.82 S2:12.12 out1:12.57 O16:12.62 sendN:13.2 dc:13.21 lh:13.42 out0:13.73 out4:13.81 out6:13.83 cnt:14.45
so:15.57 gx:15.77 q:18.58 u16:19.65 I2p:20.81 kp:21.54 gs:22.94 Gs:23.18 period:23.33 sc:24.31 r:24.48 scat:24.56 Mh:25.08 Mh2:25.09
out7:25.68 KI:25.91 I2:26.4 out5:27.66 off:28.32 inc:29.69 G:30.02 fx:30.28"""


def build(opt):
    ops = []
    cur = {"s": None, "t": -1}

    def add(q, fn, r, w, fx=0.0, cy=0.0, ga=0, sca=0, tc=0, **kw):
        ops.append(dict(q=q, fn=fn, r=list(r), w=list(w), s=cur["s"], t=cur["t"], c=(fx, cy, ga, sca, tc), **kw))

    def full(name):
        return (name, lambda T: T[name][:])

    def cols(name, a, b, step=1, key=None):
        return (key or name, lambda T: T[name][:, a:b:step] if step != 1 else T[name][:, a:b])

    def mat(name, a=0, b=128):
        i = 128 * MATS.index(name)
        return cols("MAT", i + a, i + b, key=name)

    def tile(name):
        i = 64 * sorted(TILES).index(name)
        return cols("KT", i, i + 64, key=name)

    def pk(name, s, a=0, b=64):
        bank, i = PS[name, s]
        return ("ps%d:%d" % (bank, i), lambda T: T["ps%d" % bank][:, 64 * i + a:64 * i + b])

    def two(name, other, s):
        return ([pk(name, s)[0], pk(other, s)[0]], pk(name, s, 0, 128)[1])

    def sb(name, s):
        n = "%s_%d" % (name, s)
        if n in SMALL:
            return cols(SMALL[n][0], SMALL[n][1], SMALL[n][1] + 64, key=n)
        return full(n)

    def slot(name, s, k=None):
        n, a = ("ps%d" % PS[name, s][0], 64 * PS[name, s][1]) if (name, s) in PS else ("%s_%d" % (name, s), 0)
        m = 2 if name in PAIRS else 3
        key = lambda j: "%s:%s%d" % (n, name, j)
        return cols(n, a, a + 64 * m, key=[key(j) for j in range(m)]) if k is None else cols(n, a + k, a + 64 * m, m, key=key(k))

    def inps(x):
        return (x[0] if isinstance(x[0], str) else x[0][0]).startswith("ps")

    def num(x):
        return isinstance(x, (int, float))

    def tt(name, out, a, b, op, n=64):
        add("v", lambda g, T: g.vector.tensor_tensor(out[1](T), a[1](T), b[1](T), op), [a[0], b[0]], [out[0]],
            cy=max(64, n * (1 if inps(a) or inps(b) else 2)), name=name)

    def ts(name, out, a, s1, op0, s2=None, op1=None, n=64):
        def fn(g, T):
            sc = s1 if num(s1) else s1[1](T)
            if op1 is None:
                return g.vector.tensor_scalar(out[1](T), a[1](T), sc, None, op0)
            return g.vector.tensor_scalar(out[1](T), a[1](T), sc, s2, op0, op1)
        add("v", fn, [a[0]] + ([] if num(s1) else [s1[0]]), [out[0]], cy=max(64, n), name=name)

    def cp(name, out, a, n=64):
        add("v", lambda g, T: g.vector.tensor_copy(out[1](T), a[1](T)), [a[0]], [out[0]], cy=max(64, n), name=name)

    def scan(name, out, d0, d1, op1, n):
        add("v", lambda g, T: g.vector.tensor_tensor_scan(out[1](T), d0[1](T), d1[1](T), 0.0, OP.mult, op1), [d0[0], d1[0]], [out[0]],
            cy=max(64, n), name=name)

    def act(name, out, a, func, scale=1.0, bias=0.0, n=64, accum=None, ga=0):
        def fn(g, T):
            kw = {}
            if scale != 1.0:
                kw["scale"] = scale
            if bias != 0.0:
                kw["bias"] = bias
            if accum is not None:
                kw["accum_out"] = accum[1](T)
            return g.scalar.activation(out[1](T), a[1](T), func, **kw)
        add("a", fn, [a[0]], [out[0]] + ([accum[0]] if accum is not None else []), fx=0.065 if ga else 0.02, cy=0 if ga else max(64, n),
            ga=ga, name=name)

    def mm(name, out, terms, first=True, last=True, after=(), n=64):
        def fn(g, T):
            r = None
            for k, x in enumerate(terms):
                r = g.tensor.matmul((x[2] if len(x) > 2 else out)[1](T), x[0][1](T), x[1][1](T), first and k == 0, last and k == len(terms) - 1)
            return r
        add("t", fn, [y[0] for x in terms for y in x[:2]] + list(after), [out[0]], tc=n * len(terms), name=name, first=first, last=last)

    def window(s, lst):
        return (["X%d" % s, lst[0]], lambda T: T["X%d" % s][:, 0:4096].indirect(lst[1](T)))

    def memset(out, val, n, again=False):
        add("v", lambda g, T: g.vector.memset(out[1](T), val), [out[0]] if again else [], [out[0]], cy=max(64, n), name="fill")

    nd = {"in": 0, "out": 0}

    def dma(q, kind, out, src, kb):
        add(q, lambda g, T: (g.sync if q == "s" else g.scalar).dma_start(out[1](T), src[1](T)), [src[0]], [out[0]], fx=0.1,
            sem="%s%d" % (kind, nd[kind]), lat=kb, name=kind + str(nd[kind] % 8))
        nd[kind] += 1

    def piece(name, s, p):
        return cols("%s_%d" % (name, s), p[0] * QB, p[1] * QB, key=["%s_%d.%d" % (name, s, k) for k in range(*p)])

    def col16(name, s, j):
        return cols("%s_%d" % (name, s), j, NB, 16, key=["%s_%d.%d" % (name, s, p) for p in range(4)])

    def cuts(text):
        out, a = [], 0
        for x in text.split():
            out.append((x[0], (a, a + int(x[1])), int(x[1]) * QB))
            a += int(x[1])
        return out

    def part(name, c, a, b, key):
        return (key, lambda T: T[name][64 * c:64 * c + 64, a:b])

    def rows(x, s):
        return (x[0], lambda T: x[1](T)[64 * s:64 * s + 64, :])

    dma("s", "in", full("zn"), (None, lambda T: T.zp[:]), 70)
    dma("a", "in", cols("iab", 128, 256, key="ib"), (None, lambda T: T.bb[:]), 170)
    dma("s", "in", cols("iab", 0, 128, key="ia"), (None, lambda T: T.ba[:]), 270)
    for s in range(NS):
        for c in range(2):
            dma("as"[c], "in", part("X%d" % s, c, 0, 4096, "Xin%d.%d" % (s, c)), part("xt", s, 0, 4096, None), 1300 + 1024 * s)
        if s == 0:
            dma("s", "in", full("wn"), (None, lambda T: T.wl[:]), 1330)

    def gp(fn, r, w, n):
        add("g", fn, r, w, fx=0.17, cy=2 * n, name=w[0])
    I, nI = mat("I"), mat("nI")
    memset(mat("ones"), 1.0, 64)
    sel = lambda o, i, pat, cmp, b, ch: gp(lambda g, T: g.affine_select(mat(o)[1](T), mat(i)[1](T), pat, cmp, 0.0, b, ch), [i], [o], 128)
    sel("I", "ones", [[-1, 128]], OP.is_equal, 0, 1)
    sel("bt", "ones", [[-16, 8], [0, 16]], OP.is_ge, 0, 1)
    sel("BM", "bt", [[16, 8], [0, 16]], OP.is_ge, 15, -1)
    sel("TRI", "BM", [[1, 128]], OP.is_gt, 0, -1)
    gp(lambda g, T: g.iota(T.mi[:], [[-1, 64]], 64, 1), [], ["mi"], 64)
    gp(lambda g, T: g.iota(T.ri[:, 0:1], [[0, 1]], 0, 1), [], ["ri0"], 1)
    gp(lambda g, T: g.iota(T.bi[:], [[2048, 2], [512, 4]], 0, 0, allow_small_or_imprecise_dtypes=True), [], ["bi"], 8)
    for s in range(NS):
        memset(full("zbuf_%d" % s), 0.0, NB // 2)
        memset(slot("chz", s), 0.0, 96)
        memset(slot("sH", s), 0.0, 128)
    memset(full("zmask"), 1.0, NB // 4)
    memset(cols("zmask", 0, NB // 2, 16), 0.0, 64, again=True)
    for n in sorted(TILES):
        if n != "r32" or opt["t32"] == "t":
            memset(tile(n), TILES[n], 64)
    for n in sorted(SCALED):
        ts("scaled", mat(n), I, SCALED[n], OP.mult)
    memset(full("nQ"), 0.0, 72)
    i0 = 128 * MATS.index("BM")
    ts("nQ", cols("nQ", 15, 143, 16), cols("MAT", i0, i0 + 128, 16, key="BM"), -1.0, OP.mult)
    ts("scaled", mat("TRIm"), I, -16.0, OP.mult)
    tt("TRIm", mat("TRIm"), mat("TRIm"), mat("TRI"), OP.add, n=128)
    ts("scaled", mat("BMs"), mat("BM"), (1.0 if opt["yv"] == "a" else 2.0) / 128, OP.mult)
    ts("scaled", mat("TRIo"), mat("TRI"), -31.0 / 32, OP.mult)
    cp("Sw", mat("Sw", 0, 64), mat("I", 64, 128))
    cp("Sw", mat("Sw", 64, 128), mat("I", 0, 64))
    ts("scaled", mat("hSw"), mat("Sw"), 0.5, OP.mult)
    memset(mat("p2"), 2.0, 64)
    for s in range(NS):
        wp = pk("wp", 1, s, s + 1)
        mm("wp", wp, [(rows(mat(n), s), rows(full("wn"), s)) for n in ("I", "Sw")])
        ts("Wb", mat("Wb%d" % s), mat("BM"), wp, OP.mult)
        ts("Wb", mat("nWb%d" % s), mat("Wb%d" % s), -1.0, OP.mult)
    ts("abn", full("abn"), (["ia", "ib"], lambda T: T.iab[:]), -2048.0, OP.add, n=256)
    ts("mk", full("mj"), full("mi"), 15, OP.bitwise_and)
    ts("mk", full("mk"), full("mj"), 0.0, OP.not_equal, -64.0, OP.mult)
    ri = lambda k: cols("ri", k, k + 1, key="ri%d" % k)
    ts("base", ri(1), ri(0), 15, OP.bitwise_and)
    ts("base", ri(2), ri(0), 64, OP.bitwise_and)
    tt("base", cols("rf", 0, 1, key="rf0"), ri(1), ri(2), OP.add, n=1)
    tt("base", cols("rf", 1, 2, key="rf1"), ri(1), ri(2), OP.subtract, n=1)
    ts("base", cols("rf", 2, 4, key="rf2"), (["rf0", "rf1"], lambda T: T.rf[:, 0:2]), 32.0, OP.mult)
    for c in range(2):
        ts("base", cols("base", 4 * c, 4 * c + 4), cols("bi", 4 * c, 4 * c + 4), cols("rf", 2 + c, 3 + c, key="rf2"), OP.add)

    def spread(s, src, a):
        return [(rows(mat("I" if c == s else "Sw"), s), rows(cols(src, a + 64 * c, a + 64 * c + 64), s)) for c in range(2)]

    def whole(k):
        return [(I, tile(k)), (nI, tile(k))]

    for t in range(NT):
        last, splice = t == NT - 1, t >= 2
        for s in range(NS):
            cur["s"], cur["t"] = s, t
            lk, zk, ik, X = "l%d_%d" % (t, s), "z%d_%d" % (t, s), "ig%d_%d" % (t, s), "X%d" % s
            ca, cb = 64 * (t % 2), 64 * (1 - t % 2)
            Hc, Oc = cols("HO_%d" % s, ca, ca + 64), cols("HO_%d" % s, cb, cb + 64)
            z = cols("Z%d" % t, 192 * s, 192 * s + 64, key=zk)
            Iold = cols("Z%d" % t, 192 * s + 64, 192 * s + 128, key=ik)
            Gold = cols("Z%d" % t, 192 * s + 128, 192 * s + 192, key=ik)
            lists = cols("L%d" % t, 128 * s, 128 * s + 128, key=lk)
            if t > 0:
                for k, key in (("L", lk), ("Z", zk), ("N", ik)):
                    add(None, None, ["send_%d_%d_%s" % (t - 1, s, k)], [key], arr="arr_%d_%d_%s" % (t, s, k), name="arr" + k)
                ts("HO", sb("HO", s), lists, -2048.0, OP.add)
            else:
                mm("a0", pk("Mh", s), spread(s, "abn", 0))
                mm("a0", pk("Mh2", s), spread(s, "abn", 128))
                mm("z0", pk("zd", s), spread(s, "zn", 0))
                ts("l0", lists, two("Mh", "Mh2", s), 2048.0, OP.add, n=128)
                cp("HO", sb("HO", s), two("Mh", "Mh2", s), n=128)
                act("z1", z, pk("zd", s), AF.Copy)
                add(None, None, ["Xin%d.0" % s, "Xin%d.1" % s], [X], name="X0")
            zb = cols("zbuf_%d" % s, 0, NB, 16)
            add("g", lambda g, T, zb=zb, z=z: g.affine_select(zb[1](T), z[1](T), [[0, 64]], OP.is_equal, 0.0, 0, 0), [zk, zb[0]], [zb[0]],
                fx=0.17, cy=128, name="zbuf")
            for k, (e, p, n) in enumerate(cuts(opt["zexp"])):
                scan("zexp%d" % k, piece("zexp", s, p), cols("zmask", 0, n), cols("zbuf_%d" % s, p[0] * QB, p[1] * QB), OP.add, n // 2)
            Hp, OH, HC = pk("Hp", s), slot("A", s, 0), slot("A", s, 1)
            mm("Hp", Hp, [(I, Hc), (I, tile("k2048"))])
            mm("L", pk("L", s), [(mat("c2080"), Hc), (mat("c1184"), Oc)])
            mm("OH", OH, [(I, Oc), (nI, Hc)])
            tt("P", sb("P", s), Oc, Hp, OP.mult)
            tt("S", sb("S", s), sb("P", s), pk("L", s), OP.add)
            ts("ci", sb("ci", s), sb("S", s), 5, OP.arith_shift_right, 4095, OP.bitwise_and)
            cp("c16", sb("c16", s), sb("ci", s))
            ts("set", sb("set", s), OH, 0.0, OP.is_equal)
            tt("HC", HC, Hp, sb("ci", s), OP.subtract)
            cp("C", slot("A", s, 2), sb("ci", s))

            def lst(name, a, p, key=None):
                return cols(name, a + p[0] * 16, a + p[1] * 16, key=key)
            ny = 0
            for nm, raw, ab, l in (("h", "hr", "ha", lambda p: lst("L%d" % t, 128 * s + ca, p, lk)),
                                   ("o", "od", "oa", lambda p: lst("L%d" % t, 128 * s + cb, p, lk)),
                                   ("c", "cd", "ca", lambda p: lst("c16_%d" % s, 0, p))):
                for k, (e, p, n) in enumerate(cuts(opt[nm])):
                    w, o, ze = window(s, l(p)), piece(raw, s, p), piece("zexp", s, p)
                    if e == "R":
                        act("g%s%d" % (nm, k), o, w, AF.Copy, ga=n)
                        yb = cols("ps%d" % (ny % 2), 0, n, key="ps%d:y" % (ny % 2))
                        ny += 1
                        mm("y%s%d" % (nm, k), yb, [(I, o), (nI, ze)], n=n)
                        act("a%s%d" % (nm, k), piece(ab, s, p), yb, AF.Abs, n=n)
                    else:
                        add("v", lambda g, T, o=o, w=w, ze=ze: g.vector.tensor_tensor(o[1](T), w[1](T), ze[1](T), OP.subtract),
                            [w[0], ze[0]], [o[0]], fx=0.05, ga=n, name="g%s%d" % (nm, k))
                        act("a%s%d" % (nm, k), piece(ab, s, p), o, AF.Abs, n=n)
            qs = lambda name: [(cols("nQ", 15 - j, 143 - j), col16(name, s, j)) for j in range(16)]
            mm("dh", pk("dh", s), qs("ha"))
            act("dhs", sb("dhs", s), pk("dh", s), AF.Copy)
            mm("pen", pk("do", s), [(mat("p8I"), sb("set", s))], last=False)
            mm("do", pk("do", s), qs("oa"), first=False)
            mm("dc", pk("dc", s), qs("ca"))
            tt("thr", pk("pen", s) if t else sb("thr", s), pk("do", s), sb("dhs", s), OP.max)
            if t:
                tt("thr2", sb("thr", s), pk("pen", s), Gold, OP.add)
            tt("w", sb("w", s), pk("dc", s), sb("thr", s), OP.is_gt)
            mm("cnt", pk("cnt", s), [(mat("TRIm"), sb("w", s))])
            rec, nam, rej = slot("chz", s, 1), slot("chz", s, 2), sb("rej", s)
            tt("m", sb("m", s), pk("dc", s), sb("dhs", s), OP.max)
            tt("rec", rec, pk("do", s), sb("m", s), OP.is_ge)
            ts("nam", nam, pk("cnt", s), -13.0, OP.is_ge)
            scan("cho", slot("R", s), slot("chz", s), slot("A", s), OP.add, 192)
            cp("ch16", sb("ch16", s), slot("R", s, 2))
            tt("d2", pk("d2", s), Hp, slot("R", s, 2), OP.subtract)
            mm("hsum", pk("V", s), [(nI, col16("hr", s, j)) for j in range(16)], last=False, after=["ch16_%d" % s])
            for k, (e, p, n) in enumerate(cuts(opt["ch"])):
                w, o = window(s, lst("ch16_%d" % s, 0, p)), piece("ch", s, p)
                if e == "a":
                    act("gch%d" % k, o, w, AF.Copy, ga=n)
                else:
                    add("v", lambda g, T, o=o, w=w: g.vector.tensor_copy(o[1](T), w[1](T)), [w[0]], [o[0]], fx=0.05, ga=n, name="gch%d" % k)
                scan("M%d" % k, piece("Mf", s, p), cols("zmask", 0, n), o, OP.max, n // 2)
            mm("V", pk("V", s), [(I, col16("ch", s, j)) for j in range(16)], first=False)
            M, Wb = col16("Mf", s, 15), mat("Wb%d" % s)
            tt("setH", slot("sH", s, 1), sb("set", s), Hp, OP.mult)
            mm("L2", slot("U", s, 1), [(mat("c32"), Oc), (I, tile("kL2"))] + ([(full("KI"), sb("set", s))] if t else []))
            mm("u", slot("U", s, 0), [(mat("c63"), tile("k325")), (mat("nWb%d" % s), M)] + whole("r4096") + [(Wb, M)])
            scan("S2", slot("S2", s), slot("sH", s), slot("U", s), OP.add, 128)
            sl, sz, sh = "SL%d" % t, "SZ%d" % t, "send_%d_%d" % (t, s)
            ts("fx", sb("fx", s), slot("S2", s, 1), 5, OP.arith_shift_right, 4095, OP.bitwise_and)
            if not last:
                mm("zd", pk("zd", s), [(I, z), (nI, M)])
                act("zz", cols(sz, 192 * s, 192 * s + 64, key=sh + "_zz"), pk("zd", s), AF.Abs)
                add("g", None, [sh + "_zz"], [sh + "_Z"], send=(t, s, "Z"), name="sendZ")
                if opt["t32"] == "v":
                    mm("v", pk("v", s), [(Wb, M), (I, tile("k155"))])
                    ts("t32", sb("t32", s), pk("v", s), TILES["r32"], OP.add, -TILES["r32"], OP.add)
                    mm("r", pk("r", s), [(Wb, M), (nI, sb("t32", s)), (I, full("mk"))])
                else:
                    mm("r", pk("r", s), [(nI, tile("k155")), (mat("nWb%d" % s), M)] + whole("r32") + [(Wb, M), (I, full("mk"))])
                scan("sc", sb("sc", s), cols("zmask", 0, 64), pk("r", s), OP.max, 64)
                b, c0 = SMALL["sc_%d" % s]
                pick = cols(b, c0 + 15, c0 + 64, 16, key="sc_%d" % s)
                mm("off", pk("off", s, 0, 8), [(I, full("base")), (I, pick, pk("off", s, 0, 4)), (mat("Sw"), pick, pk("off", s, 4, 8))])
                cp("u16", sb("u16", s), pk("off", s, 0, 8))
                mm("Mh", pk("Mh", s), [(mat("hI"), M)])
                mm("Mh2", pk("Mh2", s), [(mat("hSw"), M)])
                w = window(s, sb("u16", s))
                act("gx", sb("gx", s), w, AF.Copy, scale=0.5, bias=-0.25, ga=128)
                tt("gs", sb("gs", s), sb("gx", s), two("Mh", "Mh2", s), OP.add, n=128)
                add("v", lambda g, T, w=w, s=s: g.vector.tensor_copy(w[1](T), T["gs_%d" % s][:]), [w[0], "gs_%d" % s], [X], fx=0.05, sca=128, name="scat")
            yv, votes = sb("yv", s), (mat("BMs"), sb("yv", s))
            if opt["yv"] == "a":
                act("yv", yv, pk("V", s), AF.Sign, bias=0.5)
            else:
                ts("yv", yv, pk("V", s), 0.0, OP.is_ge)
            y0 = 0.0 if opt["yv"] == "a" else 16.0
            y1, i0 = (1 + y0) / 128, (255 - y0) / 128
            mm("cntv", pk("cntv", s), [votes])
            ts("rej", rej, pk("cntv", s), y1, OP.is_lt)
            tt("back", pk("d2", s), rej, pk("d2", s), OP.mult)
            mm("ys", pk("ys", s), [(mat("c100"), rec), (mat("n100"), nam), (mat("c200"), sb("set", s)), votes])
            mm("Gs", pk("Gs", s), [(mat("n100"), nam), votes] + ([(mat("cG"), Gold)] if t else []))
            out = lambda a, name, b, key: cols("SO", 256 * s + a, 256 * s + a + 64, key=sh + key) if last else cols(name, b, b + 64, key=sh + key)
            oh, oo = out(ca, sl, 128 * s + ca, "_h"), out(cb, sl, 128 * s + cb, "_o")
            oi, og = out(128, sz, 192 * s + 64, "_i"), out(192, sz, 192 * s + 128, "_g")
            ad = sb("lh", s) if splice else oh
            tt("ad", ad, slot("R", s, 2), pk("d2", s), OP.add)
            if splice:
                sp, q = sb("sp", s), pk("q", s)
                tt("sp", sp, pk("ys", s), Iold, OP.is_lt)
                mm("cnt2", pk("cnt2", s), [(mat("TRIo"), sp)] + whole("r2") + [(mat("TRI"), sp)])
                tt("so", sb("so", s), sp, HC, OP.mult)
                tt("q", q, sb("so", s), pk("cnt2", s), OP.mult)
                tt("spoh", pk("spoh", s), sp, OH, OP.mult)
                tt("pre", sb("pre", s), sb("fx", s), pk("spoh", s), OP.subtract)
                tt("lo", oo, sb("pre", s), q, OP.subtract)
                tt("lh", oh, ad, q, OP.subtract)
            else:
                cp("O16", oo, sb("fx", s))
            if t == 0:
                ts("inc", oi, pk("ys", s), y1, OP.is_lt, -i0, OP.add)
            else:
                act("inc", sb("inc", s), pk("ys", s), AF.Sign, scale=-1.0, bias=y1)
                mm("I2p", pk("I2", s), [(I, Iold), (mat("hI"), sb("inc", s))] + ([(mat("n3I"), sb("sp", s))] if splice else []))
                act("I2", oi, pk("I2", s), AF.Copy, bias=0.5 + (i0 if last else 0.0))
            if last:
                ts("G", og, pk("Gs", s), y1, OP.is_ge)
                for x, y, qq in ((oi, "yi", "ss"), (og, "yg", "ss"), (oh, "ya", "sa"), (oo, "yb", "sa")):
                    a = 256 * s + {"ya": ca, "yb": cb, "yi": 128, "yg": 192}[y]
                    for c in range(2):
                        dma(qq[c], "out", part(y, s, 64 * c, 64 * c + 64, None), part("SO", c, a, a + 64, x[0]), 30)
            else:
                act("G", og, pk("Gs", s), AF.Relu, scale=2.0 ** 20, bias=-y1 * 2.0 ** 20)
                mm("dm", pk("k%d" % s, 1), [(mat("p2"), rej)])
                add("g", None, [sh + "_o", sh + "_h"], [sh + "_L"], send=(t, s, "L"), name="sendL")
                add("g", None, [sh + "_i", sh + "_g", sh + "_L"], [sh + "_N"], send=(t, s, "N"), name="sendN")
        if not last:
            act("kp", full("kw"), two("k0", "k1", 1), AF.Copy, n=128, accum=full("ks"))
            ts("KI", full("KI"), I, full("ks"), OP.mult)
    return ops


def cost(o, fig):
    fx, cy, ga, sca, tc = o["c"]
    return fig["issue"] if "send" in o else fx + fig["cy"] * (cy + fig["ga"] * ga + fig["sca"] * sca) + fig["pcy"] * tc


def late(o, fig):
    return fig["hop"] if "arr" in o else 2.0 + o["lat"] / fig["dma"] if "lat" in o else 0.0


def graph(opt):
    ops = build(opt)
    deps, succ = [set() for _ in ops], [[] for _ in ops]
    lastw, readers = {}, {}

    def keys(l):
        out = []
        for k in l:
            out += keys(k) if isinstance(k, (list, tuple)) else ([k] if k else [])
        return out
    for i, o in enumerate(ops):
        o["r"], o["w"] = keys(o["r"]), keys(o["w"])
        for k in o["r"] + o["w"]:
            if k in lastw:
                deps[i].add(lastw[k])
        for k in o["w"]:
            deps[i].update(readers.get(k, ()))
        for k in o["r"]:
            readers.setdefault(k, []).append(i)
        for k in o["w"]:
            lastw[k] = i
            readers[k] = []
        deps[i].discard(i)
        o["banks"] = sorted(set(k.split(":")[0] for k in o["r"] + o["w"] if k.startswith("ps")))
        for j in sorted(deps[i]):
            succ[j].append(i)
    return ops, deps, succ


def events(gr, ph, fig):
    ops, deps, succ = gr
    n, w = len(ops), fig["wake"]
    key = [0.0] * n
    for i in range(n - 1, -1, -1):
        o = ops[i]
        if o["t"] < 0:
            key[i] = -99.0 + i * 1e-3 if "sem" in o else ph.get(o["name"], min(min(key[k] for k in succ[i]) - 3.0, 5.0))
        else:
            key[i] = o["t"] * ph["period"] + o["s"] * (ph["lag"] + ph.get("lag%d" % o["t"], 0.0)) + ph.get(o["name"], 12.0) if o["q"] else -99.0
    left, end, order = [len(d) for d in deps], [0.0] * n, []
    rdy, free, bank, shut = dict((q, {}) for q in "vatgs"), dict.fromkeys("vatgs", 0.0), {}, set()
    deps = [set(d) for d in deps]

    def done(i, st):
        o = ops[i]
        end[i] = st + cost(o, fig) + (-w if o["q"] == "t" and not o["last"] else late(o, fig))
        order.append(i)
        for k in succ[i]:
            left[k] -= 1
            if not left[k]:
                m = max(end[j] for j in deps[k])
                if ops[k]["q"]:
                    rdy[ops[k]["q"]][k] = m + w
                else:
                    done(k, m)
    for i in range(n):
        if not deps[i]:
            rdy[ops[i]["q"]][i] = 0.0
    while len(order) < n:
        best = None
        for q in rdy:
            es = []
            for i, st in rdy[q].items():
                if q == "t" and ops[i]["first"] and ops[i]["banks"][0] in shut:
                    continue
                es.append((max([st, free[q]] + [end[j] + w for b in ops[i]["banks"] for p, j in bank.get(b, {}).items() if p != q]), i))
            if es:
                m = min(es)[0]
                if best is None or m < best[0]:
                    best = (m, q) + min((key[i], st, i) for st, i in es if st <= m + ph["look"])[1:]
        m, q, st, i = best
        del rdy[q][i]
        for b in ops[i]["banks"]:
            deps[i].update(j for p, j in bank.get(b, {}).items() if p != q)
            bank.setdefault(b, {})[q] = i
        if q == "t":
            if ops[i]["last"]:
                shut.discard(ops[i]["banks"][0])
            else:
                shut.add(ops[i]["banks"][0])
        free[q] = st + cost(ops[i], fig)
        done(i, st)
    return deps, order, max(end)


def plan(opt=None):
    gr = graph(opt or OPT)
    ops = gr[0]
    deps, order, span = events(gr, dict((x.split(":")[0], float(x.split(":")[1])) for x in PHASE.split()), FIG)
    count = {}
    for i in order:
        o = ops[i]
        if "sem" in o:
            o["ev"] = [(o["sem"], 16)]
        elif "arr" in o:
            o["ev"] = [(o["arr"], None)]
        elif "send" in o:
            o["ev"] = []
        elif o["q"] is None:
            o["ev"] = [e for j in deps[i] for e in ops[j]["ev"]]
        else:
            s = "q" + o["q"]
            count[s] = count.get(s, 0) + 1
            o["ev"] = [(s, count[s])]
    return ops, deps, order, count, span


def send_aps(o, far, near):
    t, s, k = o["send"]
    a, b, w = {"L": (128 * s, 128 * s + 128, "L"), "Z": (192 * s, 192 * s + 64, "Z"), "N": (192 * s + 64, 192 * s + 192, "Z")}[k]
    return [(far["%s%d" % (w, t + 1)][:, a:b], near["S%s%d" % (w, t)][:, a:b])]


_PLAN = []


def rank_program(g, core, T, topo):
    rank = T.rank_of(core)
    if rank is None:
        return
    if not _PLAN:
        _PLAN.append(plan())
    ops, deps, order, count, _ = _PLAN[0]
    n = len(T.cores)
    nxt, prv = T.cores[(rank + 1) % n], T.cores[(rank - 1) % n]
    mask = topo.mask(core, nxt)
    n_in, n_out = len(topo.engines(prv, core)), len(topo.engines(core, nxt))
    rid, pid = topo.addr(nxt)[:2]
    queues = {"v": g.vector, "a": g.scalar, "t": g.tensor, "g": g, "s": g.sync}
    seen = {}
    sent = 0
    for i in order:
        o = ops[i]
        if o["q"] is None:
            continue
        q = queues[o["q"]]
        need = {}
        for j in deps[i]:
            if o["q"] == "t" and ops[j]["q"] == "t" and not ops[j]["last"] and ops[j]["w"] == o["w"]:
                continue
            for s, v in ops[j]["ev"]:
                need[s] = max(need.get(s, 0), n_in if v is None else v)
        for s in sorted(need):
            if seen.get((o["q"], s), 0) < need[s]:
                q.wait_ge(T.sem[s], need[s])
                seen[o["q"], s] = need[s]
        if "send" in o:
            t, s, k = o["send"]
            dst, src = send_aps(o, T, T)[0]
            g.remote_dma(dst, src, T.sem["arr_%d_%d_%s" % (t + 1, s, k)], T.sem.loc, pid, rid, mask)
            sent += n_out
            continue
        o["fn"](g, T).then_inc(T.sem[o["ev"][0][0]], 16 if "sem" in o else 1)
    for s in sorted(count):
        g.wait_ge(T.sem[s], count[s])
    for k in range(NOUT):
        g.wait_ge(T.sem["out%d" % k], 16)
    g.wait_ge(T.sem.loc, sent)
